import numpy as np, ml_dtypes
CORES = [48,51,52,55]
N = 4
BF = ml_dtypes.bfloat16
T0, L, M, RO, KILL, HOPS, TILE = 1536, 256, 4, 5, 200, [1, 1, 1, 1], [0, 1, 2, 1, 2]
NS, GB, W = L * M, T0 + L * RO, T0 + L * (2 * RO - 1)
LAST = NS - M + max(TILE)
R4 = np.arange(N).reshape(N, 1, 1, 1); G4 = np.arange(8).reshape(1, 8, 1, 1); R3 = R4[..., 0]; G3 = G4[..., 0]
def members(rng, of, cl, k):
    tab = np.argsort(of, axis=-1, kind="stable").reshape(N, 8, 32, -1)
    return tab[R4, G4, cl[:, :, None, :], rng.integers(0, tab.shape[3], (N, 8, k, cl.shape[2]))]
def around(rng, cen, cl):
    n = cl.shape[2]; w = rng.choice(np.array([2, 6, 10]), (N, 8, n, 1))
    p = cen[R3, G3, cl] + np.rint(w * (2 * rng.random((N, 8, n, 16)) - 1)).astype(np.int64)
    return np.ascontiguousarray(np.clip(p, 0, 63).transpose(0, 1, 3, 2))
def parts(rng):
    cen = np.where(rng.random((N, 8, 32, 1)) < 0.7, rng.integers(0, 64, (1, 8, 32, 16)), rng.integers(0, 64, (N, 8, 32, 16)))
    cv = np.argsort(rng.random((N, 8, T0)), axis=-1) % 32; cz = np.argsort(rng.random((N, 8, NS)), axis=-1) % 32
    two = rng.permutation(8)[:2]; cz[:, two] = np.repeat(np.argsort(rng.random((2, L)), axis=-1) % 32, M, axis=1)
    V = around(rng, cen, cv); Z = around(rng, cen, cz)
    stray = rng.choice(np.array([0.0, 0.1, 0.1, 0.5, 0.5]), (N, 8, 1, NS))
    S = np.where(rng.random((N, 8, 16, NS)) < stray, rng.integers(0, T0, (N, 8, 16, NS)), members(rng, cv, cz, 16))
    Q = np.where(rng.random((N, 8, 16, T0)) < 0.4, rng.integers(0, NS, (N, 8, 16, T0)), members(rng, cz, cv, 16))
    Q[R4, G4, np.arange(5).reshape(1, 1, 5, 1), S[:, :, :5]] = np.arange(NS)
    u = rng.random((N, 8, T0))
    kid = np.where(u < 0.15, np.arange(T0), np.where(u < 0.4, rng.integers(0, T0, (N, 8, T0)), members(rng, cv, cv, 1)[:, :, 0]))
    u = rng.random((N, 8, NS)); best = np.take_along_axis(S, rng.integers(0, 16, (N, 8, 1, NS)), 2)[:, :, 0]
    best = np.where(u < 0.07, -1, np.where(u < 0.2, rng.integers(0, T0, (N, 8, NS)), best))
    return V, Z, S, Q, kid, best
def pack(V, Z, S, Q, kid, best):
    def p(x): return np.ascontiguousarray(x).reshape(N, 128, -1)
    return {"vn": p(V).astype(np.float32).astype(BF), "zs": p(Z).astype(np.float32).astype(BF), "sn": p(S).astype(np.int32), "nq": p(Q).astype(np.int32),
            "kid": np.ascontiguousarray(kid).astype(np.int32), "bst": np.ascontiguousarray(best).astype(np.int32)}
def setup_inputs(rng):
    return pack(*parts(rng))
def setup_inputs_spread(rng):
    def pts(n):
        x = np.minimum((np.exp2(6 * rng.random((N, 8, 1, n))) * rng.random((N, 8, 16, n))).astype(np.int64), 63)
        return np.where(rng.random((N, 8, 1, n)) < 0.5, x, 63 - x)
    def lst(n, k, hi):
        return np.minimum((hi * rng.random((N, 8, k, n)) ** rng.choice(np.array([1.0, 2.0, 6.0]), (N, 8, 1, n))).astype(np.int64), hi - 1)
    return pack(pts(T0), pts(NS), lst(NS, 16, T0), lst(T0, 16, NS), lst(T0, 1, T0)[:, :, 0], lst(NS, 1, T0 + 1)[:, :, 0] - 1)
def edge(rng, shape, lo, hi, by):
    m = rng.choice(np.array([0.0, 0.5, 0.5, 1.0]), shape[:-2] + (1, shape[-1]))
    return np.where(rng.random(by) < 0.2, rng.integers(lo, hi + 1, shape), np.where(rng.random(shape) < m, hi, lo))
def setup_inputs_ends(rng):
    V = edge(rng, (N, 8, 16, T0), 0, 63, (N, 8, 1, T0)); Z = edge(rng, (N, 8, 16, NS), 0, 63, (N, 8, 1, NS))
    S = edge(rng, (N, 8, 16, NS), 0, T0 - 1, (N, 8, 16, NS)); Q = edge(rng, (N, 8, 16, T0), 0, NS - 1, (N, 8, 16, T0))
    kid = edge(rng, (N, 8, 1, T0), 0, T0 - 1, (N, 8, 1, T0))[:, :, 0]; best = edge(rng, (N, 8, 1, NS), -1, T0 - 1, (N, 8, 1, NS))[:, :, 0]
    for q in range(N):
        for g in range(8):
            hi = 63 if g % 2 == 0 else 0; own = (g // 2) % 2 == 1
            V[q, g, :, 0] = 63 - hi; V[q, g, :, [3, 8, T0 - 1]] = hi
            kid[q, g, 0] = 0 if own else T0 - 1; kid[q, g, T0 - 1] = T0 - 1 if own else 0; kid[q, g, 3] = 3; kid[q, g, 8] = 8
            Z[q, g, :, LAST] = hi; S[q, g, :, LAST] = 0; S[q, g, 4, LAST] = 3; S[q, g, 9, LAST] = 8; S[q, g, 15, LAST] = T0 - 1
            Z[q, g, :, LAST - 1] = 63 - hi; S[q, g, :, LAST - 1] = T0 - 1; Z[q, g, :, 0] = hi; S[q, g, :, 0] = 0
            Q[q, g, :, 3] = LAST; Q[q, g, :, T0 - 1] = LAST - 1
    return pack(V, Z, S, Q, kid, best)
def setup_inputs_corners(rng):
    V, Z, S, Q, kid, best = parts(rng); sh = int(rng.integers(0, 8))
    for q in range(N):
        for g in range(8):
            c = (g + q + sh) % 8
            if c == 0:
                kid[q, g] = np.arange(T0); best[q, g] = -1
            elif c == 1:
                kid[q, g] = 0; best[q, g] = 0; S[q, g, :, ::3] = 0
            elif c == 2:
                kid[q, g] = T0 - 1; best[q, g] = T0 - 1; S[q, g, :, 1::3] = T0 - 1
            elif c == 3:
                kid[q, g] = (np.arange(T0) + 1) % T0
            elif c == 4:
                o = rng.permutation(T0)[:6]; kid[q, g, o] = o; Z[q, g] = 0
                for j in range(6):
                    s = KILL - 1 + j // 2; x = np.full(16, s // 16); x[rng.permutation(16)[:s % 16]] += 1; V[q, g, :, o[j]] = x
                typ = rng.integers(0, 5, NS); s = o[rng.integers(0, 2, (16, NS))]
                s = np.where((np.arange(16)[:, None] == rng.integers(0, 16, NS)) & (typ == 1), o[2], s); s = np.where(typ == 2, o[3], s)
                s = np.where(typ == 3, o[rng.integers(0, 6, (16, NS))], s); S[q, g] = np.where(typ == 4, S[q, g], s)
            elif c == 5:
                S[q, g] = np.arange(NS); Q[q, g] = np.arange(T0) % NS; kid[q, g, ::2] = np.arange(0, T0, 2)
            elif c == 6:
                V[q, g] = rng.choice(np.array([0, 1, 62, 63]), (16, T0)); Z[q, g] = rng.choice(np.array([0, 63]), (16, NS))
                S[q, g, :, ::2] = rng.choice(np.array([0, T0 - 1]), (16, (NS + 1) // 2))
                o = rng.permutation(T0)[:10]; kid[q, g, o] = o; kid[q, g, o[8]] = o[7]; flip = (q + g) % 2 == 1
                for j in range(10):
                    x = 63 - (rng.permutation(16) < 8 - j); V[q, g, :, o[j]] = 63 - x if flip else x
                far = (np.arange(NS) // M) % 2 == 1; least = (np.arange(NS) // (2 * M)) % 10
                Z[q, g] = np.where(far, 63 if flip else 0, Z[q, g]); S[q, g] = np.where(far, o[rng.integers(least, 10, (16, NS))], S[q, g])
            else:
                Q[q, g] = rng.choice(np.array([0, NS - 1]), (16, T0)); best[q, g] = rng.choice(np.array([-1, 0, T0 - 1]), NS)
    return pack(V, Z, S, Q, kid, best)
def setup_inputs_crowd(rng):
    V, Z, S, Q, kid, best = parts(rng); sh = int(rng.integers(0, 8)); e = NS - M
    for q in range(N):
        for g in range(8):
            c = (g + sh) % 8; p = T0 - 1 if (q + g) % 2 else int(rng.integers(1, T0 - 1)); o = (p + 1) % T0
            kid[q, g, p] = p; kid[q, g, o] = o; V[q, g, :, p] = 0
            if c in (0, 1, 5):
                Z[q, g] = np.maximum(Z[q, g], 20); S[q, g] = p
            if c == 1: S[q, g, :, e:] = o
            if c in (2, 3):
                Z[q, g] = rng.integers(0, 4, (16, NS)); S[q, g] = p
            if c == 2: Z[q, g, :, e:] = 63
            if c == 4: S[q, g] = rng.choice(np.array([p, o, (p + 2) % T0]), (16, NS))
            if c == 5:
                Q[q, g, :, p] = NS - 1; best[q, g, NS - 1] = p
            if c >= 6:
                V[q, g, :, p] = 31; S[q, g] = p
                Z[q, g] = np.where(rng.random((1, NS)) < 0.5, rng.integers(50, 64, (16, NS)), rng.integers(0, 13, (16, NS))); Z[q, g, :, NS - 1] = 63; Z[q, g, :, 0] = 0
                best[q, g, 0] = p; best[q, g, NS - 1] = p; Q[q, g, :, p] = NS - 1; Q[q, g, (15 if c == 6 else 8):, p] = 0
            if c == 7:
                Z[q, g, :, 1] = 31
                if q % 4 == 3: Q[q, g, 0, p] = 1
                else: Q[q, g, 16 - q % 4:, p] = 1
    return pack(V, Z, S, Q, kid, best)
def setup_inputs_ties(rng):
    V, Z, S, Q, kid, best = parts(rng)
    pts = rng.integers(0, 64, (8, 48, 16)); pts[1::2] = 20 + 25 * (pts[1::2] % 2)
    few = rng.choice(np.array([3, 6, 16, 48]), (N, 8, 1))
    V = pts[G3, rng.integers(0, 48, (N, 8, T0)) % few].transpose(0, 1, 3, 2); Z = pts[G3, rng.integers(0, 48, (N, 8, NS))].transpose(0, 1, 3, 2)
    return pack(V, Z, S, Q, kid, best)
def check_inputs(d):
    bad = []
    for k, lo, hi in (("vn", 0, 63), ("zs", 0, 63), ("sn", 0, T0 - 1), ("nq", 0, NS - 1), ("kid", 0, T0 - 1), ("bst", -1, T0 - 1)):
        x = np.asarray(d[k]).astype(np.float64)
        if not (np.min(x) >= lo and np.max(x) <= hi and np.all(x == np.floor(x))): bad.append("range of " + k)
    return bad
def columns(x):
    return np.ascontiguousarray(x.astype(np.float32).astype(np.int32).reshape(N, 8, 16, -1).transpose(0, 1, 3, 2))
def rows(x):
    return np.ascontiguousarray(x.transpose(0, 1, 3, 2)).reshape(N, 128, -1)
def dist(a, b):
    return np.add.reduce(np.abs(a - b), axis=-1)
def reference(vn, zs, sn, nq, kid, bst):
    V = np.zeros((N, 8, W, 16), np.int32); V[:, :, :T0] = columns(vn); Z = columns(zs); S = columns(sn)
    Q = np.zeros((N, 8, W, 16), np.int32); Q[:, :, :T0] = columns(nq)
    child = np.tile(np.arange(W), (N, 8, 1)); child[:, :, :T0] = kid
    best = bst.astype(np.int64); lane = np.arange(L)
    for t in range(RO):
        v = M * lane + TILE[t]; z = Z[:, :, v]; z1 = z[:, :, :, None, :]; s = S[:, :, v].astype(np.int64)
        e = child[R4, G4, s]
        ds = dist(V[R4, G4, s], z1); de = dist(V[R4, G4, e], z1)
        s = np.where(de < ds, e, s); d = np.minimum(ds, de)
        if t > 0:
            m = GB + L * (t - 1) + lane; dm = dist(V[:, :, m], z)
            put = (np.arange(16) == np.argmax(d, axis=3)[..., None]) & (dm < np.max(d, axis=3))[..., None]
            s = np.where(put, m[:, None], s); d = np.where(put, dm[..., None], d)
        S[:, :, v] = s
        b = np.argmin(d, axis=3); a = np.take_along_axis(s, b[..., None], 3)[..., 0]
        live = np.max(d, axis=3) >= KILL
        best[:, :, v] = np.where(live, a, -1)
        va = V[R3, G3, a]; va1 = va[:, :, :, None, :]; qa = Q[R3, G3, a]
        bq = best[R4, G4, qa]; zq = Z[R4, G4, qa]
        att = (bq >= 0) & ((bq == a[..., None]) | (dist(V[R4, G4, np.maximum(bq, 0)], va1) >= dist(zq, va1)))
        pull = np.add.reduce(np.where(att[..., None], np.clip(zq - va1, -1, 1), 0), axis=3)
        new = np.clip(va + np.clip(pull, -2, 2), 0, 63); n = T0 + L * t + lane
        V[:, :, n] = new
        low = np.full((N, 8, W), L); np.minimum.at(low, (R3, G3, a), np.where(live, lane, L))
        child = np.where(low < L, T0 + L * t + low, child)
        if t < RO - 1:
            Q[:, :, n] = qa; m = GB + L * t + lane
            V[:, :, m] = np.roll(new, HOPS[t], axis=0); Q[:, :, m] = np.roll(qa, HOPS[t], axis=0)
    h = NS // 2
    return {"yv": rows(V[:, :, T0:GB]).astype(np.float32).astype(BF), "ys": rows(S[:, :, :h] + 4096 * S[:, :, h:]).astype(np.float32), "yk": child.astype(np.float32), "yb": best.astype(np.float32)}

@@ -1,0 +1,844 @@
+import numpy as np
+from concourse.bass import DstId, RemoteDMATransfer
+from concourse.mybir import dt, AluOpType, AxisListType, ActivationFunctionType
+
+T0, L, RO, KILL = 1536, 256, 5, 200
+TILE = [0, 1, 2, 1, 2]
+HOPS = [1, 1, 1, 1]
+GB, W = T0 + L * RO, T0 + L * (2 * RO - 1)
+NONE = W
+EPS = 2.0 ** -15
+ALU = AluOpType
+ACT = ActivationFunctionType
+
+B, F4, I4, U2 = "bfloat16", "float32", "int32", "uint16"
+
+
+def _s(shape, d):
+    return ("sbuf", [128] + list(shape), d)
+
+
+SCRATCH = {
+    "V": _s([W + 16], B), "F": _s([W + 16], B), "T2": _s([W + L], B), "Q": _s([W], I4),
+    "Z": _s([1024], B), "VB": _s([1024], F4), "VBt": _s([1024], B),
+    "SN4": _s([16, 16, 4], I4), "KI": _s([96], I4), "KJ": _s([96], I4), "KK": _s([96], I4), "KL": _s([96], B), "KH": _s([96], B),
+    "DI": _s([120], I4), "DJ": _s([240], I4), "DL": _s([240], B),
+    "BI": _s([64], I4), "B64": _s([64], F4), "Bt": _s([64], F4), "Bo": _s([4, 16], F4), "B16": _s([64], U2),
+    "XB": _s([4, 2, 16], F4), "XBT": _s([128], F4), "Y1": _s([16], F4), "YB": _s([2, 16], F4), "YBT": _s([32], F4),
+    "X2": _s([16, 2, 16], F4), "XT": _s([512], F4), "YS": _s([512], F4), "Yt": _s([128], F4), "Yc": _s([8, 16], F4),
+    "YL": _s([240], B), "YH": _s([240], B), "YK": _s([240], F4),
+    "zr0": _s([4096], B), "zr1": _s([4096], B), "zr2": _s([4096], B), "ZT": _s([16, 16, 16], B), "Z4": _s([16, 16, 4], B),
+    "S0": _s([L], U2), "S1": _s([L], U2), "S2": _s([L], U2),
+    "P0": _s([L], I4), "P1": _s([L], I4), "P2": _s([L], I4),
+    "G2": _s([4096], B), "DA": _s([4096], B), "DS": _s([4096], B), "DB": _s([4096], B),
+    "DC": _s([4096], B), "AC": _s([4096], B), "U": _s([8, 2 * L], B), "vr": _s([4096], B), "GR": _s([4096], B),
+    "E": _s([16, L], B), "e16": _s([L], U2), "q16": _s([L], U2), "ar16": _s([L], U2),
+    "Pi": _s([L], I4), "Pj": _s([L], I4), "dP": _s([L], I4), "ids": _s([L], I4),
+    "kx": _s([L], F4), "sc1": _s([L], F4), "sc2": _s([L], F4), "sc3": _s([L], F4), "tB": _s([L], F4),
+    "tg": _s([16], F4), "cd": _s([16], F4), "Pm": _s([16], F4), "thm": _s([16], F4), "lv": _s([16], F4),
+    "t1": _s([16], F4), "t2": _s([16], F4), "t3": _s([16], F4), "aD": _s([16], F4), "apf": _s([16], F4),
+    "a16": _s([16], U2), "ap16": _s([16], U2), "o16": _s([16], U2),
+    "va": _s([L], B), "nFa": _s([L], B), "lo": _s([L], B), "hi": _s([L], B), "dg": _s([L], B), "att": _s([L], B),
+    "A1": _s([L], F4), "wx": _s([2, L], B), "fl": _s([L], F4), "sc4": _s([L], F4),
+    "LV": _s([4, L], B), "LQ": _s([4, L], I4),
+    "pI": _s([16], I4), "pJ": _s([16], I4), "pc": _s([16], F4), "XI": _s([144], F4), "CG": _s([128], F4), "KX": _s([L], F4),
+    "SEL": _s([3, 144], B), "BO": _s([128], B), "BOW": _s([128], B), "DW": _s([128], B), "ID": _s([128], B), "NID": _s([128], B),
+    "EXP": _s([16, 128], B), "M16": _s([L], F4), "thr": _s([L], F4), "seg": _s([L], F4), "big": _s([L], F4),
+    "E4": _s([L], F4), "ID4": _s([128], F4), "cm32": _s([L], B), "pw": _s([16], F4), "hz": _s([2, 16], F4),
+    "dum": _s([16], F4), "mg": _s([16], F4), "oT": _s([16], U2), "oB": _s([16], U2), "oE": _s([16], U2), "oI": _s([3, 16], I4),
+    "p0": ("psum", [128, 512], F4), "p1": ("psum", [128, 512], F4),
+    "p2": ("psum", [128, 512], F4), "p3": ("psum", [128, 512], F4), "p4": ("psum", [128, 512], F4),
+    "p5": ("psum", [128, 512], F4), "p6": ("psum", [128, 512], F4), "p7": ("psum", [128, 512], F4),
+}
+IO = {"vn": ([128, T0], B), "zs": ([128, 1024], B), "sn": ([128, 1024], I4), "nq": ([128, T0], I4), "kid": ([8, T0], I4),
+      "bst": ([8, 1024], I4), "yv": ([128, L * RO], B), "ys": ([128, 512], F4), "yk": ([8, W], F4), "yb": ([8, 1024], F4)}
+NDMA = 48
+SEMAPHORES = ["cv", "ca", "cp", "cg", "snt"] + ["d%d" % i for i in range(NDMA)] + ["av%d" % i for i in range(4)] + ["aq%d" % i for i in range(4)]
+CNT = {"v": "cv", "a": "ca", "p": "cp", "g": "cg"}
+S_ = slice
+ALL = slice(None)
+TUNE = {"nv_copy": 10, "zact": 5, "actpath": 2, "act0": 2, "dsact": 2, "pos1": 0, "posb": 0, "posc": 0, "mult": 0, "nclip": 2,
+        "parts": ((0, 4),), "nv_first": 0, "ng": 4, "ng_first": 5, "nz": 11, "sact": (), "ds0": 0, "early": 8}
+NOM = {"f": 1.25, "ga": 1.56, "sca": 3.5, "pe": 0.42, "ov": 45.0, "lat": 110.0, "lat0": 60.0, "dma": 2000.0, "rem": 3000.0, "holds": (0.3, 0.7, 1.0),
+       "also": ({}, {"ga": 1.2, "sca": 2.5, "f": 1.1, "lat": 200.0, "lat0": 100.0}, {"ga": 1.9, "sca": 5.0, "f": 1.4, "pe": 0.5})}
+
+
+def _shape(n):
+    return SCRATCH[n][1] if n in SCRATCH else IO[n][0]
+
+
+def _dtype(n):
+    return SCRATCH[n][2] if n in SCRATCH else IO[n][1]
+
+
+def _where(n):
+    return SCRATCH[n][0] if n in SCRATCH else "dram"
+
+
+def R(n, *ix):
+    return {"n": n, "p": ALL, "ix": ix, "off": None}
+
+
+def RP(n, p, *ix):
+    return {"n": n, "p": p, "ix": ix, "off": None}
+
+
+def IND(win, off):
+    return {"n": win["n"], "p": ALL, "ix": win["ix"], "off": off}
+
+
+_FOOT = {}
+
+
+def _foot(r):
+    key = (r["n"], repr(r["p"]), repr(r["ix"]))
+    if key not in _FOOT:
+        sh = _shape(r["n"])
+        m = np.zeros(sh[1:], dtype=bool)
+        m[tuple(r["ix"])] = True
+        pm = np.zeros(sh[0], dtype=bool)
+        pm[r["p"]] = True
+        fb = int.from_bytes(np.packbits(m.reshape(-1), bitorder="little").tobytes(), "little")
+        pb = int.from_bytes(np.packbits(pm, bitorder="little").tobytes(), "little")
+        _FOOT[key] = (fb, pb, int(m.sum()), int(pm.sum()))
+    return _FOOT[key]
+
+
+def _count(r):
+    return 16 * _foot(r["off"])[2] if r["off"] is not None else _foot(r)[2]
+
+
+def _ap(T, r):
+    if not isinstance(r, dict):
+        return r
+    a = T[r["n"]][(r["p"],) + tuple(r["ix"])]
+    return a.indirect(_ap(T, r["off"])) if r["off"] is not None else a
+
+
+def build_ops(tune):
+    ops = []
+    group = {}
+
+    def add(eng, kind, args, reads, writes, **kw):
+        rd = []
+        for r in reads:
+            if isinstance(r, dict):
+                rd.append(r)
+        for r in list(rd) + list(writes):
+            if r["off"] is not None:
+                rd.append(r["off"])
+        o = {"eng": eng, "kind": kind, "args": args, "rd": rd, "wr": list(writes), "id": len(ops), "prio": 0.0}
+        o.update(kw)
+        ops.append(o)
+        return o
+
+    def cp(out, a, eng="v"):
+        if eng == "a":
+            return act(out, a, ACT.Copy)
+        return add("v", "copy", (out, a), [a], [out])
+
+    def tt(out, a, b, op):
+        return add("v", "tt", (out, a, b, op), [a, b], [out])
+
+    def ts(out, a, s1, op0, s2=None, op1=None):
+        return add("v", "ts", (out, a, s1, s2, op0, op1), [a, s1, s2], [out])
+
+    def scan(out, d0, d1, init, op0, op1):
+        return add("v", "scan", (out, d0, d1, init, op0, op1), [d0, d1], [out])
+
+    def tr(out, a):
+        return add("v", "tr", (out, a), [a], [out])
+
+    def ms(out, c):
+        return add("v", "ms", (out, c), [], [out])
+
+    def act(out, a, fn, bias=0.0, scale=1.0):
+        return add("a", "act", (out, a, fn, bias, scale), [a, bias, scale], [out])
+
+    def mm(lst):
+        bank = lst[0][0]["n"]
+        if lst[0][3]:
+            group[bank] = len(ops)
+        return add("p", "mm", lst, [x for m in lst for x in m[1:3]], [m[0] for m in lst], group=group[bank])
+
+    def iota(out, pat, base, cm):
+        return add("g", "iota", (out, pat, base, cm), [], [out])
+
+    def dma(out, a, eng="s"):
+        return add(eng, "dma", (out, a), [a], [out])
+
+    def dpass(ps, src, c, first=False, last=False, n=1024, neg=0):
+        w = n // 16
+        return mm([(R(ps, S_(w * c, w * c + w)), R("SEL", neg, S_(15 - m, 143 - m)), R(src, S_(n * c + m, n * (c + 1), 16)), first and m == 0, last and m == 15)
+                   for m in range(16)])
+
+    def ch(n, c):
+        return R(n, S_(1024 * c, 1024 * c + 1024))
+
+    def oc(n, c):
+        return R(n, S_(64 * c, 64 * c + 64))
+
+    dma(R("KI"), R("kid")); dma(R("Z4"), R("zs"), "a"); dma(R("SN4"), R("sn")); dma(R("V", S_(0, T0)), R("vn"), "a")
+    dma(R("BI"), R("bst"))
+    iota(R("pI"), [[0, 16]], 0, 1)
+    iota(R("oI", 0), [[32, 16]], 0, 0); iota(R("oI", 1), [[1, 16]], 0, 0); iota(R("oI", 2), [[16, 16]], 15, 0)
+    iota(R("XI"), [[1, 144]], 0, 0)
+    iota(R("CG"), [[1, 8], [0, 16]], 0, 0)
+    iota(R("KX"), [[0, 16], [1, 16]], 0, 0)
+    iota(RP("DI", S_(0, 32)), [[1, 120]], 0, 120)
+    ms(R("T2", S_(0, T0)), 0.0)
+    ts(R("pJ"), R("pI"), 31, ALU.bitwise_and)
+    tt(R("pJ"), R("pJ"), R("oI", 0), ALU.add)
+    cp(R("oT"), R("pJ")); cp(R("oB"), R("oI", 1)); cp(R("oE"), R("oI", 2))
+    ts(R("oI", 0, S_(0, 1)), R("pI", S_(0, 1)), 4, ALU.arith_shift_right)
+    ts(R("oI", 0, S_(1, 2)), R("pI", S_(0, 1)), 15, ALU.bitwise_and)
+    cp(R("pc", S_(0, 2)), R("oI", 0, S_(0, 2)))
+    cp(R("pc", S_(2, 3)), R("pI", S_(0, 1)))
+    ts(R("pc", S_(3, 4)), R("pc", S_(0, 1)), 16.0, ALU.mult, 15.0, ALU.add)
+    pc = lambda i: R("pc", S_(i, i + 1))
+    ts(R("SEL", 0), R("XI"), pc(3), ALU.is_equal)
+    if tune["pos1"]:
+        ts(R("SEL", 1), R("XI"), pc(3), ALU.is_equal, -8192.0, ALU.mult)
+    if tune["posb"] or tune["posc"]:
+        ts(R("SEL", 2), R("XI"), pc(3), ALU.is_equal, -1.0, ALU.mult)
+    ts(R("BO"), R("CG"), pc(0), ALU.is_equal)
+    ms(R("cm32"), -1.0 / 32)
+    ts(R("ID4"), R("XI", S_(0, 128)), pc(2), ALU.is_equal)
+    iota(R("F", S_(0, W)), [[0, W]], 0, 0); ms(R("F", S_(W, W + 16)), 200.0)
+    ts(R("ID"), R("XI", S_(0, 128)), pc(2), ALU.is_equal)
+    ts(R("NID"), R("XI", S_(0, 128)), pc(2), ALU.is_equal, -1.0, ALU.mult)
+    ts(R("M16"), R("KX"), pc(1), ALU.is_equal)
+    ts(R("mg"), R("KX", S_(0, 16)), pc(1), ALU.is_equal, 1.0 if tune["mult"] else -128.0, ALU.mult)
+    for k in range(16):
+        act(R("EXP", k), R("BO"), ACT.Identity, 0.0, R("mg", S_(k, k + 1)))
+    ms(R("hz", 0), 0.5); ms(R("hz", 1), 0.0)
+    scan(R("pw"), R("hz", 0), R("hz", 1), 65536.0, ALU.mult, ALU.add)
+    tt(R("pw"), R("pw"), R("M16", S_(0, 16)), ALU.mult)
+    add("v", "red", (pc(4), R("pw")), [R("pw")], [pc(4)])
+    ts(pc(5), pc(4), 2.0, ALU.mult, 1.0, ALU.add)
+    ts(R("DW"), R("BO"), pc(4), ALU.mult)
+    ts(R("BOW"), R("BO"), 65536.0, ALU.mult)
+    ts(R("thr"), R("M16"), pc(5), ALU.mult, -1.0, ALU.add)
+    ts(R("seg"), R("KX"), 0.0, ALU.is_gt)
+    ts(R("big"), R("KX"), 0.0, ALU.is_equal, 2.0 ** 25, ALU.mult)
+    cx, ck = R("p7", S_(0, L)), R("p7", S_(L, 2 * L))
+    ts(R("dum"), R("XI", S_(0, 16)), 16.0, ALU.mult, pc(1), ALU.add)
+    iota(R("V", S_(T0, W + 16)), [[0, W + 16 - T0]], 0, 0)
+    ts(R("KJ"), R("KI"), 63, ALU.bitwise_and); ts(R("KK"), R("KI"), 4032, ALU.bitwise_and)
+    ts(R("KL"), R("KJ"), EPS, ALU.mult); ts(R("KH"), R("KK"), EPS, ALU.mult)
+    dma(RP("T2", S_(0, 128, 16), S_(0, T0)), R("KL")); dma(RP("T2", S_(1, 128, 16), S_(0, T0)), R("KH"), "a")
+    p32 = S_(0, 32)
+    h0, h1 = S_(0, 120), S_(120, 240)
+    ts(RP("DJ", p32, h0), RP("DI", p32), 63, ALU.bitwise_and); ts(RP("DJ", p32, h1), RP("DI", p32), 4032, ALU.bitwise_and)
+    ts(RP("DL", p32), RP("DJ", p32), EPS, ALU.mult)
+    dma(RP("F", S_(0, 1), S_(0, W)), RP("DL", p32, h0)); dma(RP("F", S_(1, 2), S_(0, W)), RP("DL", p32, h1))
+    for gq in range(1, 8):
+        dma(RP("F", S_(16 * gq, 16 * gq + 2), S_(0, W)), RP("F", S_(0, 2), S_(0, W)))
+    dma(R("T2", S_(T0, W)), R("F", S_(T0, W)))
+
+    def to_lanes(tau):
+        for b in range(2):
+            cp(R("X2", ALL, b, ALL), R("SN4", ALL, ALL, tau))
+        tr(R("XT"), R("X2"))
+        cp(R("S%d" % tau), IND(R("XT"), R("oT")))
+        cp(R("P%d" % tau), IND(R("XT"), R("oT")))
+
+    def ys_rows(tau):
+        ts(R("Yt"), R("ids", S_(128, 256)), 4096.0, ALU.mult)
+        tt(R("Yc"), R("Yt"), R("ids", S_(0, 128)), ALU.add)
+        for b in range(2):
+            cp(R("X2", S_(0, 8), b, ALL), R("Yc"), "a")
+        tr(R("XT", S_(0, 256)), R("X2", S_(0, 8)))
+        cp(R("YS", S_(tau, 512, 4)), IND(R("XT", S_(0, 256)), R("oT", S_(0, 8))))
+
+    def yb_rows(tau):
+        ts(R("Y1"), R("apf"), float(NONE), ALU.is_equal, -float(NONE + 1), ALU.mult)
+        for b in range(2):
+            tt(R("YB", b), R("Y1"), R("apf"), ALU.add)
+        tr(R("YBT"), R("YB"))
+        cp(R("B64", S_(tau, 64, 4)), IND(R("YBT"), R("oT", S_(0, 1))))
+
+    def zrep(tau):
+        for k in range(16):
+            o, a = R("ZT", ALL, k, ALL), R("Z4", ALL, ALL, tau)
+            if tau:
+                add("g", "asel", (o, a, [[0, 16], [0, 16]]), [a], [o])
+            else:
+                cp(o, a, "v" if k < tune["nz"] else "a")
+        n = 2 if tau else 4
+        for c in range(n):
+            dma(R("zr%d" % tau, S_(4096 // n * c, 4096 // n * (c + 1))), R("ZT", S_(16 // n * c, 16 // n * (c + 1))))
+
+    def diff(raw, dif, out, win, off, rep, c, nact, scale, ps=None, last=False, pos=None, sign=False):
+        na = min(2, max(0, nact - 2 * c))
+        b0, mid, b1 = 1024 * c, 1024 * c + 512 * na, 1024 * c + 1024
+        o = None
+        if na:
+            act(R(raw, S_(b0, mid)), IND(win, R(off, S_(b0 // 16, mid // 16))), ACT.Copy)
+        for h in range(na):
+            x = S_(b0 + 512 * h, b0 + 512 * h + 512)
+            mm([(R("p%d" % h), R("ID"), R(raw, x), True, False), (R("p%d" % h), R("NID"), R(rep, x), False, True)])
+            act(R(out, x), R("p%d" % h), ACT.Abs, 0.0, scale)
+            if sign:
+                act(R(raw, x), R("p%d" % h), ACT.Sign)
+        if na < 2:
+            x = S_(mid, b1)
+            o = tt(R(dif, x), IND(win, R(off, S_(mid // 16, b1 // 16))), R(rep, x), ALU.subtract)
+            if pos and not na:
+                dpass(ps, dif, c, neg=1 if scale > 1 else 2)
+                ts(R(pos, x), R(dif, x), 0.0, ALU.max, 2.0 * scale, ALU.mult)
+                dpass(ps, pos, c, last=last)
+                return o
+            act(R(out, x), R(dif, x), ACT.Abs, 0.0, scale)
+        if ps:
+            dpass(ps, out, c, last=last)
+        return o
+
+    parts = tune["parts"]
+    pbank = lambda c: "p2" if c < parts[0][1] else "p3"
+    ebank = "p3" if len(parts) == 1 else "p5"
+
+    def zdiff(c):
+        nz, mult = tune["zact"], tune["mult"]
+        diff("DC", "DC", "AC", R("Z"), "q16", "vr", c, nz, 1.0, "p4", False, "AC" if c >= 4 - tune["posc"] else None, mult)
+        if mult and 2 * c + 2 > nz:
+            x = R("DC", S_(max(1024 * c, 512 * nz), 1024 * c + 1024))
+            if c >= 4 - tune["nclip"]:
+                ts(x, x, -1.0, ALU.max, 1.0, ALU.min)
+            else:
+                act(x, x, ACT.Sign)
+
+    def first_dist(tau, nact):
+        for c in range(4):
+            diff("GR", "DS", "DS", R("V", S_(0, T0)), "S%d" % tau, "zr%d" % tau, c, nact, 8192.0)
+        dpass("p5", "DS", 0, True, True, 4096)
+        tt(R("P%d" % tau), R("p5", S_(0, L)), R("P%d" % tau), ALU.add)
+
+    def children(t):
+        win = R("T2", S_(0, T0 if t < 3 else W))
+        for (c0, c1) in parts:
+            for c in range(c0, c1):
+                act(ch("G2", c), IND(win, oc("S%d" % TILE[t], c)), ACT.Identity, 0.0, 1.0 / EPS)
+                dpass(ebank, "G2", c, True, True)
+                cp(oc("e16", c), oc(ebank, c))
+                act(oc("E4", c), oc(ebank, c), ACT.Identity, 4096.0)
+                mm([(oc(pbank(c), c), R("ID4"), oc("E4", c), c == c0, False)])
+
+    to_lanes(0)
+    zrep(0)
+    late = len(ops) - 1
+    dma(R("Z"), R("zs"))["after"] = late
+    dma(R("Q", S_(0, T0)), R("nq"))["after"] = late
+    children(0)
+    first_dist(0, tune["ds0"])
+    cp(R("B64"), R("BI"))
+    ts(R("Bt"), R("B64"), 0.0, ALU.is_lt, float(NONE + 1), ALU.mult)
+    tt(R("Bo"), R("Bt"), R("B64"), ALU.add)
+    for b in range(2):
+        cp(R("XB", ALL, b, ALL), R("Bo"))
+    tr(R("XBT"), R("XB"))
+    for h in range(4):
+        cp(R("B16", S_(h, 64, 4)), IND(R("XBT", S_(32 * h, 32 * h + 32)), R("oT", S_(0, 1))))
+    act(R("VBt"), IND(R("V"), R("B16")), ACT.Copy)
+    for h in range(2):
+        tt(R("VB", S_(512 * h, 512 * h + 512)), IND(R("F"), R("B16", S_(32 * h, 32 * h + 32))), R("VBt", S_(512 * h, 512 * h + 512)), ALU.add)
+    zrep(1)
+    iota(R("Q", S_(T0, W)), [[0, W - T0]], 0, 0)
+    zrep(2)
+    ts(R("Yc"), R("SN4", S_(8, 16), ALL, 3), 4096.0, ALU.mult)
+    tt(R("YS", S_(3, 512, 4)), R("Yc"), R("SN4", S_(0, 8), ALL, 3), ALU.add)
+    to_lanes(1)
+
+    ends = lambda n: R(n, S_(15, L, 16))
+    for t in range(RO):
+        tau = TILE[t]
+        n0 = T0 + L * t
+        ewin = R("V", S_(0, T0 if t == 0 else GB + L * (t - 1)))
+        vwin = R("V", S_(0, T0 if t == 0 else GB + L * t))
+        D1, D2, AR, WW = R("p3", S_(0, L)), R("p4", S_(0, L)), R("p2", S_(0, L)), R("p5", S_(0, L))
+        nz, mult = tune["zact"], tune["mult"]
+        act(ck, R("KX"), ACT.Identity, 0.0, 512.0)
+        if t > 0:
+            act(cx, R("KX"), ACT.Identity, 8192.0, -512.0)
+        for c in range(4):
+            diff("GR", "DA", "DA", ewin, "e16", "zr%d" % tau, c, (tune["actpath"] if t else tune["act0"]) + (4 * c - 6 if len(parts) > 1 else 0), 8192.0,
+                 pbank(c), c == 3, "GR" if c < tune["pos1"] else None)
+        if t > 0:
+            mm([(R("p4", S_(0, L)), R("ID"), R("LV", t - 1), True, False), (R("p4", S_(0, L)), R("NID"), R("Z", S_(tau, 1024, 4)), False, True)])
+            act(R("dg"), R("p4", S_(0, L)), ACT.Abs, 0.0, 8192.0)
+            dpass("p5", "dg", 0, True, True, 256)
+            act(R("mg"), R("dum"), ACT.Identity, float(GB + L * (t - 1)))
+            act(R("thm"), R("p5", S_(0, 16)), ACT.Identity, 8192.0)
+            tt(R("Pm"), R("p5", S_(0, 16)), R("mg"), ALU.add)
+            act(R("fl"), IND(R("Pm"), R("oB")), ACT.Copy)
+            act(R("p5", S_(L, 2 * L)), R("fl"), ACT.Copy)
+            cp(R("V", S_(GB + L * (t - 1), GB + L * t)), R("LV", t - 1), "a")
+        mm([(D2, R("BO"), R("cm32"), True, False)])
+        Pn = "Pj" if t else "Pi"
+        x0, x1 = R("p6", S_(0, L)), R("p6", S_(L, 2 * L))
+        for (c0, c1) in parts:
+            u0, u1, w0, w1 = 64 * c0, 64 * c1, 4 * c0, 4 * c1
+            A = lambda n, at=0: R(n, S_(at + u0, at + u1))
+            Bn = lambda n: R(n, S_(w0, w1))
+            en = lambda n: R(n, S_(u0 + 15, u1, 16))
+            of = lambda n: R(n, S_(0, w1 - w0))
+            o = tt(A("Pi"), A(pbank(c0)), A("P%d" % tau), ALU.min)
+            if c0:
+                o["after"] = ahead
+            if t > 0:
+                ts(A("dP"), A("Pi"), -8192, ALU.bitwise_and)
+                tt(A("kx"), A("dP"), A("p7"), ALU.add)
+                scan(A("sc1"), A("seg"), A("kx"), 0.0, ALU.mult, ALU.max)
+                tt(A("p6", L), A("p5", L), A("Pi"), ALU.subtract)
+                tt(Bn("cd"), Bn("thm"), en("sc1"), ALU.is_lt)
+                tt(Bn("tg"), Bn("cd"), en("sc1"), ALU.mult)
+                tt(A("tB"), IND(Bn("tg"), of("oB")), A("kx"), ALU.is_equal)
+                tt(A("p6"), A("p6", L), A("tB"), ALU.mult)
+                tt(A("Pj"), A("p6"), A("Pi"), ALU.add)
+            ts(A("dP"), A(Pn), -8192, ALU.bitwise_and)
+            tt(A("kx"), A("dP"), A("p7", L), ALU.add)
+            scan(A("sc2"), A("big"), A("kx"), 0.0, ALU.add, ALU.min)
+            ts(A("ids"), A(Pn), 4095, ALU.bitwise_and)
+            tt(A("tB"), IND(A("sc2"), of("oE")), A("kx"), ALU.is_equal)
+            scan(A("sc1"), A("seg"), A("kx"), 0.0, ALU.mult, ALU.max)
+            tt(A("p6"), A("tB"), A("ids"), ALU.mult)
+            scan(A("sc3"), A("seg"), A("p6"), 0.0, ALU.mult, ALU.add)
+            cp(Bn("a16"), en("sc3"))
+            cp(A("va"), IND(vwin, Bn("a16")), "a")
+            ahead = cp(A("q16"), IND(R("Q", S_(0, T0 if t == 0 else W)), Bn("a16")))["id"]
+            for k in range(16):
+                o, a = R("vr", S_(16 * u0 + k, 16 * u1, 16)), A("va")
+                nv, ng = (tune["nv_copy"], tune["ng"]) if c1 == 4 else (tune["nv_first"], tune["ng_first"])
+                if k >= 16 - ng:
+                    add("g", "asel", (o, a, [[0, u1 - u0]]), [a], [o])
+                else:
+                    cp(o, a, "v" if k < nv else "a")
+            if c1 < 4:
+                for c in range(c0, c1):
+                    zdiff(c)
+        ts(R("lv"), ends("sc1"), 8192.0 * KILL, ALU.is_ge)
+        ts(R("t1"), ends("sc3"), -float(NONE), ALU.add)
+        tt(R("t2"), R("t1"), R("lv"), ALU.mult)
+        ts(R("ap16"), R("t2"), float(NONE), ALU.add)
+        act(R("apf"), R("t2"), ACT.Identity, float(NONE))
+        tt(R("t3"), R("t1"), R("dum"), ALU.subtract)
+        tt(R("aD"), R("t3"), R("lv"), ALU.mult)
+        act(R("nFa"), IND(R("F"), R("a16")), ACT.Identity, 0.0, -1.0)
+        tt(R("VB", S_(tau, 1024, 4)), IND(R("F"), R("ap16")), R("va"), ALU.add)
+        mm([(AR, R("BO"), R("nFa"), True, True)])
+        mm([(D1, R("BO"), R("nFa"), True, False)])
+        if t < RO - 1:
+            cp(R("Q", S_(n0, n0 + L)), R("q16"))
+            add("g", "send", (R("LQ", t), R("Q", S_(n0, n0 + L)), "aq%d" % t, HOPS[t]), [R("Q", S_(n0, n0 + L))], [])
+            add(None, "recv", "aq%d" % t, [], [R("LQ", t)], after=len(ops) - 1)
+            dma(R("Q", S_(GB + L * t, GB + L * t + L)), R("LQ", t))
+        ts(R("ar16"), AR, -1.0 / EPS, ALU.mult)
+        for h in range(16):
+            ts(R("E", h, S_(0, L - 16 * h)), R("ar16", S_(16 * h, L)), R("apf", S_(h, h + 1)), ALU.is_equal)
+        mm([(WW, R("DW"), R("E", ALL, S_(0, 16)), True, False)] +
+           [(R("p5", S_(16 * h + 16, L)), R("BOW"), R("E", h, S_(16, L - 16 * h)), False, h == 14) for h in range(15)])
+        tt(R("fl"), WW, R("thr"), ALU.is_lt)
+        scan(R("sc4"), R("seg"), R("fl"), 0.0, ALU.mult, ALU.add)
+        tt(R("t3"), ends("sc4"), R("aD"), ALU.mult)
+        tt(R("t3"), R("t3"), R("dum"), ALU.add)
+        ts(R("o16"), R("t3"), float(W), ALU.add)
+        sca = cp(IND(R("T2"), R("o16")), R("F", S_(n0, n0 + L)))
+        for c in range(4):
+            o = diff(None, "DB", "DB", R("VB"), "q16", "vr", c, 0, 1.0, "p3", c == 3, "DA" if c >= 4 - tune["posb"] else None)
+            if c == tune["early"] and t < RO - 1:
+                o["after"] = sca["id"]
+        act(R("A1"), D1, ACT.Abs)
+        act(R("wx", 0), D1, ACT.Relu, -8800.0, 8.0)
+        act(R("wx", 1), R("A1"), ACT.Relu, 2048.0, -2.0 ** 26)
+        for c in range(parts[-1][0], 4):
+            zdiff(c)
+        mm([(D2, R("ID"), R("wx", 0), False, False), (D2, R("NID"), R("wx", 1), False, True)])
+        act(R("lo"), R("va"), ACT.Relu, -2.0)
+        act(R("hi"), R("va"), ACT.Relu, 61.0, -1.0)
+        act(R("hi"), R("hi"), ACT.Identity, 63.0, -1.0)
+        H = x1
+        banks = ["p2", "p3", "p7", "p5", "p0", "p1", "p4", "p7"]
+
+        def pre(b):
+            lst = []
+            for j in range(2):
+                k = 2 * b + j
+                lst.append((R(banks[b], S_(L * j, L * j + L)), R("ID"), R("DC", S_(k, 4096, 16)), j == 0, False))
+                if nz:
+                    lst.append((R(banks[b], S_(L * j, L * j + 32 * nz)), R("NID"), R("va", S_(0, 32 * nz)), False, False))
+            mm(lst)
+
+        for b in range(0 if mult else 6):
+            pre(b)
+        o = tt(R("att"), D2, R("A1"), ALU.is_lt if mult else ALU.is_ge)
+        if tune["early"] == 8 and t < RO - 1:
+            o["after"] = sca["id"]
+        mm([(H, R("ID"), R("va"), True, False)])
+        if mult:
+            if t < RO - 1:
+                children(t + 1)
+            for b in range(8):
+                pb = ["p0", "p1", "p5", "p7"][b % 4]
+                mm([(R(pb, S_(L * j, L * j + L)), R("EXP", 2 * b + j), R("att"), j == 0, j == 1) for j in range(2)])
+                for j in range(2):
+                    tt(R("U", b, S_(L * j, L * j + L)), R("DC", S_(2 * b + j, 4096, 16)), R(pb, S_(L * j, L * j + L)), ALU.mult)
+                mm([(H, R("ID"), R("U", b, S_(L * j, L * j + L)), False, False) for j in range(2)])
+        else:
+            pre(6)
+        for b in range(0 if mult else 8):
+            pb = banks[b]
+            mm([(R(pb, S_(L * j, L * j + L)), R("EXP", 2 * b + j), R("att"), False, j == 1) for j in range(2)])
+            if b in tune["sact"] or (t == RO - 1 and b % 2):
+                act(R("U", b), R(pb), ACT.Sign)
+            else:
+                ts(R("U", b), R(pb), -1.0, ALU.max, 1.0, ALU.min)
+            if b == 2:
+                pre(7)
+            if b == (1 if len(parts) == 1 else 3) and t < RO - 1:
+                children(t + 1)
+            if b == 0:
+                mm([(H, R("BO"), R("att"), False, False)])
+            mm([(H, R("ID"), R("U", b, S_(L * j, L * j + L)), False, b == 7 and j == 1) for j in range(2)])
+        tt(x0, H, R("lo"), ALU.max)
+        tt(R("V", S_(n0, n0 + L)), x0, R("hi"), ALU.min)
+        if t < RO - 1:
+            add("g", "send", (R("LV", t), R("V", S_(n0, n0 + L)), "av%d" % t, HOPS[t]), [R("V", S_(n0, n0 + L))], [])
+            add(None, "recv", "av%d" % t, [], [R("LV", t)], after=len(ops) - 1)
+        dma(R("yv", S_(L * t, L * t + L)), R("V", S_(n0, n0 + L)))
+        if tau in TILE[t + 1:]:
+            cp(R("S%d" % tau), R("ids"))
+            ts(R("P%d" % tau), R(Pn), -4097, ALU.bitwise_and)
+        else:
+            ys_rows(tau)
+            yb_rows(tau)
+        if t == 0:
+            first_dist(1, tune["dsact"])
+            to_lanes(2)
+        if t == 1:
+            first_dist(2, tune["dsact"])
+    dma(R("ys"), R("YS")); dma(R("yb"), R("B64"))
+    dma(R("YL"), RP("T2", S_(0, 128, 16), S_(0, W))); dma(R("YH"), RP("T2", S_(1, 128, 16), S_(0, W)))
+    tt(R("YK"), R("YL"), R("YH"), ALU.add)
+    ts(R("YK"), R("YK"), 1.0 / EPS, ALU.mult)
+    dma(R("yk"), R("YK"))
+
+    hist = {}
+    for o in ops:
+        dep = set()
+        acc = [(r, False) for r in o["rd"]] + [(r, True) for r in o["wr"]]
+        for r, wr in acc:
+            fb, pb = _foot(r)[:2]
+            ps = _where(r["n"]) == "psum"
+            for (j, fb2, pb2, wr2) in hist.get(r["n"], []):
+                if j == o["id"]:
+                    continue
+                if ps and o["eng"] == "p" and ops[j]["eng"] == "p":
+                    if ops[j]["group"] != o["group"] or j == o["group"]:
+                        dep.add(j)
+                elif (ps and ops[j]["eng"] != o["eng"]) or ((wr or wr2) and (fb & fb2) and (pb & pb2)):
+                    dep.add(j)
+        for r, wr in acc:
+            fb, pb = _foot(r)[:2]
+            hist.setdefault(r["n"], []).append((o["id"], fb, pb, wr))
+        if "after" in o:
+            dep.add(o["after"])
+        o["dep"] = dep
+    return ops
+
+
+def cost(o, m):
+    cyc = 0.83 * m["f"]
+    k, a = o["kind"], o["args"]
+    if k == "recv":
+        return 0.0, m["rem"]
+    if k == "send":
+        return 300.0, 1000.0
+    if k == "dma":
+        fo, fi = _foot(a[0]), _foot(a[1])
+        by = fo[2] * fo[3] * (2 if _dtype(a[0]["n"]) in (B, U2) else 4)
+        return 60.0, m["dma"] + by / 150.0 + 5.0 * max(fo[3], fi[3])
+    if k == "mm":
+        d = sum(max(64, _foot(x[2])[2]) * (4 if _dtype(x[2]["n"]) == F4 else 1) for x in a) * m["pe"] * m["f"]
+        return d, d + 100.0
+    n = _count(a[0])
+    if k == "iota":
+        d = 130.0 + 2 * n * cyc
+    elif k == "asel":
+        d = 170.0 + 2 * n * cyc
+    elif a[0]["off"] is not None:
+        d = 50.0 + n * m["sca"] * cyc
+    elif isinstance(a[1], dict) and a[1]["off"] is not None:
+        d = 60.0 + n * m["ga"] * cyc
+    else:
+        big = [x for x in a if isinstance(x, dict) and _foot(x)[2] > 1]
+        two = all(_dtype(x["n"]) in (B, U2) for x in big)
+        if k == "tt":
+            c = 2.0 if _where(a[1]["n"]) == "sbuf" and _where(a[2]["n"]) == "sbuf" else 1.0
+        elif k in ("act", "red"):
+            c = 1.0
+        else:
+            c = 0.5 if two else 1.0
+        d = max(64.0, n * c) * cyc + m["ov"]
+    return d, d
+
+
+def _pass(ops, cs, nxt, nprev, pr, m, back, hold):
+    n = len(ops)
+    left = list(nprev)
+    ready = [(cs[i][1] - cs[i][0]) if back else 0.0 for i in range(n)]
+    cand = {}
+    for i in range(n):
+        if left[i] == 0:
+            cand.setdefault(ops[i]["eng"], []).append(i)
+    free = {}
+    order, start, end = [], [0.0] * n, 0.0
+    while len(order) < n:
+        best = None
+        for e, lst in cand.items():
+            if not lst:
+                continue
+            fr = free.get(e, 0.0) if e else 0.0
+            lst.sort(key=lambda i: -pr[i])
+            soon = 1e30
+            for i in lst:
+                st = max(ready[i], fr)
+                if (e is None or soon >= st + cs[i][0] * hold) and (best is None or (st, -pr[i]) < best[0]):
+                    best = ((st, -pr[i]), i)
+                soon = min(soon, st)
+        (st, _), i = best
+        e = ops[i]["eng"]
+        cand[e].remove(i)
+        order.append(i)
+        start[i] = st
+        end = max(end, st + (cs[i][0] if back else cs[i][1]))
+        if e:
+            free[e] = st + cs[i][0]
+        for j in nxt[i]:
+            lat = (0.0 if e == "p" else m["lat0"]) if ops[j]["eng"] == e else m["lat"]
+            ready[j] = max(ready[j], st + (cs[i][0] + cs[j][1] - cs[j][0] if back else cs[i][1]) + lat)
+            left[j] -= 1
+            if left[j] == 0:
+                cand.setdefault(ops[j]["eng"], []).append(j)
+    return order, start, end
+
+
+def schedule(ops, m, turns=4, tries=60, moves=12000):
+    n = len(ops)
+    cs = [cost(o, m) for o in ops]
+    pred = [sorted(o["dep"]) for o in ops]
+    succ = [[] for _ in ops]
+    for o in ops:
+        for j in o["dep"]:
+            succ[j].append(o["id"])
+    best = None
+    for hold in m["holds"]:
+        pr = [0.0] * n
+        for i in range(n - 1, -1, -1):
+            pr[i] = cs[i][1] + max([pr[j] + m["lat"] for j in succ[i]] + [0.0])
+        for _ in range(turns):
+            order, st, end = _pass(ops, cs, succ, [len(x) for x in pred], pr, m, False, hold)
+            if best is None or end < best[0]:
+                best = (end, order, [st[i] + cs[i][0] for i in range(n)])
+            _o, bs, _e = _pass(ops, cs, pred, [len(x) for x in succ], [st[i] + cs[i][0] for i in range(n)], m, True, hold)
+            pr = [bs[i] + cs[i][0] for i in range(n)]
+    rng = np.random.default_rng(7)
+    for _ in range(tries):
+        hold = float(rng.choice(m["holds"]))
+        at = np.array(best[2])
+        near = np.abs(at - rng.random() * best[0]) < float(rng.choice([3000.0, 8000.0]))
+        pr = (at + near * rng.normal(0.0, float(rng.choice([300.0, 1500.0, 4000.0])), n)).tolist()
+        order, st, end = _pass(ops, cs, succ, [len(x) for x in pred], [-x for x in pr], m, False, hold)
+        if end < best[0]:
+            best = (end, order, [st[i] + cs[i][0] for i in range(n)])
+        for _ in range(1):
+            _o, bs, _e = _pass(ops, cs, pred, [len(x) for x in succ], pr, m, True, hold)
+            order, st, end = _pass(ops, cs, succ, [len(x) for x in pred], [bs[i] + cs[i][0] for i in range(n)], m, False, hold)
+            pr = [st[i] + cs[i][0] for i in range(n)]
+            if end < best[0]:
+                best = (end, order, pr)
+    return _polish(ops, best[1], m, moves) if moves else best[1]
+
+
+def _polish(ops, order, m, moves):
+    n = len(ops)
+    anc = [0] * n
+    pred = []
+    for o in ops:
+        far = 0
+        for j in o["dep"]:
+            far |= anc[j]
+        pred.append([j for j in o["dep"] if not (far >> j) & 1])
+        for j in o["dep"]:
+            far |= 1 << j
+        anc[o["id"]] = far
+    eng = [o["eng"] for o in ops]
+    tabs = []
+    for ch in m["also"]:
+        x = dict(m, **ch)
+        cs = [cost(o, x) for o in ops]
+        tabs.append((cs, [[(j, cs[j][1] + ((0.0 if eng[i] == "p" else x["lat0"]) if eng[j] == eng[i] else x["lat"])) for j in pred[i]] for i in range(n)]))
+
+    def run(od, tab):
+        cs, pl = tab
+        st = [0.0] * n
+        by = [-1] * n
+        free = {}
+        end, last = 0.0, -1
+        for i in od:
+            s, w = free.get(eng[i], (0.0, -1))
+            for j, d in pl[i]:
+                if st[j] + d > s:
+                    s, w = st[j] + d, j
+            st[i], by[i] = s, w
+            if eng[i]:
+                free[eng[i]] = (s + cs[i][0], i)
+            if s + cs[i][1] > end:
+                end, last = s + cs[i][1], i
+        return end, by, last
+
+    base = [run(order, t) for t in tabs]
+    norm = [b[0] for b in base]
+    cur = float(len(tabs))
+    best = (cur, order)
+    rng = np.random.default_rng(11)
+    for it in range(moves):
+        _e, by, i = base[int(rng.integers(len(tabs)))]
+        pairs = []
+        while by[i] >= 0:
+            if eng[by[i]] == eng[i] and not (anc[i] >> by[i]) & 1:
+                pairs.append((by[i], i))
+            i = by[i]
+        if not pairs:
+            continue
+        p, i = pairs[int(rng.integers(len(pairs)))]
+        a, b = order.index(p), order.index(i)
+        if rng.random() < 0.5:
+            for _ in range(int(rng.integers(0, 4))):
+                c = a - 1
+                while c >= 0 and eng[order[c]] != eng[i]:
+                    c -= 1
+                if c < 0 or (anc[i] >> order[c]) & 1:
+                    break
+                a = c
+            mid = order[a:b + 1]
+            new = order[:a] + [x for x in mid if x == i or (anc[i] >> x) & 1] + [x for x in mid if x != i and not (anc[i] >> x) & 1] + order[b + 1:]
+        else:
+            for _ in range(int(rng.integers(0, 12))):
+                c = b + 1
+                while c < n and eng[order[c]] != eng[i]:
+                    c += 1
+                if c >= n or (anc[order[c]] >> p) & 1:
+                    break
+                b = c
+            mid = order[a:b + 1]
+            new = order[:a] + [x for x in mid if x != p and not (anc[x] >> p) & 1] + [x for x in mid if x == p or (anc[x] >> p) & 1] + order[b + 1:]
+        res = [run(new, t) for t in tabs]
+        val = sum(r[0] / z for r, z in zip(res, norm))
+        if val <= cur + 0.002 * (1.0 - it / moves) * rng.random():
+            order, base, cur = new, res, val
+            if val < best[0]:
+                best = (val, new)
+    return best[1]
+
+
+_PLAN = []
+
+
+def plan():
+    if not _PLAN:
+        ops = build_ops(TUNE)
+        _PLAN.append((ops, schedule(ops, NOM)))
+    return _PLAN[0]
+
+
+def rank_program(g, core, T, topo):
+    rank = T.rank_of(core)
+    if rank is None:
+        return
+    ops, order = plan()
+    qs = {"v": g.vector, "a": g.scalar, "p": g.tensor, "g": g, "s": g.sync}
+    known = {e: {} for e in qs}
+    done = {}
+    cnt = {e: 0 for e in CNT}
+    ndma = [0]
+    final = {}
+    nr = len(T.cores)
+    closes = {ops[i]["group"]: i for i in order if ops[i]["eng"] == "p"}
+
+    def lanes(src, dst):
+        en = topo.engines(src, dst)[::2]
+        return sum(1 << x for x in en), len(en)
+
+    for i in order:
+        o = ops[i]
+        e, k, a = o["eng"], o["kind"], o["args"]
+        if k == "recv":
+            src = T.cores[(rank - ops[o["after"]]["args"][3]) % nr]
+            done[i] = (a, lanes(src, core)[1], {})
+            final[a] = done[i][1]
+            continue
+        q = qs[e]
+        kn = known[e]
+        need = {}
+        for j in o["dep"]:
+            if e == "p" and ops[j]["eng"] == "p":
+                continue
+            need[j] = done[j]
+        for j in sorted(need, reverse=True):
+            s, v, imp = need[j]
+            top = max(x[1] for x in need.values() if x[0] == s)
+            if kn.get(s, 0) < v and v == top:
+                q.wait_ge(T.sem[s], v)
+                kn[s] = v
+                for s2, v2 in imp.items():
+                    kn[s2] = max(kn.get(s2, 0), v2)
+        x = [_ap(T, r) for r in a] if k != "mm" else None
+        if k == "send":
+            dst = T.cores[(rank + a[3]) % nr]
+            rid, pid, _ = topo.addr(dst)
+            mask, ne = lanes(core, dst)
+            g.remote_dma(x[0], x[1], T.sem[a[2]], T.sem["snt"], pid, rid, mask)
+            final["snt"] = final.get("snt", 0) + ne
+            done[i] = ("snt", final["snt"], dict(kn))
+            continue
+        if k == "dma":
+            s = "d%d" % ndma[0]
+            ndma[0] += 1
+            q.dma_start(x[0], x[1]).then_inc(T.sem[s], 16)
+            done[i] = (s, 16, dict(kn))
+            final[s] = 16
+            continue
+        if k == "copy":
+            ins = q.tensor_copy(x[0], x[1])
+        elif k == "tt":
+            ins = q.tensor_tensor(x[0], x[1], x[2], x[3])
+        elif k == "ts":
+            ins = q.tensor_scalar(x[0], x[1], x[2], None, x[4]) if x[5] is None else q.tensor_scalar(x[0], x[1], x[2], x[3], x[4], x[5])
+        elif k == "scan":
+            ins = q.tensor_tensor_scan(x[0], x[1], x[2], x[3], x[4], x[5])
+        elif k == "tr":
+            ins = q.transpose(x[0], x[1])
+        elif k == "ms":
+            ins = q.memset(x[0], x[1])
+        elif k == "red":
+            ins = q.tensor_reduce(x[0], x[1], AxisListType.X, ALU.add)
+        elif k == "act":
+            ins = q.activation(x[0], x[1], x[2], bias=x[3], scale=x[4])
+        elif k == "iota":
+            if _dtype(a[0]["n"]) == I4:
+                ins = q.iota(x[0], x[1], x[2], x[3])
+            else:
+                ins = q.iota(x[0], x[1], x[2], x[3], allow_small_or_imprecise_dtypes=True)
+        elif k == "asel":
+            ins = q.affine_select(x[0], x[1], x[2], ALU.is_ge, 0.0, 0, 0)
+        else:
+            for z, (po, lt, rh, st, sp) in enumerate(a):
+                ins = q.matmul(_ap(T, po), _ap(T, lt), _ap(T, rh), st, closes[o["group"]] == i and z == len(a) - 1)
+        cnt[e] += 1
+        ins.then_inc(T.sem[CNT[e]], 1)
+        imp = dict(kn)
+        imp[CNT[e]] = cnt[e]
+        done[i] = (CNT[e], cnt[e], imp)
+        final[CNT[e]] = cnt[e]
+    for s, v in final.items():
+        g.sync.wait_ge(T.sem[s], v)

@@ -6,8 +6,10 @@ T0, L, RO, KILL = 1536, 256, 5, 200
 TILE = [0, 1, 2, 1, 2]
 HOPS = [1, 1, 1, 1]
 GB, W = T0 + L * RO, T0 + L * (2 * RO - 1)
-NONE = W
+NONE = GB - 1
 EPS = 2.0 ** -15
+DU, TIE, BIG = 16384.0, 4096.0, 2.0 ** 24
+RND = 1.5 * 2.0 ** 37
 ALU = AluOpType
 ACT = ActivationFunctionType
 
@@ -18,49 +20,52 @@ def _s(shape, d):
     return ("sbuf", [128] + list(shape), d)
 
 
+CUBE = [4096]
+NARROW = (("th1", "th3", "Pm", "mg", "sg1", "dd", "apf", "t1", "t2", "Y1", "dumW", "nz0", "nz1", "nz2"), ("Ri", "ai", "pI", "pJ"),
+          ("a16", "ap16", "o16", "oT", "oB", "oP0", "oP1", "oP2"))
+AT = {n: (b, 16 * i) for b, ns in zip(("nf4", "ni4", "nu2"), NARROW) for i, n in enumerate(ns)}
 SCRATCH = {
-    "V": _s([W + 16], B), "F": _s([W + 16], B), "T2": _s([W + L], B), "Q": _s([W], I4),
-    "Z": _s([1024], B), "VB": _s([1024], F4), "VBt": _s([1024], B),
-    "SN4": _s([16, 16, 4], I4), "KI": _s([96], I4), "KJ": _s([96], I4), "KK": _s([96], I4), "KL": _s([96], B), "KH": _s([96], B),
+    "V": _s([W], B), "F": _s([W + 16], B), "T2": _s([W + L], B), "Q": _s([W], I4),
+    "Z": _s([1024], B), "VB": _s([1024], F4), "VBt": _s([1024], B), "ZS": _s([480], B),
+    "SN": _s([1024], I4), "KI": _s([2, 96], I4), "KJ": _s([2, 96], I4), "KK": _s([2, 96], I4), "KL": _s([2, 96], B), "KH": _s([2, 96], B),
     "DI": _s([120], I4), "DJ": _s([240], I4), "DL": _s([240], B),
     "BI": _s([64], I4), "B64": _s([64], F4), "Bt": _s([64], F4), "Bo": _s([4, 16], F4), "B16": _s([64], U2),
-    "XB": _s([4, 2, 16], F4), "XBT": _s([128], F4), "Y1": _s([16], F4), "YB": _s([2, 16], F4), "YBT": _s([32], F4),
-    "X2": _s([16, 2, 16], F4), "XT": _s([512], F4), "YS": _s([512], F4), "Yt": _s([128], F4), "Yc": _s([8, 16], F4),
+    "XB": _s([4, 2, 16], F4), "XBT": _s([128], F4), "YB": _s([2, 16], F4), "YBT": _s([32], F4),
+    "X2": _s([8, 2, 16], F4), "XT": _s([256], F4), "YS": _s([512], F4), "Yt": _s([128], F4), "Yc": _s([8, 16], F4),
     "YL": _s([240], B), "YH": _s([240], B), "YK": _s([240], F4),
-    "zr0": _s([4096], B), "zr1": _s([4096], B), "zr2": _s([4096], B), "ZT": _s([16, 16, 16], B), "Z4": _s([16, 16, 4], B),
-    "S0": _s([L], U2), "S1": _s([L], U2), "S2": _s([L], U2),
-    "P0": _s([L], I4), "P1": _s([L], I4), "P2": _s([L], I4),
-    "G2": _s([4096], B), "DA": _s([4096], B), "DS": _s([4096], B), "DB": _s([4096], B),
-    "DC": _s([4096], B), "AC": _s([4096], B), "U": _s([8, 2 * L], B), "vr": _s([4096], B), "GR": _s([4096], B),
+    "zr0": _s(CUBE, B), "zr1": _s(CUBE, B), "zr2": _s(CUBE, B), "ZT": _s([16, 16, 16], B), "Z4": _s([16, 16, 4], B),
+    "Zp": _s([L], B), "Pp": _s([L], F4),
+    "S0": _s([L], U2), "S1": _s([L], U2), "S2": _s([L], U2), "Ps": _s([L], F4), "K1": _s([L], I4), "K2": _s([L], I4),
+    "G2": _s(CUBE, B), "DA": _s(CUBE, B), "DS": _s(CUBE, B), "DB": _s(CUBE, B),
+    "DC": _s(CUBE, B), "AC": _s([16, 128], B), "U": _s([8, 2 * L], B), "vr": _s(CUBE, B), "GR": _s(CUBE, B),
     "E": _s([16, L], B), "e16": _s([L], U2), "q16": _s([L], U2), "ar16": _s([L], U2),
-    "Pi": _s([L], I4), "Pj": _s([L], I4), "dP": _s([L], I4), "ids": _s([L], I4),
-    "kx": _s([L], F4), "sc1": _s([L], F4), "sc2": _s([L], F4), "sc3": _s([L], F4), "tB": _s([L], F4),
-    "tg": _s([16], F4), "cd": _s([16], F4), "Pm": _s([16], F4), "thm": _s([16], F4), "lv": _s([16], F4),
-    "t1": _s([16], F4), "t2": _s([16], F4), "t3": _s([16], F4), "aD": _s([16], F4), "apf": _s([16], F4),
-    "a16": _s([16], U2), "ap16": _s([16], U2), "o16": _s([16], U2),
-    "va": _s([L], B), "nFa": _s([L], B), "lo": _s([L], B), "hi": _s([L], B), "dg": _s([L], B), "att": _s([L], B),
-    "A1": _s([L], F4), "wx": _s([2, L], B), "fl": _s([L], F4), "sc4": _s([L], F4),
-    "LV": _s([4, L], B), "LQ": _s([4, L], I4),
-    "pI": _s([16], I4), "pJ": _s([16], I4), "pc": _s([16], F4), "XI": _s([144], F4), "CG": _s([128], F4), "KX": _s([L], F4),
-    "SEL": _s([3, 144], B), "BO": _s([128], B), "BOW": _s([128], B), "DW": _s([128], B), "ID": _s([128], B), "NID": _s([128], B),
-    "EXP": _s([16, 128], B), "M16": _s([L], F4), "thr": _s([L], F4), "seg": _s([L], F4), "big": _s([L], F4),
-    "E4": _s([L], F4), "ID4": _s([128], F4), "cm32": _s([L], B), "pw": _s([16], F4), "hz": _s([2, 16], F4),
-    "dum": _s([16], F4), "mg": _s([16], F4), "oT": _s([16], U2), "oB": _s([16], U2), "oE": _s([16], U2), "oI": _s([3, 16], I4),
-    "p0": ("psum", [128, 512], F4), "p1": ("psum", [128, 512], F4),
-    "p2": ("psum", [128, 512], F4), "p3": ("psum", [128, 512], F4), "p4": ("psum", [128, 512], F4),
-    "p5": ("psum", [128, 512], F4), "p6": ("psum", [128, 512], F4), "p7": ("psum", [128, 512], F4),
+    "P1": _s([L], F4), "P2": _s([L], F4), "Pi": _s([L], I4), "ids": _s([L], I4), "Pmb": _s([L], F4),
+    "sc1": _s([L], F4), "sc2": _s([L], F4), "sc3": _s([L], F4), "sc4": _s([L], F4),
+    "FL": _s([L + 16], B), "FM": _s([L + 16], B), "lo": _s([L], B), "hi": _s([L], B), "x0": _s([L], B), "cnt": _s([L], B), "cx": _s([L], B), "nf": _s([L], B),
+    "nf4": _s([16 * len(NARROW[0])], F4), "ni4": _s([16 * len(NARROW[1])], I4), "nu2": _s([16 * len(NARROW[2])], U2),
+    "sgn": _s([L + 16], B), "IDH": _s([128], B), "IDT": _s([128], B),
+    "va": _s([L], B), "nFa": _s([L], B), "tk": _s([L], B), "cl": _s([L], B), "dg": _s([16, 16], B), "att": _s([L], B),
+    "A1": _s([L], F4), "wx": _s([2, L], B), "fl": _s([L], B), "E4": _s([L], F4),
+    "pc": _s([8], F4), "XI": _s([148], F4), "CG": _s([128], F4), "KX": _s([L], F4),
+    "SEL": _s([6, 144], B), "BO": _s([128], B), "DW": _s([128], B), "ID": _s([128], B), "NID": _s([128], B),
+    "IDB": _s([128], B), "NIDB": _s([128], B), "QN": _s([128], B), "MAP": _s([128], B), "ID4": _s([128], F4),
+    "EXP": _s([16, 128], B), "thr": _s([L], F4), "seg": _s([L], B), "big": _s([L], B), "stp": _s([L], B),
+    "cm32": _s([L], B), "one": _s([L], B), "oI": _s([3, 16], I4),
 }
+SCRATCH.update({"p%d" % i: ("psum", [128, 512], F4) for i in range(8)})
 IO = {"vn": ([128, T0], B), "zs": ([128, 1024], B), "sn": ([128, 1024], I4), "nq": ([128, T0], I4), "kid": ([8, T0], I4),
       "bst": ([8, 1024], I4), "yv": ([128, L * RO], B), "ys": ([128, 512], F4), "yk": ([8, W], F4), "yb": ([8, 1024], F4)}
-NDMA = 48
+NDMA = 56
 SEMAPHORES = ["cv", "ca", "cp", "cg", "snt"] + ["d%d" % i for i in range(NDMA)] + ["av%d" % i for i in range(4)] + ["aq%d" % i for i in range(4)]
 CNT = {"v": "cv", "a": "ca", "p": "cp", "g": "cg"}
 S_ = slice
 ALL = slice(None)
-TUNE = {"nv_copy": 10, "zact": 5, "actpath": 2, "act0": 2, "dsact": 2, "pos1": 0, "posb": 0, "posc": 0, "mult": 0, "nclip": 2,
-        "parts": ((0, 4),), "nv_first": 0, "ng": 4, "ng_first": 5, "nz": 11, "sact": (), "ds0": 0, "early": 8}
-NOM = {"f": 1.25, "ga": 1.56, "sca": 3.5, "pe": 0.42, "ov": 45.0, "lat": 110.0, "lat0": 60.0, "dma": 2000.0, "rem": 3000.0, "holds": (0.3, 0.7, 1.0),
-       "also": ({}, {"ga": 1.2, "sca": 2.5, "f": 1.1, "lat": 200.0, "lat0": 100.0}, {"ga": 1.9, "sca": 5.0, "f": 1.4, "pe": 0.5})}
+TUNE = {"zact": [4, 4, 3, 3, 3], "eact": [3, 1, 1, 2, 2], "epos": [0, 0, 0, 0, 0], "bpos": [0, 0, 0, 0, 0], "sact": [(1, 3, 5, 7)] * 5,
+        "g2v": [(), (), (), (), ()], "lowv": [1, 1, 0, 0, 0], "lohi": 1,
+        "parts": ((0, 4),), "ng": 6, "na": 0, "z0": (7, 5), "eqv": 1, "hold": (9, 9), "e4": 1, "keep": 0}
+NOM = {"f": 1.25, "ga": 1.56, "sca": 3.5, "pe": 0.42, "ov": 45.0, "lat": 110.0, "lat0": 60.0, "dma": 2000.0, "rem": 3000.0, "holds": (0.3, 0.7, 1.0), "spans": (300, 200, 300), "heat": 400.0,
+       "also": ({"ga": 1.25, "sca": 2.5, "f": 1.08, "lat": 230.0, "lat0": 140.0},
+                {"ga": 1.8, "sca": 5.0, "f": 1.4, "lat": 400.0, "lat0": 300.0, "rem": 6000.0, "dma": 3000.0}, {"ga": 1.2, "f": 1.2, "pe": 0.56})}
 
 
 def _shape(n):
@@ -76,6 +81,9 @@ def _where(n):
 
 
 def R(n, *ix):
+    if n in AT:
+        a, b = ix[0].indices(16)[:2] if ix else (0, 16)
+        n, ix = AT[n][0], (S_(AT[n][1] + a, AT[n][1] + b),)
     return {"n": n, "p": ALL, "ix": ix, "off": None}
 
 
@@ -120,14 +128,9 @@ def build_ops(tune):
     group = {}
 
     def add(eng, kind, args, reads, writes, **kw):
-        rd = []
-        for r in reads:
-            if isinstance(r, dict):
-                rd.append(r)
-        for r in list(rd) + list(writes):
-            if r["off"] is not None:
-                rd.append(r["off"])
-        o = {"eng": eng, "kind": kind, "args": args, "rd": rd, "wr": list(writes), "id": len(ops), "prio": 0.0}
+        rd = [r for r in reads if isinstance(r, dict)]
+        rd += [r["off"] for r in rd + list(writes) if r["off"] is not None]
+        o = {"eng": eng, "kind": kind, "args": args, "rd": rd, "wr": list(writes), "id": len(ops)}
         o.update(kw)
         ops.append(o)
         return o
@@ -135,6 +138,8 @@ def build_ops(tune):
     def cp(out, a, eng="v"):
         if eng == "a":
             return act(out, a, ACT.Copy)
+        if eng == "g":
+            return asel(out, a, [[0, _count(out)]], ALU.is_ge, 0.0, 0, 0)
         return add("v", "copy", (out, a), [a], [out])
 
     def tt(out, a, b, op):
@@ -155,79 +160,98 @@ def build_ops(tune):
     def act(out, a, fn, bias=0.0, scale=1.0):
         return add("a", "act", (out, a, fn, bias, scale), [a, bias, scale], [out])
 
-    def mm(lst):
+    def mm(lst, more=False):
         bank = lst[0][0]["n"]
         if lst[0][3]:
             group[bank] = len(ops)
-        return add("p", "mm", lst, [x for m in lst for x in m[1:3]], [m[0] for m in lst], group=group[bank])
+        return add("p", "mm", lst, [x for m in lst for x in m[1:3]], [m[0] for m in lst], group=group[bank], more=more)
 
     def iota(out, pat, base, cm):
         return add("g", "iota", (out, pat, base, cm), [], [out])
 
+    def asel(out, a, pat, op, fill, base, cm):
+        return add("g", "asel", (out, a, pat, op, fill, base, cm), [a], [out])
+
     def dma(out, a, eng="s"):
         return add(eng, "dma", (out, a), [a], [out])
 
-    def dpass(ps, src, c, first=False, last=False, n=1024, neg=0):
-        w = n // 16
-        return mm([(R(ps, S_(w * c, w * c + w)), R("SEL", neg, S_(15 - m, 143 - m)), R(src, S_(n * c + m, n * (c + 1), 16)), first and m == 0, last and m == 15)
+    def send(name, t, c0, sem):
+        land = R(name, S_(GB + L * t, GB + L * t + L))
+        add("g", "send", (land, R(name, S_(c0, c0 + L)), sem, HOPS[t]), [R(name, S_(c0, c0 + L))], [])
+        add(None, "recv", sem, [], [land], after=len(ops) - 1)
+
+    def dpass(ps, src, c0, c1, sel, first=False, mid=False):
+        if mid:
+            return mm([(R(ps, S_(0, L)), R("SEL", sel, S_(15 - m, 143 - m)), R(src, S_(L * m, L * m + L)), first and m == 4 * c0, False)
+                       for m in range(4 * c0, 4 * c1)])
+        return mm([(R(ps, S_(64 * c0, 64 * c1)), R("SEL", sel, S_(15 - m, 143 - m)), R(src, S_(1024 * c0 + m, 1024 * c1, 16)), first and m == 0, False)
                    for m in range(16)])
 
-    def ch(n, c):
-        return R(n, S_(1024 * c, 1024 * c + 1024))
+    ch = lambda n, c: R(n, S_(1024 * c, 1024 * c + 1024))
+    oc = lambda n, c: R(n, S_(64 * c, 64 * c + 64))
+    ONES, KID, OWN, TWO, NEG, NEG1 = range(6)
 
-    def oc(n, c):
-        return R(n, S_(64 * c, 64 * c + 64))
-
-    dma(R("KI"), R("kid")); dma(R("Z4"), R("zs"), "a"); dma(R("SN4"), R("sn")); dma(R("V", S_(0, T0)), R("vn"), "a")
+    dma(R("KI", 0), R("kid")); dma(R("Z"), R("zs")); dma(R("V", S_(0, T0)), R("vn")); dma(R("SN"), R("sn"))
     dma(R("BI"), R("bst"))
+    pc = lambda i: R("pc", S_(i, i + 1))
     iota(R("pI"), [[0, 16]], 0, 1)
-    iota(R("oI", 0), [[32, 16]], 0, 0); iota(R("oI", 1), [[1, 16]], 0, 0); iota(R("oI", 2), [[16, 16]], 15, 0)
-    iota(R("XI"), [[1, 144]], 0, 0)
-    iota(R("CG"), [[1, 8], [0, 16]], 0, 0)
+    iota(R("XI"), [[1, 148]], -4, 0)
+    iota(R("oI", 0), [[32, 16]], 0, 0); iota(R("oI", 1), [[1, 16]], 0, 0)
+    iota(R("CG"), [[16, 8], [0, 16]], 0, 0)
     iota(R("KX"), [[0, 16], [1, 16]], 0, 0)
     iota(RP("DI", S_(0, 32)), [[1, 120]], 0, 120)
-    ms(R("T2", S_(0, T0)), 0.0)
+    ts(R("oI", 2, S_(0, 1)), R("pI", S_(0, 1)), 112, ALU.bitwise_and)
+    ts(R("oI", 2, S_(1, 2)), R("pI", S_(0, 1)), 15, ALU.bitwise_and)
+    ts(R("oI", 2, S_(2, 3)), R("pI", S_(0, 1)), 12, ALU.bitwise_and, 2, ALU.arith_shift_right)
+    cp(R("pc", S_(0, 3)), R("oI", 2, S_(0, 3)))
+    ts(R("QN"), R("XI", S_(0, 128)), pc(0), ALU.subtract, pc(2), ALU.is_equal)
+    act(pc(4), pc(1), ACT.Identity, 0.0, 96.0)
+    ts(R("KI", 1), R("XI", S_(4, 100)), pc(4), ALU.add)
+    ts(R("KJ"), R("KI"), 63, ALU.bitwise_and); ts(R("KK"), R("KI"), 4032, ALU.bitwise_and)
+    ts(R("KL"), R("KJ"), -1.0 / DU, ALU.mult); ts(R("KH"), R("KK"), -1.0 / DU, ALU.mult)
+    for j, (n, b) in enumerate((("KL", 0), ("KH", 0), ("KL", 1), ("KH", 1))):
+        dma(RP("GR", S_(j, 32, 4), S_(0, T0)), R(n, b), "sa"[j % 2])
+    p32 = S_(0, 32)
+    iota(R("one"), [[0, L]], 1, 0)
+    asel(RP("MAP", p32), RP("one", p32, S_(0, 128)), [[-4, 8], [-1, 16]], ALU.is_equal, 0.0, 0, 1)
+    asel(RP("MAP", p32), RP("MAP", p32), [[0, 8], [-1, 16]], ALU.is_ge, 0.0, 3, 0)
+    for h, bank in enumerate(("p0", "p1", "p6")):
+        x = S_(512 * h, 512 * h + 512)
+        mm([(R(bank), R("QN"), R("V", x), True, False)])
+        mm([(R(bank), RP("MAP", p32), RP("GR", p32, x), False, False)])
+        if h < 2:
+            act(R("T2", x), R(bank), ACT.Identity, 0.0, -DU * EPS)
+        else:
+            ts(R("T2", x), R(bank), -DU * EPS, ALU.mult)
+    ts(pc(5), pc(1), 2.0, ALU.is_ge)
+    ts(R("SEL", ONES), R("XI", S_(0, 144)), pc(0), ALU.subtract, 11.0, ALU.is_equal)
+    asel(R("SEL", KID), R("SEL", ONES), [[1, 144]], ALU.is_ge, 0.0, -14, -1)
+    asel(R("SEL", OWN), R("SEL", ONES), [[-1, 144]], ALU.is_ge, 0.0, 13, 1)
+    for j, w in ((TWO, 2 * DU), (NEG, -DU), (NEG1, -1.0)):
+        if j != NEG1 or any(tune["bpos"]):
+            act(R("SEL", j), R("SEL", ONES), ACT.Identity, 0.0, w)
     ts(R("pJ"), R("pI"), 31, ALU.bitwise_and)
     tt(R("pJ"), R("pJ"), R("oI", 0), ALU.add)
-    cp(R("oT"), R("pJ")); cp(R("oB"), R("oI", 1)); cp(R("oE"), R("oI", 2))
-    ts(R("oI", 0, S_(0, 1)), R("pI", S_(0, 1)), 4, ALU.arith_shift_right)
-    ts(R("oI", 0, S_(1, 2)), R("pI", S_(0, 1)), 15, ALU.bitwise_and)
-    cp(R("pc", S_(0, 2)), R("oI", 0, S_(0, 2)))
-    cp(R("pc", S_(2, 3)), R("pI", S_(0, 1)))
-    ts(R("pc", S_(3, 4)), R("pc", S_(0, 1)), 16.0, ALU.mult, 15.0, ALU.add)
-    pc = lambda i: R("pc", S_(i, i + 1))
-    ts(R("SEL", 0), R("XI"), pc(3), ALU.is_equal)
-    if tune["pos1"]:
-        ts(R("SEL", 1), R("XI"), pc(3), ALU.is_equal, -8192.0, ALU.mult)
-    if tune["posb"] or tune["posc"]:
-        ts(R("SEL", 2), R("XI"), pc(3), ALU.is_equal, -1.0, ALU.mult)
+    cp(R("oT"), R("pJ")); cp(R("oB"), R("oI", 1))
     ts(R("BO"), R("CG"), pc(0), ALU.is_equal)
-    ms(R("cm32"), -1.0 / 32)
-    ts(R("ID4"), R("XI", S_(0, 128)), pc(2), ALU.is_equal)
-    iota(R("F", S_(0, W)), [[0, W]], 0, 0); ms(R("F", S_(W, W + 16)), 200.0)
-    ts(R("ID"), R("XI", S_(0, 128)), pc(2), ALU.is_equal)
-    ts(R("NID"), R("XI", S_(0, 128)), pc(2), ALU.is_equal, -1.0, ALU.mult)
-    ts(R("M16"), R("KX"), pc(1), ALU.is_equal)
-    ts(R("mg"), R("KX", S_(0, 16)), pc(1), ALU.is_equal, 1.0 if tune["mult"] else -128.0, ALU.mult)
-    for k in range(16):
-        act(R("EXP", k), R("BO"), ACT.Identity, 0.0, R("mg", S_(k, k + 1)))
-    ms(R("hz", 0), 0.5); ms(R("hz", 1), 0.0)
-    scan(R("pw"), R("hz", 0), R("hz", 1), 65536.0, ALU.mult, ALU.add)
-    tt(R("pw"), R("pw"), R("M16", S_(0, 16)), ALU.mult)
-    add("v", "red", (pc(4), R("pw")), [R("pw")], [pc(4)])
-    ts(pc(5), pc(4), 2.0, ALU.mult, 1.0, ALU.add)
-    ts(R("DW"), R("BO"), pc(4), ALU.mult)
-    ts(R("BOW"), R("BO"), 65536.0, ALU.mult)
-    ts(R("thr"), R("M16"), pc(5), ALU.mult, -1.0, ALU.add)
-    ts(R("seg"), R("KX"), 0.0, ALU.is_gt)
-    ts(R("big"), R("KX"), 0.0, ALU.is_equal, 2.0 ** 25, ALU.mult)
-    cx, ck = R("p7", S_(0, L)), R("p7", S_(L, 2 * L))
-    ts(R("dum"), R("XI", S_(0, 16)), 16.0, ALU.mult, pc(1), ALU.add)
-    iota(R("V", S_(T0, W + 16)), [[0, W + 16 - T0]], 0, 0)
-    ts(R("KJ"), R("KI"), 63, ALU.bitwise_and); ts(R("KK"), R("KI"), 4032, ALU.bitwise_and)
-    ts(R("KL"), R("KJ"), EPS, ALU.mult); ts(R("KH"), R("KK"), EPS, ALU.mult)
-    dma(RP("T2", S_(0, 128, 16), S_(0, T0)), R("KL")); dma(RP("T2", S_(1, 128, 16), S_(0, T0)), R("KH"), "a")
-    p32 = S_(0, 32)
+    iota(R("FL", S_(0, 16)), [[0, 16]], 0, 0); iota(R("FM", S_(0, 16)), [[0, 16]], 0, 0)
+    act(R("cm32"), R("one"), ACT.Identity, 0.0, -1.0 / 32)
+    asel(R("ID"), R("one", S_(0, 128)), [[-1, 128]], ALU.is_equal, 0.0, 0, 1)
+    for n, w in (("ID4", 1.0), ("NID", -1.0), ("IDB", BIG), ("NIDB", -BIG), ("IDH", DU / 2), ("IDT", TIE)):
+        act(R(n), R("ID"), ACT.Identity, 0.0, w)
+    asel(R("DW"), R("BO"), [[1, 128]], ALU.is_gt, 0.0, 0, -1)
+    ts(R("thr"), R("KX"), pc(1), ALU.is_equal, 4096.0, ALU.mult)
+    K16 = [[0, 16], [1, 16]]
+    asel(R("seg"), R("one"), K16, ALU.is_gt, 0.0, 0, 0)
+    act(R("big"), R("seg"), ACT.Identity, 2 * BIG, -2 * BIG)
+    act(R("stp"), R("seg"), ACT.Identity, 4 * BIG, -4 * BIG - DU)
+    act(R("dumW"), R("XI", S_(4, 20)), ACT.Identity, pc(1), 16.0)
+    act(R("dumW"), R("dumW"), ACT.Identity, float(W))
+    ms(R("ZS"), 0.0)
+    for gq in range(8):
+        dma(RP("F", S_(16 * gq + 2, 16 * gq + 16), S_(0, W)), RP("ZS", S_(0, 112)))
+    ms(R("F", S_(NONE, NONE + 1)), 200.0)
+    iota(R("F", S_(W, W + 16)), [[0, 16]], 200, 0)
     h0, h1 = S_(0, 120), S_(120, 240)
     ts(RP("DJ", p32, h0), RP("DI", p32), 63, ALU.bitwise_and); ts(RP("DJ", p32, h1), RP("DI", p32), 4032, ALU.bitwise_and)
     ts(RP("DL", p32), RP("DJ", p32), EPS, ALU.mult)
@@ -236,290 +260,301 @@ def build_ops(tune):
         dma(RP("F", S_(16 * gq, 16 * gq + 2), S_(0, W)), RP("F", S_(0, 2), S_(0, W)))
     dma(R("T2", S_(T0, W)), R("F", S_(T0, W)))
 
-    def to_lanes(tau):
-        for b in range(2):
-            cp(R("X2", ALL, b, ALL), R("SN4", ALL, ALL, tau))
-        tr(R("XT"), R("X2"))
-        cp(R("S%d" % tau), IND(R("XT"), R("oT")))
-        cp(R("P%d" % tau), IND(R("XT"), R("oT")))
-
     def ys_rows(tau):
         ts(R("Yt"), R("ids", S_(128, 256)), 4096.0, ALU.mult)
         tt(R("Yc"), R("Yt"), R("ids", S_(0, 128)), ALU.add)
         for b in range(2):
-            cp(R("X2", S_(0, 8), b, ALL), R("Yc"), "a")
-        tr(R("XT", S_(0, 256)), R("X2", S_(0, 8)))
-        cp(R("YS", S_(tau, 512, 4)), IND(R("XT", S_(0, 256)), R("oT", S_(0, 8))))
+            cp(R("X2", ALL, b, ALL), R("Yc"), "g")
+        tr(R("XT"), R("X2"))
+        cp(R("YS", S_(tau, 512, 4)), IND(R("XT"), R("oT", S_(0, 8))), "a")
 
     def yb_rows(tau):
-        ts(R("Y1"), R("apf"), float(NONE), ALU.is_equal, -float(NONE + 1), ALU.mult)
+        act(R("Y1"), R("dd"), ACT.Identity, 0.0, -2.0)
+        tt(R("Y1"), R("Y1"), R("apf"), ALU.add)
         for b in range(2):
-            tt(R("YB", b), R("Y1"), R("apf"), ALU.add)
+            ts(R("YB", b), R("Y1"), -1.0, ALU.max)
         tr(R("YBT"), R("YB"))
-        cp(R("B64", S_(tau, 64, 4)), IND(R("YBT"), R("oT", S_(0, 1))))
+        cp(R("B64", S_(tau, 64, 4)), IND(R("YBT"), R("oT", S_(0, 1))), "a")
 
-    def zrep(tau):
+    def zrep(t):
+        if t < 3:
+            act(R("Zp"), IND(R("Z"), R("oP%d" % t)), ACT.Copy)
+            mm([(R("p3", S_(L, L + 16)), R("SEL", NEG, S_(15 - m, 143 - m)), R("Zp", S_(16 * m, 16 * m + 16)), m == 0, False) for m in range(16)])
+            cp(R("nz%d" % t), R("p3", S_(L, L + 16)), "a")
         for k in range(16):
-            o, a = R("ZT", ALL, k, ALL), R("Z4", ALL, ALL, tau)
-            if tau:
-                add("g", "asel", (o, a, [[0, 16], [0, 16]]), [a], [o])
+            nv, na = tune["z0"] if t == 0 else (0, 0)
+            if t < 3:
+                cp(R("zr%d" % t, S_(k, 4096, 16)), R("Zp"), "v" if k < nv else "a" if k < nv + na else "g")
             else:
-                cp(o, a, "v" if k < tune["nz"] else "a")
-        n = 2 if tau else 4
-        for c in range(n):
-            dma(R("zr%d" % tau, S_(4096 // n * c, 4096 // n * (c + 1))), R("ZT", S_(16 // n * c, 16 // n * (c + 1))))
+                cp(R("ZT", ALL, k, ALL), R("Z4", ALL, ALL, TILE[t]), "g")
+        if t >= 3:
+            dma(R("zr%d" % (t - 3)), R("ZT"))
 
-    def diff(raw, dif, out, win, off, rep, c, nact, scale, ps=None, last=False, pos=None, sign=False):
+    def diff(raw, dif, out, win, off, rep, c, nact, scale, ps, mid=False, pos=None, first=False):
         na = min(2, max(0, nact - 2 * c))
-        b0, mid, b1 = 1024 * c, 1024 * c + 512 * na, 1024 * c + 1024
-        o = None
+        b0, md, b1 = 1024 * c, 1024 * c + 512 * na, 1024 * c + 1024
         if na:
-            act(R(raw, S_(b0, mid)), IND(win, R(off, S_(b0 // 16, mid // 16))), ACT.Copy)
+            act(R(raw, S_(b0, md)), IND(win, R(off, S_(b0 // 16, md // 16))), ACT.Copy)
         for h in range(na):
             x = S_(b0 + 512 * h, b0 + 512 * h + 512)
             mm([(R("p%d" % h), R("ID"), R(raw, x), True, False), (R("p%d" % h), R("NID"), R(rep, x), False, True)])
             act(R(out, x), R("p%d" % h), ACT.Abs, 0.0, scale)
-            if sign:
-                act(R(raw, x), R("p%d" % h), ACT.Sign)
         if na < 2:
-            x = S_(mid, b1)
-            o = tt(R(dif, x), IND(win, R(off, S_(mid // 16, b1 // 16))), R(rep, x), ALU.subtract)
+            x = S_(md, b1)
+            tt(R(dif, x), IND(win, R(off, S_(md // 16, b1 // 16))), R(rep, x), ALU.subtract)
             if pos and not na:
-                dpass(ps, dif, c, neg=1 if scale > 1 else 2)
+                dpass(ps, dif, c, c + 1, NEG if scale > 1 else NEG1, first, mid)
                 ts(R(pos, x), R(dif, x), 0.0, ALU.max, 2.0 * scale, ALU.mult)
-                dpass(ps, pos, c, last=last)
-                return o
+                return dpass(ps, pos, c, c + 1, ONES, False, mid)
             act(R(out, x), R(dif, x), ACT.Abs, 0.0, scale)
-        if ps:
-            dpass(ps, out, c, last=last)
-        return o
+        return dpass(ps, out, c, c + 1, ONES, first, mid)
 
     parts = tune["parts"]
-    pbank = lambda c: "p2" if c < parts[0][1] else "p3"
-    ebank = "p3" if len(parts) == 1 else "p5"
+    pbank = lambda c: "p2" if c < parts[0][1] else "p6"
+    starts = [c0 for c0, c1 in parts]
 
-    def zdiff(c):
-        nz, mult = tune["zact"], tune["mult"]
-        diff("DC", "DC", "AC", R("Z"), "q16", "vr", c, nz, 1.0, "p4", False, "AC" if c >= 4 - tune["posc"] else None, mult)
-        if mult and 2 * c + 2 > nz:
-            x = R("DC", S_(max(1024 * c, 512 * nz), 1024 * c + 1024))
-            if c >= 4 - tune["nclip"]:
-                ts(x, x, -1.0, ALU.max, 1.0, ALU.min)
-            else:
-                act(x, x, ACT.Sign)
+    whole = {}
 
-    def first_dist(tau, nact):
+    def first_dist(t):
+        cp(R("S%d" % t), IND(R("SN"), R("oP%d" % t)))
+        act(R("Pp"), IND(R("nz%d" % t), R("oB")), ACT.Identity, BIG)
+        mm([(R("p5", S_(0, L)), R("NIDB"), R("one"), True, False)])
         for c in range(4):
-            diff("GR", "DS", "DS", R("V", S_(0, T0)), "S%d" % tau, "zr%d" % tau, c, nact, 8192.0)
-        dpass("p5", "DS", 0, True, True, 4096)
-        tt(R("P%d" % tau), R("p5", S_(0, L)), R("P%d" % tau), ALU.add)
+            tt(ch("DS", c), IND(R("V", S_(0, T0)), oc("S%d" % t, c)), ch("zr%d" % t, c), ALU.max)
+            whole[c] = dpass("p5", "DS", c, c + 1, TWO, False, True)["id"]
 
     def children(t):
         win = R("T2", S_(0, T0 if t < 3 else W))
-        for (c0, c1) in parts:
-            for c in range(c0, c1):
+        for c in range(4):
+            if c in tune["g2v"][t]:
+                ts(ch("G2", c), IND(win, oc("S%d" % TILE[t], c)), 1.0 / EPS, ALU.mult)
+            else:
                 act(ch("G2", c), IND(win, oc("S%d" % TILE[t], c)), ACT.Identity, 0.0, 1.0 / EPS)
-                dpass(ebank, "G2", c, True, True)
-                cp(oc("e16", c), oc(ebank, c))
-                act(oc("E4", c), oc(ebank, c), ACT.Identity, 4096.0)
-                mm([(oc(pbank(c), c), R("ID4"), oc("E4", c), c == c0, False)])
+            dpass("p7", "G2", c, c + 1, KID, True)
+            cp(oc("e16", c), oc("p7", c))
+            if t < 3:
+                dpass("p5", "G2", c, c + 1, OWN, False, True)["after"] = whole[c]
+            elif tune["e4"]:
+                act(oc("E4", c), oc("p7", c), ACT.Identity, TIE)
+        if t < 3:
+            tt(R("Ps"), R("p5", S_(0, L)), R("Pp"), ALU.add)
 
-    to_lanes(0)
+    act(pc(6), pc(1), ACT.Identity, 0.0, 64.0)
+    act(R("t1"), R("XI", S_(4, 20)), ACT.Identity, pc(6), 4.0)
+    for t in range(3):
+        ts(R("oP%d" % t), R("t1"), float(t), ALU.add)
     zrep(0)
     late = len(ops) - 1
-    dma(R("Z"), R("zs"))["after"] = late
+    dma(R("Z4"), R("zs"))["after"] = late
     dma(R("Q", S_(0, T0)), R("nq"))["after"] = late
+    dma(R("V", S_(T0, GB)), R("V", S_(0, GB - T0)))["after"] = late
+    dma(R("Q", S_(T0, GB)), R("Q", S_(0, GB - T0)))
+    first_dist(0)
     children(0)
-    first_dist(0, tune["ds0"])
     cp(R("B64"), R("BI"))
     ts(R("Bt"), R("B64"), 0.0, ALU.is_lt, float(NONE + 1), ALU.mult)
     tt(R("Bo"), R("Bt"), R("B64"), ALU.add)
     for b in range(2):
-        cp(R("XB", ALL, b, ALL), R("Bo"))
+        cp(R("XB", ALL, b, ALL), R("Bo"), "a")
     tr(R("XBT"), R("XB"))
     for h in range(4):
         cp(R("B16", S_(h, 64, 4)), IND(R("XBT", S_(32 * h, 32 * h + 32)), R("oT", S_(0, 1))))
-    act(R("VBt"), IND(R("V"), R("B16")), ACT.Copy)
-    for h in range(2):
-        tt(R("VB", S_(512 * h, 512 * h + 512)), IND(R("F"), R("B16", S_(32 * h, 32 * h + 32))), R("VBt", S_(512 * h, 512 * h + 512)), ALU.add)
+    act(R("VBt"), IND(R("V", S_(0, GB)), R("B16")), ACT.Copy)
+    tt(R("VB"), IND(R("F"), R("B16")), R("VBt"), ALU.add)
+    ts(R("mg"), R("KX", S_(0, 16)), pc(1), ALU.is_equal, -128.0, ALU.mult)
+    for k in range(16):
+        act(R("EXP", k), R("BO"), ACT.Identity, 0.0, R("mg", S_(k, k + 1)))
     zrep(1)
-    iota(R("Q", S_(T0, W)), [[0, W - T0]], 0, 0)
-    zrep(2)
-    ts(R("Yc"), R("SN4", S_(8, 16), ALL, 3), 4096.0, ALU.mult)
-    tt(R("YS", S_(3, 512, 4)), R("Yc"), R("SN4", S_(0, 8), ALL, 3), ALU.add)
-    to_lanes(1)
+    ts(R("Yt"), R("SN", S_(515, 1024, 4)), 4096.0, ALU.mult)
+    tt(R("YS", S_(3, 512, 4)), R("Yt"), R("SN", S_(3, 512, 4)), ALU.add)
 
     ends = lambda n: R(n, S_(15, L, 16))
     for t in range(RO):
         tau = TILE[t]
         n0 = T0 + L * t
+        top = T0 if t == 0 else GB + L * t
         ewin = R("V", S_(0, T0 if t == 0 else GB + L * (t - 1)))
-        vwin = R("V", S_(0, T0 if t == 0 else GB + L * t))
-        D1, D2, AR, WW = R("p3", S_(0, L)), R("p4", S_(0, L)), R("p2", S_(0, L)), R("p5", S_(0, L))
-        nz, mult = tune["zact"], tune["mult"]
-        act(ck, R("KX"), ACT.Identity, 0.0, 512.0)
+        D1, D2, WW, H = R("p3", S_(0, L)), R("p4", S_(0, L)), R("p5", S_(0, L)), R("p6", S_(L, 2 * L))
+        nz = tune["zact"][t]
+        old = "Ps" if t < 3 else "K%d" % tau
         if t > 0:
-            act(cx, R("KX"), ACT.Identity, 8192.0, -512.0)
-        for c in range(4):
-            diff("GR", "DA", "DA", ewin, "e16", "zr%d" % tau, c, (tune["actpath"] if t else tune["act0"]) + (4 * c - 6 if len(parts) > 1 else 0), 8192.0,
-                 pbank(c), c == 3, "GR" if c < tune["pos1"] else None)
-        if t > 0:
-            mm([(R("p4", S_(0, L)), R("ID"), R("LV", t - 1), True, False), (R("p4", S_(0, L)), R("NID"), R("Z", S_(tau, 1024, 4)), False, True)])
-            act(R("dg"), R("p4", S_(0, L)), ACT.Abs, 0.0, 8192.0)
-            dpass("p5", "dg", 0, True, True, 256)
-            act(R("mg"), R("dum"), ACT.Identity, float(GB + L * (t - 1)))
-            act(R("thm"), R("p5", S_(0, 16)), ACT.Identity, 8192.0)
+            gv = R("V", S_(GB + L * (t - 1), GB + L * t))
+            mm([(R("p4", S_(0, L)), R("ID"), gv, True, False), (R("p4", S_(0, L)), R("NID"), R("Z", S_(tau, 1024, 4)), False, True)])
+            act(R("dg"), R("p4", S_(0, L)), ACT.Abs, 0.0, DU)
+            mm([(R("p5", S_(0, 16)), R("SEL", ONES, S_(15 - m, 143 - m)), R("dg", ALL, m), m == 0, False) for m in range(16)])
+            act(R("mg"), R("dumW"), ACT.Identity, GB + L * (t - 1) - W + TIE)
+            act(R("sgn", S_(L, L + 16)), R("p5", S_(0, 16)), ACT.Sign, 0.5 - KILL * DU)
             tt(R("Pm"), R("p5", S_(0, 16)), R("mg"), ALU.add)
-            act(R("fl"), IND(R("Pm"), R("oB")), ACT.Copy)
-            act(R("p5", S_(L, 2 * L)), R("fl"), ACT.Copy)
-            cp(R("V", S_(GB + L * (t - 1), GB + L * t)), R("LV", t - 1), "a")
-        mm([(D2, R("BO"), R("cm32"), True, False)])
-        Pn = "Pj" if t else "Pi"
-        x0, x1 = R("p6", S_(0, L)), R("p6", S_(L, 2 * L))
+            act(R("Pmb"), IND(R("Pm"), R("oB")), ACT.Identity, TIE)
+        for c in range(4):
+            if t >= 3 and tune["e4"]:
+                mm([(oc("p2", c), R("ID4"), oc("E4", c), c == 0, False)])
+            else:
+                if c == 0:
+                    mm([(R("p2", S_(0, L)), R("IDT"), R("one"), True, False)])
+                dpass(pbank(c), "G2", c, c + 1, KID, False, t < 3)
+            diff("GR", "DA", "DA", ewin, "e16", "zr%d" % (t % 3), c, tune["eact"][t], DU, pbank(c), t < 3, "GR" if c >= 4 - tune["epos"][t] else None)
+        Pn = "P2" if t else "P1"
         for (c0, c1) in parts:
             u0, u1, w0, w1 = 64 * c0, 64 * c1, 4 * c0, 4 * c1
             A = lambda n, at=0: R(n, S_(at + u0, at + u1))
             Bn = lambda n: R(n, S_(w0, w1))
             en = lambda n: R(n, S_(u0 + 15, u1, 16))
-            of = lambda n: R(n, S_(0, w1 - w0))
-            o = tt(A("Pi"), A(pbank(c0)), A("P%d" % tau), ALU.min)
-            if c0:
-                o["after"] = ahead
-            if t > 0:
-                ts(A("dP"), A("Pi"), -8192, ALU.bitwise_and)
-                tt(A("kx"), A("dP"), A("p7"), ALU.add)
-                scan(A("sc1"), A("seg"), A("kx"), 0.0, ALU.mult, ALU.max)
-                tt(A("p6", L), A("p5", L), A("Pi"), ALU.subtract)
-                tt(Bn("cd"), Bn("thm"), en("sc1"), ALU.is_lt)
-                tt(Bn("tg"), Bn("cd"), en("sc1"), ALU.mult)
-                tt(A("tB"), IND(Bn("tg"), of("oB")), A("kx"), ALU.is_equal)
-                tt(A("p6"), A("p6", L), A("tB"), ALU.mult)
-                tt(A("Pj"), A("p6"), A("Pi"), ALU.add)
-            ts(A("dP"), A(Pn), -8192, ALU.bitwise_and)
-            tt(A("kx"), A("dP"), A("p7", L), ALU.add)
-            scan(A("sc2"), A("big"), A("kx"), 0.0, ALU.add, ALU.min)
-            ts(A("ids"), A(Pn), 4095, ALU.bitwise_and)
-            tt(A("tB"), IND(A("sc2"), of("oE")), A("kx"), ALU.is_equal)
-            scan(A("sc1"), A("seg"), A("kx"), 0.0, ALU.mult, ALU.max)
-            tt(A("p6"), A("tB"), A("ids"), ALU.mult)
-            scan(A("sc3"), A("seg"), A("p6"), 0.0, ALU.mult, ALU.add)
-            cp(Bn("a16"), en("sc3"))
-            cp(A("va"), IND(vwin, Bn("a16")), "a")
-            ahead = cp(A("q16"), IND(R("Q", S_(0, T0 if t == 0 else W)), Bn("a16")))["id"]
+            wide = lambda n: IND(R(n), R("oB", S_(w0, w1)))
+            pb, yb = pbank(c0), "p4" if c0 else "p5"
+            tt(A("P1"), A(pb), A(old), ALU.min)
+            mm([(A(pb), R("ID4"), A("P1"), True, False)])
+            scan(A("sc2"), A("big"), A("P1"), 0.0, ALU.add, ALU.min)
+            ts(Bn("th3"), en("sc2"), RND, ALU.add, DU - RND, ALU.add)
+            if t == 0:
+                tt(A("nf"), wide("th3"), A("P1"), ALU.is_le)
+                mm([(A(pb), R("IDB"), A("nf"), False, False)])
+                scan(A("sc3"), A("stp"), A(pb), 0.0, ALU.add, ALU.min)
+                cp(Bn("Ri"), en("sc3"))
+            else:
+                tt(A("FM", 16), wide("th3"), A("P1"), ALU.is_gt)
+                scan(A("nf"), A("FM", 15), A("seg"), 0.0, ALU.max, ALU.mult)
+                mm([(A(yb, L), R("ID4"), A("Pmb"), True, False)])
+                scan(A("sc1"), A("seg"), A("P1"), 0.0, ALU.mult, ALU.max)
+                ts(Bn("th1"), en("sc1"), RND, ALU.add, -RND, ALU.add)
+                tt(A("FL", 16), wide("th1"), A("P1"), ALU.is_le)
+                scan(A("cx"), A("FL", 15), A("seg"), 0.0, ALU.max, ALU.mult)
+                mm([(A(pb), R("NIDB"), A("FM", 16), False, False), (A(pb), R("IDB"), A("one"), False, False)])["seq"] = 1
+                mm([(A(pb), R("IDB"), A("nf"), False, False)])
+                mm([(A(pb), R("IDH"), A("cx"), False, False)])
+                mm([(A(yb, L), R("NIDB"), A("FL", 16), False, False), (A(yb, L), R("IDB"), A("cx"), False, False),
+                    (A(yb, L), R("IDB"), A("one"), False, False)])
+                tt(A("Pi"), A(yb, L), A("P1"), ALU.min)
+                act(A("sgn"), A("P1"), ACT.Sign, 0.5 - KILL * DU)
+                scan(A("sc3"), A("big"), A(pb), 0.0, ALU.add, ALU.min)
+                tt(Bn("Ri"), en("sc3"), Bn("Pm"), ALU.min)
+            ts(Bn("ai"), Bn("Ri"), 4095, ALU.bitwise_and)
+            cp(Bn("a16"), Bn("ai"))
+            if t == 0:
+                scan(A("sc1"), A("seg"), A("P1"), 0.0, ALU.mult, ALU.max)
+            cp(A("va"), IND(R("V", S_(0, top)), Bn("a16")), "a")
+            cp(A("q16"), IND(R("Q", S_(0, top)), Bn("a16")))
+            act(A("nFa"), IND(R("F"), Bn("a16")), ACT.Identity, 0.0, -1.0)
+            mm([(A(pb, L), R("BO"), A("nFa"), True, True)])
+            ts(A("ar16"), A(pb, L), -1.0 / EPS, ALU.mult)
+            nv = 16 - tune["ng"] - tune["na"]
             for k in range(16):
-                o, a = R("vr", S_(16 * u0 + k, 16 * u1, 16)), A("va")
-                nv, ng = (tune["nv_copy"], tune["ng"]) if c1 == 4 else (tune["nv_first"], tune["ng_first"])
-                if k >= 16 - ng:
-                    add("g", "asel", (o, a, [[0, u1 - u0]]), [a], [o])
-                else:
-                    cp(o, a, "v" if k < nv else "a")
-            if c1 < 4:
-                for c in range(c0, c1):
-                    zdiff(c)
-        ts(R("lv"), ends("sc1"), 8192.0 * KILL, ALU.is_ge)
-        ts(R("t1"), ends("sc3"), -float(NONE), ALU.add)
-        tt(R("t2"), R("t1"), R("lv"), ALU.mult)
-        ts(R("ap16"), R("t2"), float(NONE), ALU.add)
-        act(R("apf"), R("t2"), ACT.Identity, float(NONE))
-        tt(R("t3"), R("t1"), R("dum"), ALU.subtract)
-        tt(R("aD"), R("t3"), R("lv"), ALU.mult)
-        act(R("nFa"), IND(R("F"), R("a16")), ACT.Identity, 0.0, -1.0)
+                cp(R("vr", S_(16 * u0 + k, 16 * u1, 16)), A("va"), "v" if k < nv else "a" if k < nv + tune["na"] else "g")
+        if t > 0:
+            far = R("p3", S_(L, L + 16))
+            mm([(far, R("ID"), R("sgn", S_(L, L + 16)), True, False)] + [(far, R("ID"), R("sgn", S_(k, L, 16)), False, False) for k in range(16)])
+            ts(R("dd"), far, -14.0, ALU.is_lt, 4096.0, ALU.mult)
+        else:
+            ts(R("dd"), ends("sc1"), DU * KILL, ALU.is_lt, 4096.0, ALU.mult)
+        tt(R("apf"), R("ai"), R("dd"), ALU.add)
+        ts(R("ap16"), R("apf"), float(W), ALU.min)
         tt(R("VB", S_(tau, 1024, 4)), IND(R("F"), R("ap16")), R("va"), ALU.add)
-        mm([(AR, R("BO"), R("nFa"), True, True)])
-        mm([(D1, R("BO"), R("nFa"), True, False)])
         if t < RO - 1:
             cp(R("Q", S_(n0, n0 + L)), R("q16"))
-            add("g", "send", (R("LQ", t), R("Q", S_(n0, n0 + L)), "aq%d" % t, HOPS[t]), [R("Q", S_(n0, n0 + L))], [])
-            add(None, "recv", "aq%d" % t, [], [R("LQ", t)], after=len(ops) - 1)
-            dma(R("Q", S_(GB + L * t, GB + L * t + L)), R("LQ", t))
-        ts(R("ar16"), AR, -1.0 / EPS, ALU.mult)
+            send("Q", t, n0, "aq%d" % t)
+        if t < 2:
+            act(R("tk"), IND(R("T2", S_(0, top)), R("a16")), ACT.Identity, 0.0, pc(5))
+        if t < 3:
+            zrep(t + 2)
         for h in range(16):
             ts(R("E", h, S_(0, L - 16 * h)), R("ar16", S_(16 * h, L)), R("apf", S_(h, h + 1)), ALU.is_equal)
+        last_e = len(ops) - 1
         mm([(WW, R("DW"), R("E", ALL, S_(0, 16)), True, False)] +
-           [(R("p5", S_(16 * h + 16, L)), R("BOW"), R("E", h, S_(16, L - 16 * h)), False, h == 14) for h in range(15)])
-        tt(R("fl"), WW, R("thr"), ALU.is_lt)
-        scan(R("sc4"), R("seg"), R("fl"), 0.0, ALU.mult, ALU.add)
-        tt(R("t3"), ends("sc4"), R("aD"), ALU.mult)
-        tt(R("t3"), R("t3"), R("dum"), ALU.add)
-        ts(R("o16"), R("t3"), float(W), ALU.add)
-        sca = cp(IND(R("T2"), R("o16")), R("F", S_(n0, n0 + L)))
-        for c in range(4):
-            o = diff(None, "DB", "DB", R("VB"), "q16", "vr", c, 0, 1.0, "p3", c == 3, "DA" if c >= 4 - tune["posb"] else None)
-            if c == tune["early"] and t < RO - 1:
-                o["after"] = sca["id"]
-        act(R("A1"), D1, ACT.Abs)
-        act(R("wx", 0), D1, ACT.Relu, -8800.0, 8.0)
-        act(R("wx", 1), R("A1"), ACT.Relu, 2048.0, -2.0 ** 26)
-        for c in range(parts[-1][0], 4):
-            zdiff(c)
-        mm([(D2, R("ID"), R("wx", 0), False, False), (D2, R("NID"), R("wx", 1), False, True)])
-        act(R("lo"), R("va"), ACT.Relu, -2.0)
-        act(R("hi"), R("va"), ACT.Relu, 61.0, -1.0)
-        act(R("hi"), R("hi"), ACT.Identity, 63.0, -1.0)
-        H = x1
-        banks = ["p2", "p3", "p7", "p5", "p0", "p1", "p4", "p7"]
-
-        def pre(b):
-            lst = []
-            for j in range(2):
-                k = 2 * b + j
-                lst.append((R(banks[b], S_(L * j, L * j + L)), R("ID"), R("DC", S_(k, 4096, 16)), j == 0, False))
-                if nz:
-                    lst.append((R(banks[b], S_(L * j, L * j + 32 * nz)), R("NID"), R("va", S_(0, 32 * nz)), False, False))
-            mm(lst)
-
-        for b in range(0 if mult else 6):
-            pre(b)
-        o = tt(R("att"), D2, R("A1"), ALU.is_lt if mult else ALU.is_ge)
-        if tune["early"] == 8 and t < RO - 1:
-            o["after"] = sca["id"]
-        mm([(H, R("ID"), R("va"), True, False)])
-        if mult:
-            if t < RO - 1:
-                children(t + 1)
-            for b in range(8):
-                pb = ["p0", "p1", "p5", "p7"][b % 4]
-                mm([(R(pb, S_(L * j, L * j + L)), R("EXP", 2 * b + j), R("att"), j == 0, j == 1) for j in range(2)])
-                for j in range(2):
-                    tt(R("U", b, S_(L * j, L * j + L)), R("DC", S_(2 * b + j, 4096, 16)), R(pb, S_(L * j, L * j + L)), ALU.mult)
-                mm([(H, R("ID"), R("U", b, S_(L * j, L * j + L)), False, False) for j in range(2)])
+           [(R("p5", S_(16 * h + 16, L)), R("BO"), R("E", h, S_(16, L - 16 * h)), False, False) for h in range(15)])
+        tt(R("fl"), WW, R("thr"), ALU.mult)
+        if tune["lowv"][t]:
+            scan(R("cnt"), R("seg"), R("fl"), 0.0, ALU.mult, ALU.max)
+            tt(R("t2"), ends("cnt"), R("apf"), ALU.max)
+            tt(R("t1"), R("t2"), R("dumW"), ALU.min)
         else:
-            pre(6)
-        for b in range(0 if mult else 8):
-            pb = banks[b]
-            mm([(R(pb, S_(L * j, L * j + L)), R("EXP", 2 * b + j), R("att"), False, j == 1) for j in range(2)])
-            if b in tune["sact"] or (t == RO - 1 and b % 2):
-                act(R("U", b), R(pb), ACT.Sign)
-            else:
-                ts(R("U", b), R(pb), -1.0, ALU.max, 1.0, ALU.min)
-            if b == 2:
-                pre(7)
-            if b == (1 if len(parts) == 1 else 3) and t < RO - 1:
-                children(t + 1)
-            if b == 0:
-                mm([(H, R("BO"), R("att"), False, False)])
-            mm([(H, R("ID"), R("U", b, S_(L * j, L * j + L)), False, b == 7 and j == 1) for j in range(2)])
-        tt(x0, H, R("lo"), ALU.max)
-        tt(R("V", S_(n0, n0 + L)), x0, R("hi"), ALU.min)
-        if t < RO - 1:
-            add("g", "send", (R("LV", t), R("V", S_(n0, n0 + L)), "av%d" % t, HOPS[t]), [R("V", S_(n0, n0 + L))], [])
-            add(None, "recv", "av%d" % t, [], [R("LV", t)], after=len(ops) - 1)
-        dma(R("yv", S_(L * t, L * t + L)), R("V", S_(n0, n0 + L)))
+            low = R("p5", S_(L, L + 16))
+            mm([(low, R("ID4"), R("apf"), True, False)] + [(low, R("ID"), R("fl", S_(m, L, 16)), False, False) for m in range(16)])
+            tt(R("t1"), low, R("dumW"), ALU.min)
+        cp(R("o16"), R("t1"))
+        if t < 2:
+            tt(IND(R("T2"), R("o16")), R("tk"), R("F", S_(n0, n0 + L)), ALU.add)
+        else:
+            cp(IND(R("T2"), R("o16")), R("F", S_(n0, n0 + L)))
+        scat = len(ops) - 1
+        if t == 0:
+            cp(R("Pi"), R("P1"))
+        ts(R("ids"), R("Pi"), 4095, ALU.bitwise_and)
         if tau in TILE[t + 1:]:
             cp(R("S%d" % tau), R("ids"))
-            ts(R("P%d" % tau), R(Pn), -4097, ALU.bitwise_and)
+            ts(R("K%d" % tau), R("Pi"), -12289, ALU.bitwise_and)
         else:
             ys_rows(tau)
             yb_rows(tau)
-        if t == 0:
-            first_dist(1, tune["dsact"])
-            to_lanes(2)
-        if t == 1:
-            first_dist(2, tune["dsact"])
+        if t < 2:
+            first_dist(t + 1)
+        for hf in range(2):
+            banks = ("p0", "p1", "p2", "p3" if hf else "p7")
+            if hf and t < RO - 1:
+                children(t + 1)
+            h = lambda n, *ix: R(n, *ix, S_(128 * hf, 128 * hf + 128))
+            q4 = lambda n, j: R(n, S_(128 * j, 128 * j + 128))
+            dk = lambda k: R("DC", S_(2048 * hf + k, 2048 * hf + 2048, 16))
+            sub = lambda b: [x for j in range(4) for x in [(q4(banks[b], j), R("ID"), dk(4 * b + j), j == 0, False)] +
+                             [(q4(banks[b], j), R("NID"), h("va"), False, False)] * (1 - hf)]
+            mm([(h("p4"), R("BO"), h("cm32"), True, False)])
+            mm([(h("p3"), R("BO"), h("nFa"), True, False)])
+            for c in (2 * hf, 2 * hf + 1):
+                o = len(ops)
+                diff(None, "DB", "DB", R("VB"), "q16", "vr", c, 0, 1.0, "p3", False, "DA" if c >= 4 - tune["bpos"][t] else None)
+                if t < RO - 1 and c == tune["hold"][0]:
+                    ops[o]["after"] = last_e
+                if t < RO - 1 and c == tune["hold"][1]:
+                    ops[o]["after"] = scat
+                if hf:
+                    diff(None, "DC", "GR", R("Z"), "q16", "vr", c, 0, 1.0, "p4")
+                else:
+                    act(ch("DC", c), IND(R("Z"), oc("q16", c)), ACT.Copy)
+            for b in range(4):
+                if not hf or b < 3:
+                    mm(sub(b))
+                if not hf:
+                    act(R("AC", S_(4 * b, 4 * b + 4)), R(banks[b]), ACT.Abs)
+                    mm([(h("p4"), R("SEL", ONES, S_(15 - k, 143 - k)), R("AC", k), False, False) for k in range(4 * b, 4 * b + 4)])
+                    if not tune["keep"]:
+                        mm(sub(b))
+            act(h("A1"), h("p3"), ACT.Abs)
+            act(h("wx", 0), h("p3"), ACT.Relu, -8800.0, 8.0)
+            if hf:
+                mm(sub(3))
+            if tune["eqv"]:
+                ts(h("wx", 1), h("A1"), 0.0, ALU.is_equal, 2048.0, ALU.mult)
+            else:
+                act(h("wx", 1), h("A1"), ACT.Relu, 2048.0, -2.0 ** 26)
+            mm([(h("p4"), R("ID"), h("wx", 0), False, False), (h("p4"), R("NID"), h("wx", 1), False, False)])
+            tt(h("att"), h("p4"), h("A1"), ALU.is_ge)
+            H, X = q4("p6", 2 + hf), q4("p6", hf)
+            if tune["lohi"]:
+                mm([(H, R("ID"), h("va"), True, False)])
+            mm([(H, R("BO"), h("att"), not tune["lohi"], False)])
+            for b in range(4):
+                mm([(q4(banks[b], j), R("EXP", 4 * b + j), h("att"), False, False) for j in range(4)], not hf and tune["keep"])
+                if 4 * hf + b in tune["sact"][t]:
+                    act(R("U", 4 * hf + b), R(banks[b]), ACT.Sign)
+                else:
+                    ts(R("U", 4 * hf + b), R(banks[b]), -1.0, ALU.max, 1.0, ALU.min)
+                mm([(H, R("ID"), R("U", 4 * hf + b, S_(128 * j, 128 * j + 128)), False, False) for j in range(4)])
+            if tune["lohi"]:
+                if not hf:
+                    ts(R("lo"), R("va"), -2.0, ALU.add, 0.0, ALU.max)
+                    ts(R("hi"), R("va"), 2.0, ALU.add, 63.0, ALU.min)
+                tt(X, H, h("lo"), ALU.max)
+                tt(R("V", S_(n0 + 128 * hf, n0 + 128 * hf + 128)), X, h("hi"), ALU.min)
+                continue
+            ts(h("cl"), H, -2.0, ALU.max, 2.0, ALU.min)
+            mm([(X, R("ID"), h("va"), True, False), (X, R("ID"), h("cl"), False, False)])
+            ts(R("V", S_(n0 + 128 * hf, n0 + 128 * hf + 128)), X, 0.0, ALU.max, 63.0, ALU.min)
+        if t < RO - 1:
+            send("V", t, n0, "av%d" % t)
+        dma(R("yv", S_(L * t, L * t + L)), R("V", S_(n0, n0 + L)))
     dma(R("ys"), R("YS")); dma(R("yb"), R("B64"))
     dma(R("YL"), RP("T2", S_(0, 128, 16), S_(0, W))); dma(R("YH"), RP("T2", S_(1, 128, 16), S_(0, W)))
     tt(R("YK"), R("YL"), R("YH"), ALU.add)
-    ts(R("YK"), R("YK"), 1.0 / EPS, ALU.mult)
+    act(R("YK"), R("YK"), ACT.Identity, 0.0, 1.0 / EPS)
     dma(R("yk"), R("YK"))
 
     hist = {}
@@ -533,7 +568,7 @@ def build_ops(tune):
                 if j == o["id"]:
                     continue
                 if ps and o["eng"] == "p" and ops[j]["eng"] == "p":
-                    if ops[j]["group"] != o["group"] or j == o["group"]:
+                    if ops[j]["group"] != o["group"] or j == o["group"] or "seq" in ops[j]:
                         dep.add(j)
                 elif (ps and ops[j]["eng"] != o["eng"]) or ((wr or wr2) and (fb & fb2) and (pb & pb2)):
                     dep.add(j)
@@ -552,11 +587,11 @@ def cost(o, m):
     if k == "recv":
         return 0.0, m["rem"]
     if k == "send":
-        return 300.0, 1000.0
+        return 800.0, 1500.0
     if k == "dma":
         fo, fi = _foot(a[0]), _foot(a[1])
         by = fo[2] * fo[3] * (2 if _dtype(a[0]["n"]) in (B, U2) else 4)
-        return 60.0, m["dma"] + by / 150.0 + 5.0 * max(fo[3], fi[3])
+        return 60.0 + by / 300.0, m["dma"] + by / 200.0 + 5.0 * max(fo[3], fi[3])
     if k == "mm":
         d = sum(max(64, _foot(x[2])[2]) * (4 if _dtype(x[2]["n"]) == F4 else 1) for x in a) * m["pe"] * m["f"]
         return d, d + 100.0
@@ -622,45 +657,9 @@ def _pass(ops, cs, nxt, nprev, pr, m, back, hold):
     return order, start, end
 
 
-def schedule(ops, m, turns=4, tries=60, moves=12000):
+def schedule(ops, m, turns=3, moves=110000):
     n = len(ops)
     cs = [cost(o, m) for o in ops]
-    pred = [sorted(o["dep"]) for o in ops]
-    succ = [[] for _ in ops]
-    for o in ops:
-        for j in o["dep"]:
-            succ[j].append(o["id"])
-    best = None
-    for hold in m["holds"]:
-        pr = [0.0] * n
-        for i in range(n - 1, -1, -1):
-            pr[i] = cs[i][1] + max([pr[j] + m["lat"] for j in succ[i]] + [0.0])
-        for _ in range(turns):
-            order, st, end = _pass(ops, cs, succ, [len(x) for x in pred], pr, m, False, hold)
-            if best is None or end < best[0]:
-                best = (end, order, [st[i] + cs[i][0] for i in range(n)])
-            _o, bs, _e = _pass(ops, cs, pred, [len(x) for x in succ], [st[i] + cs[i][0] for i in range(n)], m, True, hold)
-            pr = [bs[i] + cs[i][0] for i in range(n)]
-    rng = np.random.default_rng(7)
-    for _ in range(tries):
-        hold = float(rng.choice(m["holds"]))
-        at = np.array(best[2])
-        near = np.abs(at - rng.random() * best[0]) < float(rng.choice([3000.0, 8000.0]))
-        pr = (at + near * rng.normal(0.0, float(rng.choice([300.0, 1500.0, 4000.0])), n)).tolist()
-        order, st, end = _pass(ops, cs, succ, [len(x) for x in pred], [-x for x in pr], m, False, hold)
-        if end < best[0]:
-            best = (end, order, [st[i] + cs[i][0] for i in range(n)])
-        for _ in range(1):
-            _o, bs, _e = _pass(ops, cs, pred, [len(x) for x in succ], pr, m, True, hold)
-            order, st, end = _pass(ops, cs, succ, [len(x) for x in pred], [bs[i] + cs[i][0] for i in range(n)], m, False, hold)
-            pr = [st[i] + cs[i][0] for i in range(n)]
-            if end < best[0]:
-                best = (end, order, pr)
-    return _polish(ops, best[1], m, moves) if moves else best[1]
-
-
-def _polish(ops, order, m, moves):
-    n = len(ops)
     anc = [0] * n
     pred = []
     for o in ops:
@@ -671,6 +670,26 @@ def _polish(ops, order, m, moves):
         for j in o["dep"]:
             far |= 1 << j
         anc[o["id"]] = far
+    succ = [[] for _ in ops]
+    for i in range(n):
+        for j in pred[i]:
+            succ[j].append(i)
+    best = None
+    for hold in m["holds"]:
+        pr = [0.0] * n
+        for i in range(n - 1, -1, -1):
+            pr[i] = cs[i][1] + max([pr[j] + m["lat"] for j in succ[i]] + [0.0])
+        for _ in range(turns):
+            order, st, end = _pass(ops, cs, succ, [len(x) for x in pred], pr, m, False, hold)
+            if best is None or end < best[0]:
+                best = (end, order)
+            _o, bs, _e = _pass(ops, cs, pred, [len(x) for x in succ], [st[i] + cs[i][0] for i in range(n)], m, True, hold)
+            pr = [bs[i] + cs[i][0] for i in range(n)]
+    return _polish(ops, best[1], m, moves, anc, pred) if moves else best[1]
+
+
+def _polish(ops, order, m, moves, anc, pred):
+    n = len(ops)
     eng = [o["eng"] for o in ops]
     tabs = []
     for ch in m["also"]:
@@ -678,67 +697,92 @@ def _polish(ops, order, m, moves):
         cs = [cost(o, x) for o in ops]
         tabs.append((cs, [[(j, cs[j][1] + ((0.0 if eng[i] == "p" else x["lat0"]) if eng[j] == eng[i] else x["lat"])) for j in pred[i]] for i in range(n)]))
 
-    def run(od, tab):
-        cs, pl = tab
-        st = [0.0] * n
-        by = [-1] * n
-        free = {}
-        end, last = 0.0, -1
+    def run(od, cs, pl, st, free, out, last):
+        by = {}
+        free = dict(free)
+        end, at = 0.0, -1
         for i in od:
-            s, w = free.get(eng[i], (0.0, -1))
+            e = eng[i]
+            s, w = free[e]
             for j, d in pl[i]:
                 if st[j] + d > s:
                     s, w = st[j] + d, j
             st[i], by[i] = s, w
-            if eng[i]:
-                free[eng[i]] = (s + cs[i][0], i)
-            if s + cs[i][1] > end:
-                end, last = s + cs[i][1], i
-        return end, by, last
+            if e:
+                free[e] = (s + cs[i][0], i)
+            if s + out[i] > end:
+                end, at = s + out[i], i
+        for e, d in last.items():
+            if free[e][0] + d > end:
+                end, at = free[e][0] + d, free[e][1]
+        return end, by, at, free
 
-    base = [run(order, t) for t in tabs]
-    norm = [b[0] for b in base]
-    cur = float(len(tabs))
-    best = (cur, order)
+    def frame(order, lo, hi, cs, pl):
+        st = [0.0] * n
+        free = run(order[:lo], cs, pl, st, {e: (0.0, -1) for e in eng}, st, {})[3]
+        out = [c[1] for c in cs]
+        last = {}
+        for i in reversed(order[hi:]):
+            if eng[i]:
+                out[i] = max(out[i], cs[i][0] + last.get(eng[i], 0.0))
+                last[eng[i]] = out[i]
+            for j, d in pl[i]:
+                out[j] = max(out[j], d + out[i])
+        return cs, pl, st, free, out, last
+
     rng = np.random.default_rng(11)
-    for it in range(moves):
-        _e, by, i = base[int(rng.integers(len(tabs)))]
-        pairs = []
-        while by[i] >= 0:
-            if eng[by[i]] == eng[i] and not (anc[i] >> by[i]) & 1:
-                pairs.append((by[i], i))
-            i = by[i]
-        if not pairs:
-            continue
-        p, i = pairs[int(rng.integers(len(pairs)))]
-        a, b = order.index(p), order.index(i)
-        if rng.random() < 0.5:
-            for _ in range(int(rng.integers(0, 4))):
-                c = a - 1
-                while c >= 0 and eng[order[c]] != eng[i]:
-                    c -= 1
-                if c < 0 or (anc[i] >> order[c]) & 1:
-                    break
-                a = c
-            mid = order[a:b + 1]
-            new = order[:a] + [x for x in mid if x == i or (anc[i] >> x) & 1] + [x for x in mid if x != i and not (anc[i] >> x) & 1] + order[b + 1:]
-        else:
-            for _ in range(int(rng.integers(0, 12))):
-                c = b + 1
-                while c < n and eng[order[c]] != eng[i]:
-                    c += 1
-                if c >= n or (anc[order[c]] >> p) & 1:
-                    break
-                b = c
-            mid = order[a:b + 1]
-            new = order[:a] + [x for x in mid if x != p and not (anc[x] >> p) & 1] + [x for x in mid if x == p or (anc[x] >> p) & 1] + order[b + 1:]
-        res = [run(new, t) for t in tabs]
-        val = sum(r[0] / z for r, z in zip(res, norm))
-        if val <= cur + 0.002 * (1.0 - it / moves) * rng.random():
-            order, base, cur = new, res, val
-            if val < best[0]:
-                best = (val, new)
-    return best[1]
+    spans = [(lo, min(n, lo + span)) for span in m["spans"] for lo in range(0, n - span // 2, span // 2)]
+    for lo, hi in spans:
+        st = [0.0] * n
+        run(order, tabs[0][0], tabs[0][1], st, {e: (0.0, -1) for e in eng}, st, {})
+        order = [i for _s, _k, i in sorted((st[i], k, i) for k, i in enumerate(order))]
+        frames = [frame(order, lo, hi, cs, pl) for cs, pl in tabs]
+        od = order[lo:hi]
+        base = [run(od, *f) for f in frames]
+        cur = sum(b[0] for b in base)
+        best = (cur, od)
+        turns = moves // len(spans)
+        rnd = rng.random((turns, 5)).tolist()
+        for it in range(turns):
+            r = rnd[it]
+            _e, by, i, _f = base[int(r[0] * len(tabs))]
+            pairs = []
+            while by.get(i, -1) in by:
+                if eng[by[i]] == eng[i] and not (anc[i] >> by[i]) & 1:
+                    pairs.append((by[i], i))
+                i = by[i]
+            if not pairs:
+                continue
+            p, i = pairs[int(r[1] * len(pairs))]
+            a, b = od.index(p), od.index(i)
+            if r[2] < 0.5:
+                for _ in range(int(r[3] ** 2 * 8)):
+                    c = a - 1
+                    while c >= 0 and eng[od[c]] != eng[i]:
+                        c -= 1
+                    if c < 0 or (anc[i] >> od[c]) & 1:
+                        break
+                    a = c
+                mid = od[a:b + 1]
+                new = od[:a] + [x for x in mid if x == i or (anc[i] >> x) & 1] + [x for x in mid if x != i and not (anc[i] >> x) & 1] + od[b + 1:]
+            else:
+                for _ in range(int(r[3] ** 2 * 16)):
+                    c = b + 1
+                    while c < len(od) and eng[od[c]] != eng[i]:
+                        c += 1
+                    if c >= len(od) or (anc[od[c]] >> p) & 1:
+                        break
+                    b = c
+                mid = od[a:b + 1]
+                new = od[:a] + [x for x in mid if x != p and not (anc[x] >> p) & 1] + [x for x in mid if x == p or (anc[x] >> p) & 1] + od[b + 1:]
+            res = [run(new, *f) for f in frames]
+            val = sum(x[0] for x in res)
+            if val <= cur + m["heat"] * len(tabs) * (1.0 - it / turns) * r[4]:
+                od, base, cur = new, res, val
+                if val < best[0]:
+                    best = (val, new)
+        order = order[:lo] + best[1] + order[hi:]
+    return order
 
 
 _PLAN = []
@@ -766,7 +810,7 @@ def rank_program(g, core, T, topo):
     closes = {ops[i]["group"]: i for i in order if ops[i]["eng"] == "p"}
 
     def lanes(src, dst):
-        en = topo.engines(src, dst)[::2]
+        en = topo.engines(src, dst)
         return sum(1 << x for x in en), len(en)
 
     for i in order:
@@ -830,7 +874,7 @@ def rank_program(g, core, T, topo):
             else:
                 ins = q.iota(x[0], x[1], x[2], x[3], allow_small_or_imprecise_dtypes=True)
         elif k == "asel":
-            ins = q.affine_select(x[0], x[1], x[2], ALU.is_ge, 0.0, 0, 0)
+            ins = q.affine_select(x[0], x[1], x[2], x[3], x[4], x[5], x[6])
         else:
             for z, (po, lt, rh, st, sp) in enumerate(a):
                 ins = q.matmul(_ap(T, po), _ap(T, lt), _ap(T, rh), st, closes[o["group"]] == i and z == len(a) - 1)

@@ -37,18 +37,18 @@ SCRATCH = {
     "Zp": _s([L], B), "Pp": _s([L], F4),
     "S0": _s([L], U2), "S1": _s([L], U2), "S2": _s([L], U2), "Ps": _s([L], F4), "K1": _s([L], I4), "K2": _s([L], I4),
     "G2": _s(CUBE, B), "DA": _s(CUBE, B), "DS": _s(CUBE, B), "DB": _s(CUBE, B),
-    "DC": _s(CUBE, B), "AC": _s([16, 128], B), "U": _s([8, 2 * L], B), "vr": _s(CUBE, B), "GR": _s(CUBE, B),
-    "E": _s([16, L], B), "e16": _s([L], U2), "q16": _s([L], U2), "ar16": _s([L], U2),
+    "DC": _s(CUBE, B), "AC": _s([2, 16, 128], B), "U": _s([8, 2 * L], B), "vr": _s(CUBE, B), "GR": _s(CUBE, B),
+    "E": _s([16, L], B), "k16": _s([96], U2), "CV": _s([W + L], B), "tn": _s([L], B), "q16": _s([L], U2), "ar16": _s([L], U2),
     "P1": _s([L], F4), "P2": _s([L], F4), "Pi": _s([L], I4), "ids": _s([L], I4), "Pmb": _s([L], F4),
     "sc1": _s([L], F4), "sc2": _s([L], F4), "sc3": _s([L], F4), "sc4": _s([L], F4),
-    "FL": _s([L + 16], B), "FM": _s([L + 16], B), "lo": _s([L], B), "hi": _s([L], B), "x0": _s([L], B), "cnt": _s([L], B), "cx": _s([L], B), "nf": _s([L], B),
+    "FL": _s([L + 16], B), "FM": _s([L + 16], B), "lo": _s([L], B), "hi": _s([L], B), "cnt": _s([L], B), "sgm": _s([L], B), "DD": _s([16, 128], B), "nf": _s([L], B),
     "nf4": _s([16 * len(NARROW[0])], F4), "ni4": _s([16 * len(NARROW[1])], I4), "nu2": _s([16 * len(NARROW[2])], U2),
     "sgn": _s([L + 16], B), "IDH": _s([128], B), "IDT": _s([128], B),
     "va": _s([L], B), "nFa": _s([L], B), "tk": _s([L], B), "cl": _s([L], B), "dg": _s([16, 16], B), "att": _s([L], B),
     "A1": _s([L], F4), "wx": _s([2, L], B), "fl": _s([L], B), "E4": _s([L], F4),
-    "pc": _s([8], F4), "XI": _s([148], F4), "CG": _s([128], F4), "KX": _s([L], F4),
-    "SEL": _s([6, 144], B), "BO": _s([128], B), "DW": _s([128], B), "ID": _s([128], B), "NID": _s([128], B),
-    "IDB": _s([128], B), "NIDB": _s([128], B), "QN": _s([128], B), "MAP": _s([128], B), "ID4": _s([128], F4),
+    "pc": _s([16], F4), "XI": _s([148], F4), "CG": _s([128], F4), "KX": _s([L], F4),
+    "SEL": _s([7, 144], B), "BO": _s([128], B), "DW": _s([128], B), "ID": _s([128], B), "NID": _s([128], B),
+    "IDB": _s([128], B), "NIDB": _s([128], B), "QN": _s([128], B), "MAP": _s([128], B), "QC": _s([128], B), "N2ID": _s([128], B), "ID4": _s([128], F4),
     "EXP": _s([16, 128], B), "thr": _s([L], F4), "seg": _s([L], B), "big": _s([L], B), "stp": _s([L], B),
     "cm32": _s([L], B), "one": _s([L], B), "oI": _s([3, 16], I4),
 }
@@ -60,10 +60,13 @@ SEMAPHORES = ["cv", "ca", "cp", "cg", "snt"] + ["d%d" % i for i in range(NDMA)] 
 CNT = {"v": "cv", "a": "ca", "p": "cp", "g": "cg"}
 S_ = slice
 ALL = slice(None)
-TUNE = {"zact": [4, 4, 3, 3, 3], "eact": [3, 1, 1, 2, 2], "epos": [0, 0, 0, 0, 0], "bpos": [0, 0, 0, 0, 0], "sact": [(1, 3, 5, 7)] * 5,
-        "g2v": [(), (), (), (), ()], "lowv": [1, 1, 0, 0, 0], "lohi": 1,
-        "parts": ((0, 4),), "ng": 6, "na": 0, "z0": (7, 5), "eqv": 1, "hold": (9, 9), "e4": 1, "keep": 0}
-NOM = {"f": 1.25, "ga": 1.56, "sca": 3.5, "pe": 0.42, "ov": 45.0, "lat": 110.0, "lat0": 60.0, "dma": 2000.0, "rem": 3000.0, "holds": (0.3, 0.7, 1.0), "spans": (300, 200, 300), "heat": 400.0,
+TUNE = {"zact": [4, 4, 3, 3, 3], "eact": [(2, 1, 0, 0)] + [(1, 0, 0, 0)] * 4, "epos": [(), (), (), (3,), (3,)], "bpos": [0, 0, 0, 0, 0], "sact": [(0, 1, 2, 3, 5, 7)] * 5,
+        "lowv": [1, 1, 1, 1, 1], "lohi": 2,
+        "parts": ((0, 4),), "ng": 4, "na": [2, 2, 2, 2, 2], "vba": 0, "cv0": "aavaav", "zq": [0, 0, 0, 0, 0], "fva": [(3,), (0,), (0,)], "dd": [0, 0, 0, 0, 0], "late": (0, 3), "z0": (7, 5), "eqv": 0, "hold": (9, 9), "e4": 1, "keep": 0}
+LATE = ([("g", n) for n in ("CV", "DW", "FL", "FM", "F", "KX", "CG", "seg", "zr1")] +
+        [("v", n) for n in ("B64", "Bt", "Bo", "S1", "S2", "Yt", "YS", "BO", "thr", "XBT", "B16")] +
+        [("a", n) for n in ("EXP", "big", "stp", "sgm", "cm32", "IDH", "N2ID", "NIDB", "IDB", "XB", "VBt")])
+NOM = {"f": 1.25, "ga": 1.56, "sca": 3.5, "pe": 0.42, "ov": 45.0, "lat": 110.0, "lat0": 60.0, "dma": 2000.0, "rem": 3000.0, "holds": (0.3, 0.7, 1.0), "spans": (300, 200, 300), "heat": 400.0, "seed": 11,
        "also": ({"ga": 1.25, "sca": 2.5, "f": 1.08, "lat": 230.0, "lat0": 140.0},
                 {"ga": 1.8, "sca": 5.0, "f": 1.4, "lat": 400.0, "lat0": 300.0, "rem": 6000.0, "dma": 3000.0}, {"ga": 1.2, "f": 1.2, "pe": 0.56})}
 
@@ -126,6 +129,7 @@ def _ap(T, r):
 def build_ops(tune):
     ops = []
     group = {}
+    NP = len(tune["parts"])
 
     def add(eng, kind, args, reads, writes, **kw):
         rd = [r for r in reads if isinstance(r, dict)]
@@ -182,14 +186,15 @@ def build_ops(tune):
 
     def dpass(ps, src, c0, c1, sel, first=False, mid=False):
         if mid:
-            return mm([(R(ps, S_(0, L)), R("SEL", sel, S_(15 - m, 143 - m)), R(src, S_(L * m, L * m + L)), first and m == 4 * c0, False)
-                       for m in range(4 * c0, 4 * c1)])
+            w = L // NP
+            return mm([(R(ps, S_(w * (m // 16), w * (m // 16) + w)), R("SEL", sel, S_(15 - m % 16, 143 - m % 16)), R(src, S_(w * m, w * m + w)), first and m == 4 * NP * c0, False)
+                       for m in range(4 * NP * c0, 4 * NP * c1)])
         return mm([(R(ps, S_(64 * c0, 64 * c1)), R("SEL", sel, S_(15 - m, 143 - m)), R(src, S_(1024 * c0 + m, 1024 * c1, 16)), first and m == 0, False)
                    for m in range(16)])
 
     ch = lambda n, c: R(n, S_(1024 * c, 1024 * c + 1024))
     oc = lambda n, c: R(n, S_(64 * c, 64 * c + 64))
-    ONES, KID, OWN, TWO, NEG, NEG1 = range(6)
+    ONES, KID, OWN, TWO, NEG, NEG1, OWN2 = range(7)
 
     dma(R("KI", 0), R("kid")); dma(R("Z"), R("zs")); dma(R("V", S_(0, T0)), R("vn")); dma(R("SN"), R("sn"))
     dma(R("BI"), R("bst"))
@@ -215,34 +220,50 @@ def build_ops(tune):
     iota(R("one"), [[0, L]], 1, 0)
     asel(RP("MAP", p32), RP("one", p32, S_(0, 128)), [[-4, 8], [-1, 16]], ALU.is_equal, 0.0, 0, 1)
     asel(RP("MAP", p32), RP("MAP", p32), [[0, 8], [-1, 16]], ALU.is_ge, 0.0, 3, 0)
-    for h, bank in enumerate(("p0", "p1", "p6")):
-        x = S_(512 * h, 512 * h + 512)
-        mm([(R(bank), R("QN"), R("V", x), True, False)])
-        mm([(R(bank), RP("MAP", p32), RP("GR", p32, x), False, False)])
-        if h < 2:
-            act(R("T2", x), R(bank), ACT.Identity, 0.0, -DU * EPS)
-        else:
-            ts(R("T2", x), R(bank), -DU * EPS, ALU.mult)
-    ts(pc(5), pc(1), 2.0, ALU.is_ge)
-    ts(R("SEL", ONES), R("XI", S_(0, 144)), pc(0), ALU.subtract, 11.0, ALU.is_equal)
-    asel(R("SEL", KID), R("SEL", ONES), [[1, 144]], ALU.is_ge, 0.0, -14, -1)
-    asel(R("SEL", OWN), R("SEL", ONES), [[-1, 144]], ALU.is_ge, 0.0, 13, 1)
-    for j, w in ((TWO, 2 * DU), (NEG, -DU), (NEG1, -1.0)):
-        if j != NEG1 or any(tune["bpos"]):
-            act(R("SEL", j), R("SEL", ONES), ACT.Identity, 0.0, w)
     ts(R("pJ"), R("pI"), 31, ALU.bitwise_and)
     tt(R("pJ"), R("pJ"), R("oI", 0), ALU.add)
     cp(R("oT"), R("pJ")); cp(R("oB"), R("oI", 1))
+    for b in range(2):
+        cp(R("X2", S_(0, 6), b, ALL), R("KI", 0))
+    tr(R("XT", S_(0, 192)), R("X2", S_(0, 6)))
+    for u in range(6):
+        cp(R("k16", S_(u, 96, 6)), IND(R("XT", S_(32 * u, 32 * u + 32)), R("oT", S_(0, 1))))
+    act(pc(3), pc(2), ACT.Identity, 4.0)
+    ts(R("QC"), R("XI", S_(0, 128)), pc(0), ALU.subtract, pc(3), ALU.is_equal)
+    for h, bank in enumerate(("p0", "p1", "p6")):
+        x = S_(512 * h, 512 * h + 512)
+        cp(R("CV", x), IND(R("V", S_(0, T0)), R("k16", S_(32 * h, 32 * h + 32))), tune["cv0"][h])
+        mm([(R(bank), R("QN"), R("V", x), True, False)])
+        mm([(R(bank), RP("MAP", p32), RP("GR", p32, x), False, False)])
+        mm([(R(bank), R("QC"), R("CV", x), False, False)])
+        if tune["cv0"][3 + h] == "a":
+            act(R("T2", x), R(bank), ACT.Identity, 0.0, -DU * EPS)
+        else:
+            ts(R("T2", x), R(bank), -DU * EPS, ALU.mult)
+    iota(R("CV", S_(T0, W)), [[0, W - T0]], 255, 0)
+    ts(pc(7), pc(1), 2.0, ALU.is_ge)
+    ts(pc(5), pc(1), 8.0, ALU.is_lt, pc(7), ALU.mult)
+    ts(R("SEL", ONES), R("XI", S_(0, 144)), pc(0), ALU.subtract, 11.0, ALU.is_equal)
+    act(R("SEL", OWN), R("SEL", ONES), ACT.Identity, 0.0, pc(5))
+    tt(R("SEL", KID), R("SEL", ONES), R("SEL", OWN), ALU.subtract)
+    if any(tune["fva"]):
+        ts(pc(8), pc(1), 4.0, ALU.is_lt, 2.0, ALU.mult)
+        ts(pc(9), pc(8), -1.0, ALU.add, pc(5), ALU.mult)
+        act(R("SEL", OWN2), R("SEL", ONES), ACT.Identity, 0.0, pc(9))
+    for j, w in ((TWO, 2 * DU), (NEG, -DU), (NEG1, -1.0)):
+        if j != NEG1 or any(tune["bpos"]):
+            act(R("SEL", j), R("SEL", ONES), ACT.Identity, 0.0, w)
     ts(R("BO"), R("CG"), pc(0), ALU.is_equal)
-    iota(R("FL", S_(0, 16)), [[0, 16]], 0, 0); iota(R("FM", S_(0, 16)), [[0, 16]], 0, 0)
+    iota(R("FL", S_(0, 16)), [[0, 16]], 1, 0); iota(R("FM", S_(0, 16)), [[0, 16]], 1, 0)
     act(R("cm32"), R("one"), ACT.Identity, 0.0, -1.0 / 32)
     asel(R("ID"), R("one", S_(0, 128)), [[-1, 128]], ALU.is_equal, 0.0, 0, 1)
-    for n, w in (("ID4", 1.0), ("NID", -1.0), ("IDB", BIG), ("NIDB", -BIG), ("IDH", DU / 2), ("IDT", TIE)):
+    for n, w in (("ID4", 1.0), ("NID", -1.0), ("IDB", BIG), ("NIDB", -BIG), ("IDH", DU / 2), ("IDT", TIE), ("N2ID", -2.0)):
         act(R(n), R("ID"), ACT.Identity, 0.0, w)
     asel(R("DW"), R("BO"), [[1, 128]], ALU.is_gt, 0.0, 0, -1)
     ts(R("thr"), R("KX"), pc(1), ALU.is_equal, 4096.0, ALU.mult)
     K16 = [[0, 16], [1, 16]]
     asel(R("seg"), R("one"), K16, ALU.is_gt, 0.0, 0, 0)
+    act(R("sgm"), R("seg"), ACT.Identity, -1.0)
     act(R("big"), R("seg"), ACT.Identity, 2 * BIG, -2 * BIG)
     act(R("stp"), R("seg"), ACT.Identity, 4 * BIG, -4 * BIG - DU)
     act(R("dumW"), R("XI", S_(4, 20)), ACT.Identity, pc(1), 16.0)
@@ -279,7 +300,9 @@ def build_ops(tune):
     def zrep(t):
         if t < 3:
             act(R("Zp"), IND(R("Z"), R("oP%d" % t)), ACT.Copy)
-            mm([(R("p3", S_(L, L + 16)), R("SEL", NEG, S_(15 - m, 143 - m)), R("Zp", S_(16 * m, 16 * m + 16)), m == 0, False) for m in range(16)])
+            w = 16 // NP
+            mm([(R("p3", S_(L + w * (m // 16), L + w * (m // 16) + w)), R("SEL", NEG, S_(15 - m % 16, 143 - m % 16)), R("Zp", S_(w * m, w * m + w)), m == 0, False)
+                for m in range(16 * NP)])
             cp(R("nz%d" % t), R("p3", S_(L, L + 16)), "a")
         for k in range(16):
             nv, na = tune["z0"] if t == 0 else (0, 0)
@@ -316,31 +339,42 @@ def build_ops(tune):
     whole = {}
 
     def first_dist(t):
-        cp(R("S%d" % t), IND(R("SN"), R("oP%d" % t)))
-        act(R("Pp"), IND(R("nz%d" % t), R("oB")), ACT.Identity, BIG)
-        mm([(R("p5", S_(0, L)), R("NIDB"), R("one"), True, False)])
+        mm([(R("p5", S_(0, L)), R("ID4"), R("Pp"), True, False)])
         for c in range(4):
-            tt(ch("DS", c), IND(R("V", S_(0, T0)), oc("S%d" % t, c)), ch("zr%d" % t, c), ALU.max)
+            if c in tune["fva"][t]:
+                act(ch("GR", c), IND(R("V", S_(0, T0)), oc("S%d" % t, c)), ACT.Copy)
+                for b, bank in enumerate(("p6", "p7")):
+                    x = S_(1024 * c + 512 * b, 1024 * c + 512 * b + 512)
+                    mm([(R(bank), R("ID"), R("zr%d" % t, x), True, False), (R(bank), R("NID"), R("GR", x), False, False)])
+                    act(R("DS", x), R(bank), ACT.Relu)
+            else:
+                tt(ch("DS", c), IND(R("V", S_(0, T0)), oc("S%d" % t, c)), ch("zr%d" % t, c), ALU.max)
             whole[c] = dpass("p5", "DS", c, c + 1, TWO, False, True)["id"]
 
-    def children(t):
-        win = R("T2", S_(0, T0 if t < 3 else W))
+    def offspring(t):
+        top = T0 if t < 3 else W
+        for c0, c1 in parts:
+            x = S_(64 * c0, 64 * c1)
+            mm([(R(pbank(c0), x), R("ID4"), R("Pp", x), True, False), (R(pbank(c0), x), R("IDT"), R("one", x), False, False)])
         for c in range(4):
-            if c in tune["g2v"][t]:
-                ts(ch("G2", c), IND(win, oc("S%d" % TILE[t], c)), 1.0 / EPS, ALU.mult)
-            else:
-                act(ch("G2", c), IND(win, oc("S%d" % TILE[t], c)), ACT.Identity, 0.0, 1.0 / EPS)
-            dpass("p7", "G2", c, c + 1, KID, True)
-            cp(oc("e16", c), oc("p7", c))
+            at = oc("S%d" % TILE[t], c)
+            act(ch("G2", c), IND(R("T2", S_(0, top)), at), ACT.Identity, 0.0, 1.0 / EPS)
+            tt(ch("DA", c), IND(R("CV", S_(0, top)), at), ch("zr%d" % (t % 3), c), ALU.max)
+            o = dpass(pbank(c), "DA", c, c + 1, TWO, False, t < 3)
+            dpass(pbank(c), "G2", c, c + 1, KID, False, t < 3)["after"] = o["id"]
             if t < 3:
-                dpass("p5", "G2", c, c + 1, OWN, False, True)["after"] = whole[c]
-            elif tune["e4"]:
-                act(oc("E4", c), oc("p7", c), ACT.Identity, TIE)
+                dpass("p5", "G2", c, c + 1, OWN2 if c in tune["fva"][t] else OWN, False, True)["after"] = whole[c]
         if t < 3:
-            tt(R("Ps"), R("p5", S_(0, L)), R("Pp"), ALU.add)
+            cp(R("Ps"), R("p5", S_(0, L)), "a")
 
-    act(pc(6), pc(1), ACT.Identity, 0.0, 64.0)
-    act(R("t1"), R("XI", S_(4, 20)), ACT.Identity, pc(6), 4.0)
+    if NP == 1:
+        act(pc(6), pc(1), ACT.Identity, 0.0, 64.0)
+        act(R("t1"), R("XI", S_(4, 20)), ACT.Identity, pc(6), 4.0)
+    else:
+        ts(pc(7), pc(1), 8.0, ALU.is_ge, -508.0, ALU.mult)
+        act(pc(6), pc(1), ACT.Identity, pc(7), 64.0)
+        iota(R("t2"), [[512, 2], [8, 8]], 0, 0)
+        act(R("t1"), R("t2"), ACT.Identity, pc(6))
     for t in range(3):
         ts(R("oP%d" % t), R("t1"), float(t), ALU.add)
     zrep(0)
@@ -349,8 +383,9 @@ def build_ops(tune):
     dma(R("Q", S_(0, T0)), R("nq"))["after"] = late
     dma(R("V", S_(T0, GB)), R("V", S_(0, GB - T0)))["after"] = late
     dma(R("Q", S_(T0, GB)), R("Q", S_(0, GB - T0)))
+    act(R("Pp"), IND(R("nz0"), R("oB")), ACT.Copy)
+    cp(R("S0"), IND(R("SN"), R("oP0")))
     first_dist(0)
-    children(0)
     cp(R("B64"), R("BI"))
     ts(R("Bt"), R("B64"), 0.0, ALU.is_lt, float(NONE + 1), ALU.mult)
     tt(R("Bo"), R("Bt"), R("B64"), ALU.add)
@@ -368,6 +403,8 @@ def build_ops(tune):
     ts(R("Yt"), R("SN", S_(515, 1024, 4)), 4096.0, ALU.mult)
     tt(R("YS", S_(3, 512, 4)), R("Yt"), R("SN", S_(3, 512, 4)), ALU.add)
 
+    cp(R("S1"), IND(R("SN"), R("oP1"))); cp(R("S2"), IND(R("SN"), R("oP2")))
+    start = len(ops)
     ends = lambda n: R(n, S_(15, L, 16))
     for t in range(RO):
         tau = TILE[t]
@@ -377,6 +414,7 @@ def build_ops(tune):
         D1, D2, WW, H = R("p3", S_(0, L)), R("p4", S_(0, L)), R("p5", S_(0, L)), R("p6", S_(L, 2 * L))
         nz = tune["zact"][t]
         old = "Ps" if t < 3 else "K%d" % tau
+        offspring(t)
         if t > 0:
             gv = R("V", S_(GB + L * (t - 1), GB + L * t))
             mm([(R("p4", S_(0, L)), R("ID"), gv, True, False), (R("p4", S_(0, L)), R("NID"), R("Z", S_(tau, 1024, 4)), False, True)])
@@ -386,21 +424,12 @@ def build_ops(tune):
             act(R("sgn", S_(L, L + 16)), R("p5", S_(0, 16)), ACT.Sign, 0.5 - KILL * DU)
             tt(R("Pm"), R("p5", S_(0, 16)), R("mg"), ALU.add)
             act(R("Pmb"), IND(R("Pm"), R("oB")), ACT.Identity, TIE)
-        for c in range(4):
-            if t >= 3 and tune["e4"]:
-                mm([(oc("p2", c), R("ID4"), oc("E4", c), c == 0, False)])
-            else:
-                if c == 0:
-                    mm([(R("p2", S_(0, L)), R("IDT"), R("one"), True, False)])
-                dpass(pbank(c), "G2", c, c + 1, KID, False, t < 3)
-            diff("GR", "DA", "DA", ewin, "e16", "zr%d" % (t % 3), c, tune["eact"][t], DU, pbank(c), t < 3, "GR" if c >= 4 - tune["epos"][t] else None)
-        Pn = "P2" if t else "P1"
         for (c0, c1) in parts:
             u0, u1, w0, w1 = 64 * c0, 64 * c1, 4 * c0, 4 * c1
             A = lambda n, at=0: R(n, S_(at + u0, at + u1))
             Bn = lambda n: R(n, S_(w0, w1))
             en = lambda n: R(n, S_(u0 + 15, u1, 16))
-            wide = lambda n: IND(R(n), R("oB", S_(w0, w1)))
+            wide = lambda n: IND(Bn(n), R("oB", S_(0, w1 - w0)))
             pb, yb = pbank(c0), "p4" if c0 else "p5"
             tt(A("P1"), A(pb), A(old), ALU.min)
             mm([(A(pb), R("ID4"), A("P1"), True, False)])
@@ -412,18 +441,15 @@ def build_ops(tune):
                 scan(A("sc3"), A("stp"), A(pb), 0.0, ALU.add, ALU.min)
                 cp(Bn("Ri"), en("sc3"))
             else:
-                tt(A("FM", 16), wide("th3"), A("P1"), ALU.is_gt)
-                scan(A("nf"), A("FM", 15), A("seg"), 0.0, ALU.max, ALU.mult)
+                tt(A("FM", 16), wide("th3"), A("sc2"), ALU.is_gt)
                 mm([(A(yb, L), R("ID4"), A("Pmb"), True, False)])
                 scan(A("sc1"), A("seg"), A("P1"), 0.0, ALU.mult, ALU.max)
                 ts(Bn("th1"), en("sc1"), RND, ALU.add, -RND, ALU.add)
-                tt(A("FL", 16), wide("th1"), A("P1"), ALU.is_le)
-                scan(A("cx"), A("FL", 15), A("seg"), 0.0, ALU.max, ALU.mult)
-                mm([(A(pb), R("NIDB"), A("FM", 16), False, False), (A(pb), R("IDB"), A("one"), False, False)])["seq"] = 1
-                mm([(A(pb), R("IDB"), A("nf"), False, False)])
-                mm([(A(pb), R("IDH"), A("cx"), False, False)])
-                mm([(A(yb, L), R("NIDB"), A("FL", 16), False, False), (A(yb, L), R("IDB"), A("cx"), False, False),
-                    (A(yb, L), R("IDB"), A("one"), False, False)])
+                tt(A("FL", 16), wide("th1"), A("sc1"), ALU.is_le)
+                mm([(A(pb), R("NIDB"), A("FM", 16), False, False), (A(pb), R("IDB"), A("FM", 15), False, False), (A(pb), R("IDB"), A("seg"), False, False)])
+                mm([(A(pb), R("IDH"), A("FL", 15), False, False), (A(pb), R("IDH"), A("sgm"), False, False)])
+                mm([(A(yb, L), R("NIDB"), A("FL", 16), False, False), (A(yb, L), R("IDB"), A("FL", 15), False, False),
+                    (A(yb, L), R("IDB"), A("seg"), False, False)])
                 tt(A("Pi"), A(yb, L), A("P1"), ALU.min)
                 act(A("sgn"), A("P1"), ACT.Sign, 0.5 - KILL * DU)
                 scan(A("sc3"), A("big"), A(pb), 0.0, ALU.add, ALU.min)
@@ -437,9 +463,9 @@ def build_ops(tune):
             act(A("nFa"), IND(R("F"), Bn("a16")), ACT.Identity, 0.0, -1.0)
             mm([(A(pb, L), R("BO"), A("nFa"), True, True)])
             ts(A("ar16"), A(pb, L), -1.0 / EPS, ALU.mult)
-            nv = 16 - tune["ng"] - tune["na"]
+            nv = 16 - tune["ng"] - tune["na"][t]
             for k in range(16):
-                cp(R("vr", S_(16 * u0 + k, 16 * u1, 16)), A("va"), "v" if k < nv else "a" if k < nv + tune["na"] else "g")
+                cp(R("vr", S_(16 * u0 + k, 16 * u1, 16)), A("va"), "v" if k < nv else "a" if k < nv + tune["na"][t] else "g")
         if t > 0:
             far = R("p3", S_(L, L + 16))
             mm([(far, R("ID"), R("sgn", S_(L, L + 16)), True, False)] + [(far, R("ID"), R("sgn", S_(k, L, 16)), False, False) for k in range(16)])
@@ -448,7 +474,12 @@ def build_ops(tune):
             ts(R("dd"), ends("sc1"), DU * KILL, ALU.is_lt, 4096.0, ALU.mult)
         tt(R("apf"), R("ai"), R("dd"), ALU.add)
         ts(R("ap16"), R("apf"), float(W), ALU.min)
-        tt(R("VB", S_(tau, 1024, 4)), IND(R("F"), R("ap16")), R("va"), ALU.add)
+        if tune["vba"]:
+            act(R("cl"), IND(R("F"), R("ap16")), ACT.Copy)
+            mm([(R("p4", S_(L, 2 * L)), R("ID"), R("va"), True, False), (R("p4", S_(L, 2 * L)), R("ID"), R("cl"), False, False)])
+            cp(R("VB", S_(tau, 1024, 4)), R("p4", S_(L, 2 * L)), "a")
+        else:
+            tt(R("VB", S_(tau, 1024, 4)), IND(R("F"), R("ap16")), R("va"), ALU.add)
         if t < RO - 1:
             cp(R("Q", S_(n0, n0 + L)), R("q16"))
             send("Q", t, n0, "aq%d" % t)
@@ -456,6 +487,7 @@ def build_ops(tune):
             act(R("tk"), IND(R("T2", S_(0, top)), R("a16")), ACT.Identity, 0.0, pc(5))
         if t < 3:
             zrep(t + 2)
+        wide_v = []
         for h in range(16):
             ts(R("E", h, S_(0, L - 16 * h)), R("ar16", S_(16 * h, L)), R("apf", S_(h, h + 1)), ALU.is_equal)
         last_e = len(ops) - 1
@@ -471,10 +503,10 @@ def build_ops(tune):
             mm([(low, R("ID4"), R("apf"), True, False)] + [(low, R("ID"), R("fl", S_(m, L, 16)), False, False) for m in range(16)])
             tt(R("t1"), low, R("dumW"), ALU.min)
         cp(R("o16"), R("t1"))
-        if t < 2:
-            tt(IND(R("T2"), R("o16")), R("tk"), R("F", S_(n0, n0 + L)), ALU.add)
-        else:
+        if t == RO - 1:
             cp(IND(R("T2"), R("o16")), R("F", S_(n0, n0 + L)))
+        else:
+            act(R("Pp"), IND(R("nz%d" % TILE[t + 1]), R("oB")), ACT.Copy)
         scat = len(ops) - 1
         if t == 0:
             cp(R("Pi"), R("P1"))
@@ -488,39 +520,42 @@ def build_ops(tune):
         if t < 2:
             first_dist(t + 1)
         for hf in range(2):
-            banks = ("p0", "p1", "p2", "p3" if hf else "p7")
-            if hf and t < RO - 1:
-                children(t + 1)
+            banks = ("p0", "p1", "p2", "p7")
             h = lambda n, *ix: R(n, *ix, S_(128 * hf, 128 * hf + 128))
             q4 = lambda n, j: R(n, S_(128 * j, 128 * j + 128))
             dk = lambda k: R("DC", S_(2048 * hf + k, 2048 * hf + 2048, 16))
+            nq = (2, tune["zq"][t])
+            w = 64 * nq[hf]
             sub = lambda b: [x for j in range(4) for x in [(q4(banks[b], j), R("ID"), dk(4 * b + j), j == 0, False)] +
-                             [(q4(banks[b], j), R("NID"), h("va"), False, False)] * (1 - hf)]
+                             [(R(banks[b], S_(128 * j, 128 * j + w)), R("NID"), R("va", S_(128 * hf, 128 * hf + w)), False, False)] * (w > 0)]
             mm([(h("p4"), R("BO"), h("cm32"), True, False)])
             mm([(h("p3"), R("BO"), h("nFa"), True, False)])
             for c in (2 * hf, 2 * hf + 1):
-                o = len(ops)
                 diff(None, "DB", "DB", R("VB"), "q16", "vr", c, 0, 1.0, "p3", False, "DA" if c >= 4 - tune["bpos"][t] else None)
-                if t < RO - 1 and c == tune["hold"][0]:
-                    ops[o]["after"] = last_e
-                if t < RO - 1 and c == tune["hold"][1]:
-                    ops[o]["after"] = scat
-                if hf:
+                wide_v.append(len(ops) - 3)
+                if c - 2 * hf >= nq[hf]:
                     diff(None, "DC", "GR", R("Z"), "q16", "vr", c, 0, 1.0, "p4")
-                else:
+                    wide_v.append(len(ops) - 3)
+            for x in ((0, 1) if hf == 0 else ()):
+                for c in range(2 * x, 2 * x + nq[x]):
                     act(ch("DC", c), IND(R("Z"), oc("q16", c)), ACT.Copy)
+                    for b in range(2):
+                        bank = banks[2 * (c % 2) + b]
+                        mm([y for j in range(8) for y in ((oc(bank, j), R("ID"), R("DC", S_(1024 * c + 8 * b + j, 1024 * c + 1024, 16)), j == 0, False),
+                                                          (oc(bank, j), R("NID"), oc("va", c), False, False))])
+                        act(R("AC", x, S_(8 * b, 8 * b + 8), S_(64 * (c % 2), 64 * (c % 2) + 64)), R(bank), ACT.Abs)
+                        if tune["dd"][t] and x == 0:
+                            cp(R("DD", S_(8 * b, 8 * b + 8), S_(64 * c, 64 * c + 64)), R(bank), "a")
             for b in range(4):
-                if not hf or b < 3:
+                if w:
+                    mm([(R("p4", S_(128 * hf, 128 * hf + w)), R("SEL", ONES, S_(15 - k, 143 - k)), R("AC", hf, k, S_(0, w)), False, False)
+                        for k in range(4 * b, 4 * b + 4)])
+                if tune["dd"][t] and hf == 0:
+                    mm([(R(banks[b]), R("ID"), R("DD", S_(4 * b, 4 * b + 4)), True, False)])
+                else:
                     mm(sub(b))
-                if not hf:
-                    act(R("AC", S_(4 * b, 4 * b + 4)), R(banks[b]), ACT.Abs)
-                    mm([(h("p4"), R("SEL", ONES, S_(15 - k, 143 - k)), R("AC", k), False, False) for k in range(4 * b, 4 * b + 4)])
-                    if not tune["keep"]:
-                        mm(sub(b))
             act(h("A1"), h("p3"), ACT.Abs)
             act(h("wx", 0), h("p3"), ACT.Relu, -8800.0, 8.0)
-            if hf:
-                mm(sub(3))
             if tune["eqv"]:
                 ts(h("wx", 1), h("A1"), 0.0, ALU.is_equal, 2048.0, ALU.mult)
             else:
@@ -539,15 +574,22 @@ def build_ops(tune):
                     ts(R("U", 4 * hf + b), R(banks[b]), -1.0, ALU.max, 1.0, ALU.min)
                 mm([(H, R("ID"), R("U", 4 * hf + b, S_(128 * j, 128 * j + 128)), False, False) for j in range(4)])
             if tune["lohi"]:
-                if not hf:
+                if not hf and tune["lohi"] == 1:
                     ts(R("lo"), R("va"), -2.0, ALU.add, 0.0, ALU.max)
                     ts(R("hi"), R("va"), 2.0, ALU.add, 63.0, ALU.min)
-                tt(X, H, h("lo"), ALU.max)
-                tt(R("V", S_(n0 + 128 * hf, n0 + 128 * hf + 128)), X, h("hi"), ALU.min)
-                continue
-            ts(h("cl"), H, -2.0, ALU.max, 2.0, ALU.min)
-            mm([(X, R("ID"), h("va"), True, False), (X, R("ID"), h("cl"), False, False)])
-            ts(R("V", S_(n0 + 128 * hf, n0 + 128 * hf + 128)), X, 0.0, ALU.max, 63.0, ALU.min)
+                elif not hf:
+                    act(R("lo"), R("va"), ACT.Relu, -2.0)
+                    act(R("hi"), R("va"), ACT.Relu, 61.0, -1.0)
+                    act(R("hi"), R("hi"), ACT.Identity, 63.0, -1.0)
+            new = S_(n0 + 128 * hf, n0 + 128 * hf + 128)
+            tt(X, H, h("lo"), ALU.max)
+            tt(R("V", new), X, h("hi"), ALU.min)
+            if t < RO - 1:
+                to = R("o16", S_(8 * hf, 8 * hf + 8))
+                cp(IND(R("CV"), to), R("V", new))
+                mm([(X, R("QC"), R("V", new), True, False)] + [(X, R("N2ID"), h("tk"), False, False)] * (t < 2))
+                act(h("tn"), X, ACT.Identity, 0.0, -DU * EPS)
+                tt(IND(R("T2"), to), h("tn"), R("F", new), ALU.add)
         if t < RO - 1:
             send("V", t, n0, "av%d" % t)
         dma(R("yv", S_(L * t, L * t + L)), R("V", S_(n0, n0 + L)))
@@ -578,7 +620,27 @@ def build_ops(tune):
         if "after" in o:
             dep.add(o["after"])
         o["dep"] = dep
-    return ops
+    first = lambda e, n, k=0: [o["id"] for o in ops if o["eng"] == e and o["wr"] and o["wr"][0]["n"] == n][k]
+    behind = {"g": first("g", "zr0", -1), "v": first("v", "DS", tune["late"][0]), "a": first("a", "G2", tune["late"][1])}
+    for o in ops[:start]:
+        if o["wr"] and (o["eng"], o["wr"][0]["n"]) in LATE:
+            o["dep"].add(behind[o["eng"]])
+    new, seen = [], set()
+
+    def put(i):
+        if i not in seen:
+            seen.add(i)
+            for j in sorted(ops[i]["dep"]):
+                put(j)
+            new.append(i)
+
+    for i in range(len(ops)):
+        put(i)
+    at = {i: k for k, i in enumerate(new)}
+    for o in ops:
+        o.update({x: at[o[x]] for x in ("id", "group", "after") if x in o})
+        o["dep"] = {at[j] for j in o["dep"]}
+    return [ops[i] for i in new]
 
 
 def cost(o, m):
@@ -657,7 +719,7 @@ def _pass(ops, cs, nxt, nprev, pr, m, back, hold):
     return order, start, end
 
 
-def schedule(ops, m, turns=3, moves=110000):
+def schedule(ops, m, turns=3, moves=250000):
     n = len(ops)
     cs = [cost(o, m) for o in ops]
     anc = [0] * n
@@ -697,11 +759,13 @@ def _polish(ops, order, m, moves, anc, pred):
         cs = [cost(o, x) for o in ops]
         tabs.append((cs, [[(j, cs[j][1] + ((0.0 if eng[i] == "p" else x["lat0"]) if eng[j] == eng[i] else x["lat"])) for j in pred[i]] for i in range(n)]))
 
-    def run(od, cs, pl, st, free, out, last):
-        by = {}
+    def run(od, a, cs, pl, out, last, was):
+        a -= a % 8
+        st, by, marks = was[1][:], was[2][:], was[4][:a // 8 + 1]
+        free, end, at = marks[-1]
         free = dict(free)
-        end, at = 0.0, -1
-        for i in od:
+        for k in range(a, len(od)):
+            i = od[k]
             e = eng[i]
             s, w = free[e]
             for j, d in pl[i]:
@@ -712,14 +776,16 @@ def _polish(ops, order, m, moves, anc, pred):
                 free[e] = (s + cs[i][0], i)
             if s + out[i] > end:
                 end, at = s + out[i], i
+            if k % 8 == 7:
+                marks.append((dict(free), end, at))
         for e, d in last.items():
             if free[e][0] + d > end:
                 end, at = free[e][0] + d, free[e][1]
-        return end, by, at, free
+        return end, st, by, at, marks, free
 
     def frame(order, lo, hi, cs, pl):
-        st = [0.0] * n
-        free = run(order[:lo], cs, pl, st, {e: (0.0, -1) for e in eng}, st, {})[3]
+        zero = [0.0] * n
+        was = run(order[:lo], 0, cs, pl, zero, {}, (0, zero, [-1] * n, 0, [({e: (0.0, -1) for e in eng}, 0.0, -1)]))
         out = [c[1] for c in cs]
         last = {}
         for i in reversed(order[hi:]):
@@ -728,26 +794,27 @@ def _polish(ops, order, m, moves, anc, pred):
                 last[eng[i]] = out[i]
             for j, d in pl[i]:
                 out[j] = max(out[j], d + out[i])
-        return cs, pl, st, free, out, last
+        return (cs, pl, out, last), (0, was[1], was[2], 0, [(was[5], 0.0, -1)])
 
-    rng = np.random.default_rng(11)
+    rng = np.random.default_rng(m["seed"])
     spans = [(lo, min(n, lo + span)) for span in m["spans"] for lo in range(0, n - span // 2, span // 2)]
     for lo, hi in spans:
-        st = [0.0] * n
-        run(order, tabs[0][0], tabs[0][1], st, {e: (0.0, -1) for e in eng}, st, {})
+        st = frame(order, n, n, *tabs[0])[1][1]
         order = [i for _s, _k, i in sorted((st[i], k, i) for k, i in enumerate(order))]
         frames = [frame(order, lo, hi, cs, pl) for cs, pl in tabs]
         od = order[lo:hi]
-        base = [run(od, *f) for f in frames]
+        inside = set(od)
+        base = [run(od, 0, *f, was) for f, was in frames]
         cur = sum(b[0] for b in base)
         best = (cur, od)
         turns = moves // len(spans)
         rnd = rng.random((turns, 5)).tolist()
         for it in range(turns):
             r = rnd[it]
-            _e, by, i, _f = base[int(r[0] * len(tabs))]
+            z = int(r[0] * len(tabs))
+            by, i = base[z][2], base[z][3]
             pairs = []
-            while by.get(i, -1) in by:
+            while i in inside and by[i] in inside:
                 if eng[by[i]] == eng[i] and not (anc[i] >> by[i]) & 1:
                     pairs.append((by[i], i))
                 i = by[i]
@@ -775,9 +842,13 @@ def _polish(ops, order, m, moves, anc, pred):
                     b = c
                 mid = od[a:b + 1]
                 new = od[:a] + [x for x in mid if x != p and not (anc[x] >> p) & 1] + [x for x in mid if x == p or (anc[x] >> p) & 1] + od[b + 1:]
-            res = [run(new, *f) for f in frames]
+            room = m["heat"] * len(tabs) * (1.0 - it / turns) * r[4]
+            first = run(new, a, *frames[z][0], base[z])
+            if first[0] > base[z][0] + room:
+                continue
+            res = [first if y == z else run(new, a, *frames[y][0], base[y]) for y in range(len(tabs))]
             val = sum(x[0] for x in res)
-            if val <= cur + m["heat"] * len(tabs) * (1.0 - it / turns) * r[4]:
+            if val <= cur + room:
                 od, base, cur = new, res, val
                 if val < best[0]:
                     best = (val, new)

@@ -9,7 +9,6 @@ GB, W = T0 + L * RO, T0 + L * (2 * RO - 1)
 NONE = GB - 1
 EPS = 2.0 ** -15
 DU, TIE, BIG = 16384.0, 4096.0, 2.0 ** 24
-RND = 1.5 * 2.0 ** 37
 ALU = AluOpType
 ACT = ActivationFunctionType
 
@@ -21,54 +20,58 @@ def _s(shape, d):
 
 
 CUBE = [4096]
-NARROW = (("th1", "th3", "Pm", "mg", "sg1", "dd", "apf", "t1", "t2", "Y1", "dumW", "nz0", "nz1", "nz2"), ("Ri", "ai", "pI", "pJ"),
-          ("a16", "ap16", "o16", "oT", "oB", "oP0", "oP1", "oP2"))
+NARROW = (("Pm", "dd", "apf", "t1", "t2", "Y1", "dumW", "nz0", "nz1", "nz2"), ("Ri", "ai", "pI", "pJ"),
+          ("a16", "o16", "oR", "oT", "oB", "oP0", "oP1", "oP2"))
 AT = {n: (b, 16 * i) for b, ns in zip(("nf4", "ni4", "nu2"), NARROW) for i, n in enumerate(ns)}
 SCRATCH = {
-    "V": _s([W], B), "F": _s([W + 16], B), "T2": _s([W + L], B), "Q": _s([W], I4),
-    "Z": _s([1024], B), "VB": _s([1024], F4), "VBt": _s([1024], B), "ZS": _s([480], B),
+    "V": _s([W], B), "F": _s([W], B), "T2": _s([W + L], F4), "Q": _s([W], I4),
+    "Z": _s([1024], B), "VB": _s([1024], F4), "VBt": _s([1024], B), "ZE": _s([512], B), "MB": _s([128], B),
     "SN": _s([1024], I4), "KI": _s([2, 96], I4), "KJ": _s([2, 96], I4), "KK": _s([2, 96], I4), "KL": _s([2, 96], B), "KH": _s([2, 96], B),
-    "DI": _s([120], I4), "DJ": _s([240], I4), "DL": _s([240], B),
-    "BI": _s([64], I4), "B64": _s([64], F4), "Bt": _s([64], F4), "Bo": _s([4, 16], F4), "B16": _s([64], U2),
+    "DI": _s([128], I4), "DJ": _s([256], I4), "DL": _s([256], B), "DF": _s([256], F4),
+    "BI": _s([64], I4), "B64": _s([64], F4), "Bo": _s([4, 16], F4), "B16": _s([64], U2),
     "XB": _s([4, 2, 16], F4), "XBT": _s([128], F4), "YB": _s([2, 16], F4), "YBT": _s([32], F4),
     "X2": _s([8, 2, 16], F4), "XT": _s([256], F4), "YS": _s([512], F4), "Yt": _s([128], F4), "Yc": _s([8, 16], F4),
-    "YL": _s([240], B), "YH": _s([240], B), "YK": _s([240], F4),
+    "YL": _s([240], F4), "YH": _s([240], F4), "YI": _s([240], I4), "YK": _s([240], F4),
     "zr0": _s(CUBE, B), "zr1": _s(CUBE, B), "zr2": _s(CUBE, B), "ZT": _s([16, 16, 16], B), "Z4": _s([16, 16, 4], B),
     "Zp": _s([L], B), "Pp": _s([L], F4),
-    "S0": _s([L], U2), "S1": _s([L], U2), "S2": _s([L], U2), "Ps": _s([L], F4), "K1": _s([L], I4), "K2": _s([L], I4),
+    "S0": _s([L], U2), "S1": _s([L], U2), "S2": _s([L], U2), "Ps": _s([L], F4), "Pf": _s([L], F4), "K1": _s([L], I4), "K2": _s([L], I4),
     "G2": _s(CUBE, B), "DA": _s(CUBE, B), "DS": _s(CUBE, B), "DB": _s(CUBE, B),
-    "DC": _s(CUBE, B), "AC": _s([2, 16, 128], B), "U": _s([8, 2 * L], B), "vr": _s(CUBE, B), "GR": _s(CUBE, B),
-    "E": _s([16, L], B), "k16": _s([96], U2), "CV": _s([W + L], B), "tn": _s([L], B), "q16": _s([L], U2), "ar16": _s([L], U2),
-    "P1": _s([L], F4), "P2": _s([L], F4), "Pi": _s([L], I4), "ids": _s([L], I4), "Pmb": _s([L], F4),
-    "sc1": _s([L], F4), "sc2": _s([L], F4), "sc3": _s([L], F4), "sc4": _s([L], F4),
-    "FL": _s([L + 16], B), "FM": _s([L + 16], B), "lo": _s([L], B), "hi": _s([L], B), "cnt": _s([L], B), "sgm": _s([L], B), "DD": _s([16, 128], B), "nf": _s([L], B),
+    "DC": _s(CUBE, B), "AC": _s([8, 512], B), "U": _s([8, 2 * L], B), "vr": _s(CUBE, B), "GR": _s(CUBE, B),
+    "E": _s([16, 128], B), "k16": _s([96], U2), "CV": _s([W + L], B), "tn": _s([L], F4), "q16": _s([L], U2), "ar16": _s([L], U2), "fl": _s([L], B),
+    "P1": _s([L], F4), "Pi": _s([L], I4), "ids": _s([L], I4), "Pmb": _s([L], F4),
+    "sc": _s([544], F4), "sc3": _s([L], F4), "th": _s([48], F4), "near": _s([18], F4), "oW": _s([18], U2),
+    "FF": _s([576], B), "lo": _s([L], B), "hi": _s([L], B), "cnt": _s([L], B), "nf": _s([L], B),
     "nf4": _s([16 * len(NARROW[0])], F4), "ni4": _s([16 * len(NARROW[1])], I4), "nu2": _s([16 * len(NARROW[2])], U2),
-    "sgn": _s([L + 16], B), "IDH": _s([128], B), "IDT": _s([128], B),
-    "va": _s([L], B), "nFa": _s([L], B), "tk": _s([L], B), "cl": _s([L], B), "dg": _s([16, 16], B), "att": _s([L], B),
-    "A1": _s([L], F4), "wx": _s([2, L], B), "fl": _s([L], B), "E4": _s([L], F4),
-    "pc": _s([16], F4), "XI": _s([148], F4), "CG": _s([128], F4), "KX": _s([L], F4),
-    "SEL": _s([7, 144], B), "BO": _s([128], B), "DW": _s([128], B), "ID": _s([128], B), "NID": _s([128], B),
-    "IDB": _s([128], B), "NIDB": _s([128], B), "QN": _s([128], B), "MAP": _s([128], B), "QC": _s([128], B), "N2ID": _s([128], B), "ID4": _s([128], F4),
-    "EXP": _s([16, 128], B), "thr": _s([L], F4), "seg": _s([L], B), "big": _s([L], B), "stp": _s([L], B),
-    "cm32": _s([L], B), "one": _s([L], B), "oI": _s([3, 16], I4),
+    "sgn": _s([L + 16], B), "IDH": _s([128], B), "NIDH": _s([128], B),
+    "va": _s([L], B), "nFa": _s([L], B), "tk": _s([L], B), "lv": _s([16], B), "dg": _s([16, 16], B), "att": _s([L], B),
+    "A1": _s([L], F4), "wx": _s([2, L], B),
+    "pc": _s([16], F4), "XI": _s([148], F4), "XR": _s([144], F4), "CG": _s([128], F4),
+    "SEL": _s([7, 144], B), "BO": _s([128], B), "ID": _s([128], B), "NID": _s([128], B),
+    "IDB": _s([128], B), "NIDB": _s([128], B), "QN": _s([128], B), "MAP": _s([128], B), "QC": _s([128], B), "ID4": _s([128], F4),
+    "EXP": _s([16, 128], B), "tri": _s([L], B), "DW": _s([128], B), "seg": _s([L], B), "big": _s([L], B), "stp": _s([L], B),
+    "cm32": _s([L], B), "one": _s([L], B), "oI": _s([3, 16], I4), "wr": _s([2, 16], F4),
 }
 SCRATCH.update({"p%d" % i: ("psum", [128, 512], F4) for i in range(8)})
 IO = {"vn": ([128, T0], B), "zs": ([128, 1024], B), "sn": ([128, 1024], I4), "nq": ([128, T0], I4), "kid": ([8, T0], I4),
       "bst": ([8, 1024], I4), "yv": ([128, L * RO], B), "ys": ([128, 512], F4), "yk": ([8, W], F4), "yb": ([8, 1024], F4)}
-NDMA = 56
+NDMA = 90
 SEMAPHORES = ["cv", "ca", "cp", "cg", "snt"] + ["d%d" % i for i in range(NDMA)] + ["av%d" % i for i in range(4)] + ["aq%d" % i for i in range(4)]
 CNT = {"v": "cv", "a": "ca", "p": "cp", "g": "cg"}
 S_ = slice
 ALL = slice(None)
-TUNE = {"zact": [4, 4, 3, 3, 3], "eact": [(2, 1, 0, 0)] + [(1, 0, 0, 0)] * 4, "epos": [(), (), (), (3,), (3,)], "bpos": [0, 0, 0, 0, 0], "sact": [(0, 1, 2, 3, 5, 7)] * 5,
-        "lowv": [1, 1, 1, 1, 1], "lohi": 2,
-        "parts": ((0, 4),), "ng": 4, "na": [2, 2, 2, 2, 2], "vba": 0, "cv0": "aavaav", "zq": [0, 0, 0, 0, 0], "fva": [(3,), (0,), (0,)], "dd": [0, 0, 0, 0, 0], "late": (0, 3), "z0": (7, 5), "eqv": 0, "hold": (9, 9), "e4": 1, "keep": 0}
-LATE = ([("g", n) for n in ("CV", "DW", "FL", "FM", "F", "KX", "CG", "seg", "zr1")] +
-        [("v", n) for n in ("B64", "Bt", "Bo", "S1", "S2", "Yt", "YS", "BO", "thr", "XBT", "B16")] +
-        [("a", n) for n in ("EXP", "big", "stp", "sgm", "cm32", "IDH", "N2ID", "NIDB", "IDB", "XB", "VBt")])
-NOM = {"f": 1.25, "ga": 1.56, "sca": 3.5, "pe": 0.42, "ov": 45.0, "lat": 110.0, "lat0": 60.0, "dma": 2000.0, "rem": 3000.0, "holds": (0.3, 0.7, 1.0), "spans": (300, 200, 300), "heat": 400.0, "seed": 11,
-       "also": ({"ga": 1.25, "sca": 2.5, "f": 1.08, "lat": 230.0, "lat0": 140.0},
-                {"ga": 1.8, "sca": 5.0, "f": 1.4, "lat": 400.0, "lat0": 300.0, "rem": 6000.0, "dma": 3000.0}, {"ga": 1.2, "f": 1.2, "pe": 0.56})}
+HALVES = (1, 0)
+TUNE = {"bpos": [(), (), (), (), ()], "gpos": [(), (), (), (), ()], "sact": [(0, 1, 2, 3, 5, 7)] * 5,
+        "vr": ["vvvvvvvvvvaagggg", "gggggggggggggggg"], "cv0": "aavaav", "zq": ["ppff"] * 5, "fvd": [0, 0, 0], "t2g": 0, "fva": [(3,), (), ()],
+        "late": (0, 3), "z0": (7, 5), "keep": 0, "open": 0, "vrw": 12, "cut": ()}
+LATE = ([("g", n) for n in ("DW", "FF", "zr1")] +
+        [("v", n) for n in ("B64", "YK", "Bo", "S1", "S2", "Yt", "YS", "XBT", "B16")] +
+        [("a", n) for n in ("tri", "big", "stp", "cm32", "IDH", "NIDH", "NIDB", "IDB", "XB", "VBt")])
+NOM = {"f": 1.1, "ga": 1.4, "sca": 3.5, "pe": 0.42, "ov": 50.0, "lat": 200.0, "lat0": 200.0, "dma": 2000.0, "rem": 3000.0, "snd": 1500.0, "snd1": 3000.0,
+       "gx": 50.0, "dh": 100.0, "po": 0.0, "gd": 1000.0, "gd1": 2000.0, "holds": (0.3, 0.7, 1.0), "spans": (240, 160, 240, 160), "heat": 250.0, "flip": 0.08, "seed": 11, "moves": 600000,
+       "also": ({"f": 1.0, "ga": 1.45, "lat": 200.0, "lat0": 200.0, "dma": 1500.0},
+                {"f": 1.15, "ga": 1.8, "sca": 2.5, "lat": 280.0, "lat0": 280.0, "snd": 2000.0, "gx": 100.0},
+                {"f": 1.45, "ga": 1.2, "pe": 0.5, "sca": 5.0, "rem": 4000.0, "dma": 3000.0, "snd": 2500.0, "snd1": 6000.0, "gx": 100.0, "dh": 300.0,
+                 "gd": 1800.0, "gd1": 5000.0})}
 
 
 def _shape(n):
@@ -129,7 +132,6 @@ def _ap(T, r):
 def build_ops(tune):
     ops = []
     group = {}
-    NP = len(tune["parts"])
 
     def add(eng, kind, args, reads, writes, **kw):
         rd = [r for r in reads if isinstance(r, dict)]
@@ -139,12 +141,35 @@ def build_ops(tune):
         ops.append(o)
         return o
 
+    real = lambda *x: all(_dtype(r["n"]) in (B, F4) for r in x if isinstance(r, dict))
+
+    def either(eng, alt, reads, out):
+        return add(eng, alt[eng][0], alt[eng][1], reads, [out], **({"alt": alt} if len(alt) > 1 else {}))
+
     def cp(out, a, eng="v"):
-        if eng == "a":
-            return act(out, a, ACT.Copy)
-        if eng == "g":
-            return asel(out, a, [[0, _count(out)]], ALU.is_ge, 0.0, 0, 0)
-        return add("v", "copy", (out, a), [a], [out])
+        alt = {"v": ("copy", (out, a))}
+        if real(out, a) and out["off"] is None:
+            alt["a"] = ("act", (out, a, ACT.Copy, 0.0, 1.0))
+            if a["off"] is None and _where(a["n"]) == "sbuf" and _where(out["n"]) == "sbuf":
+                alt["g"] = ("asel", (out, a, [[0, _count(out)]], ALU.is_ge, 0.0, 0, 0))
+        return either(eng, alt, [a], out)
+
+    def lin(out, a, bias, scale=1.0, eng="a", floor=False):
+        alt = {"a": ("act", (out, a, ACT.Relu if floor else ACT.Identity, bias, scale))}
+        if not floor:
+            alt["v"] = ("ts", (out, a, scale, bias, ALU.mult, ALU.add))
+        elif scale == 1.0:
+            alt["v"] = ("ts", (out, a, bias, 0.0, ALU.add, ALU.max))
+        return either(eng, alt, [a, bias, scale], out)
+
+    def bunch(n):
+        part = ops[-n:]
+        del ops[-n:]
+        alts = [o.get("alt", {o["eng"]: (o["kind"], o["args"])}) for o in part]
+        alt = {e: ("many", [x[e] for x in alts]) for e in alts[0] if all(e in x for x in alts)}
+        o = either(part[0]["eng"], alt, [], part[0]["wr"][0])
+        o["rd"], o["wr"] = [r for x in part for r in x["rd"]], [r for x in part for r in x["wr"]]
+        return o
 
     def tt(out, a, b, op):
         return add("v", "tt", (out, a, b, op), [a, b], [out])
@@ -168,7 +193,7 @@ def build_ops(tune):
         bank = lst[0][0]["n"]
         if lst[0][3]:
             group[bank] = len(ops)
-        return add("p", "mm", lst, [x for m in lst for x in m[1:3]], [m[0] for m in lst], group=group[bank], more=more)
+        return add("p", "mm", lst, [x for m in lst for x in m[1:3]], [m[0] for m in lst], group=group[bank])
 
     def iota(out, pat, base, cm):
         return add("g", "iota", (out, pat, base, cm), [], [out])
@@ -176,44 +201,45 @@ def build_ops(tune):
     def asel(out, a, pat, op, fill, base, cm):
         return add("g", "asel", (out, a, pat, op, fill, base, cm), [a], [out])
 
-    def dma(out, a, eng="s"):
-        return add(eng, "dma", (out, a), [a], [out])
+    def dma(out, a, eng="s", acc=False):
+        return add(eng, "dma", (out, a), [a] + [out] * acc, [out], acc=acc)
 
     def send(name, t, c0, sem):
         land = R(name, S_(GB + L * t, GB + L * t + L))
         add("g", "send", (land, R(name, S_(c0, c0 + L)), sem, HOPS[t]), [R(name, S_(c0, c0 + L))], [])
         add(None, "recv", sem, [], [land], after=len(ops) - 1)
 
-    def dpass(ps, src, c0, c1, sel, first=False, mid=False):
+    def dpass(ps, src, c, sel, mid=False, more=False, at=None):
         if mid:
-            w = L // NP
-            return mm([(R(ps, S_(w * (m // 16), w * (m // 16) + w)), R("SEL", sel, S_(15 - m % 16, 143 - m % 16)), R(src, S_(w * m, w * m + w)), first and m == 4 * NP * c0, False)
-                       for m in range(4 * NP * c0, 4 * NP * c1)])
-        return mm([(R(ps, S_(64 * c0, 64 * c1)), R("SEL", sel, S_(15 - m, 143 - m)), R(src, S_(1024 * c0 + m, 1024 * c1, 16)), first and m == 0, False)
-                   for m in range(16)])
+            return mm([(R(ps, S_(128 * (m // 16), 128 * (m // 16) + 128)), R("SEL", sel, S_(15 - m % 16, 143 - m % 16)), R(src, S_(128 * m, 128 * m + 128)), False, False)
+                       for m in range(8 * c, 8 * c + 8)], more)
+        at = 64 * c if at is None else at
+        return mm([(R(ps, S_(at, at + 64)), R("SEL", sel, S_(15 - m, 143 - m)), R(src, S_(1024 * c + m, 1024 * c + 1024, 16)), False, False)
+                   for m in range(16)], more)
 
     ch = lambda n, c: R(n, S_(1024 * c, 1024 * c + 1024))
     oc = lambda n, c: R(n, S_(64 * c, 64 * c + 64))
+    zc = lambda t, a, b: R("zr%d" % (t % 3), S_(a, b))
     ONES, KID, OWN, TWO, NEG, NEG1, OWN2 = range(7)
 
-    dma(R("KI", 0), R("kid")); dma(R("Z"), R("zs")); dma(R("V", S_(0, T0)), R("vn")); dma(R("SN"), R("sn"))
-    dma(R("BI"), R("bst"))
+    for out, n in ((R("KI", 0), "kid"), (R("Z"), "zs"), (R("V", S_(0, T0)), "vn"), (R("SN"), "sn"), (R("BI"), "bst")):
+        dma(out, R(n))["lead"] = 1
     pc = lambda i: R("pc", S_(i, i + 1))
     iota(R("pI"), [[0, 16]], 0, 1)
     iota(R("XI"), [[1, 148]], -4, 0)
     iota(R("oI", 0), [[32, 16]], 0, 0); iota(R("oI", 1), [[1, 16]], 0, 0)
     iota(R("CG"), [[16, 8], [0, 16]], 0, 0)
-    iota(R("KX"), [[0, 16], [1, 16]], 0, 0)
-    iota(RP("DI", S_(0, 32)), [[1, 120]], 0, 120)
+    iota(RP("DI", S_(0, 32)), [[1, 128]], 0, 128)
     ts(R("oI", 2, S_(0, 1)), R("pI", S_(0, 1)), 112, ALU.bitwise_and)
     ts(R("oI", 2, S_(1, 2)), R("pI", S_(0, 1)), 15, ALU.bitwise_and)
     ts(R("oI", 2, S_(2, 3)), R("pI", S_(0, 1)), 12, ALU.bitwise_and, 2, ALU.arith_shift_right)
     cp(R("pc", S_(0, 3)), R("oI", 2, S_(0, 3)))
-    ts(R("QN"), R("XI", S_(0, 128)), pc(0), ALU.subtract, pc(2), ALU.is_equal)
-    act(pc(4), pc(1), ACT.Identity, 0.0, 96.0)
+    ts(R("XR"), R("XI", S_(0, 144)), pc(0), ALU.subtract)
+    ts(R("QN"), R("XR", S_(0, 128)), pc(2), ALU.is_equal, 32.0, ALU.mult)
+    act(pc(4), pc(1), ACT.Silu, 0.0, 96.0)["once"] = 1300.0
     ts(R("KI", 1), R("XI", S_(4, 100)), pc(4), ALU.add)
     ts(R("KJ"), R("KI"), 63, ALU.bitwise_and); ts(R("KK"), R("KI"), 4032, ALU.bitwise_and)
-    ts(R("KL"), R("KJ"), -1.0 / DU, ALU.mult); ts(R("KH"), R("KK"), -1.0 / DU, ALU.mult)
+    ts(R("KL"), R("KJ"), 32.0, ALU.mult); cp(R("KH"), R("KK"))
     for j, (n, b) in enumerate((("KL", 0), ("KH", 0), ("KL", 1), ("KH", 1))):
         dma(RP("GR", S_(j, 32, 4), S_(0, T0)), R(n, b), "sa"[j % 2])
     p32 = S_(0, 32)
@@ -225,84 +251,105 @@ def build_ops(tune):
     cp(R("oT"), R("pJ")); cp(R("oB"), R("oI", 1))
     for b in range(2):
         cp(R("X2", S_(0, 6), b, ALL), R("KI", 0))
+    bunch(2)
     tr(R("XT", S_(0, 192)), R("X2", S_(0, 6)))
     for u in range(6):
         cp(R("k16", S_(u, 96, 6)), IND(R("XT", S_(32 * u, 32 * u + 32)), R("oT", S_(0, 1))))
-    act(pc(3), pc(2), ACT.Identity, 4.0)
-    ts(R("QC"), R("XI", S_(0, 128)), pc(0), ALU.subtract, pc(3), ALU.is_equal)
+    bunch(6)
+    lin(pc(3), pc(2), 4.0)
+    ts(R("QC"), R("XR", S_(0, 128)), pc(3), ALU.is_equal, 32.0, ALU.mult)
     for h, bank in enumerate(("p0", "p1", "p6")):
         x = S_(512 * h, 512 * h + 512)
         cp(R("CV", x), IND(R("V", S_(0, T0)), R("k16", S_(32 * h, 32 * h + 32))), tune["cv0"][h])
         mm([(R(bank), R("QN"), R("V", x), True, False)])
         mm([(R(bank), RP("MAP", p32), RP("GR", p32, x), False, False)])
         mm([(R(bank), R("QC"), R("CV", x), False, False)])
-        if tune["cv0"][3 + h] == "a":
-            act(R("T2", x), R(bank), ACT.Identity, 0.0, -DU * EPS)
-        else:
-            ts(R("T2", x), R(bank), -DU * EPS, ALU.mult)
-    iota(R("CV", S_(T0, W)), [[0, W - T0]], 255, 0)
+        cp(R("T2", x), R(bank), tune["cv0"][3 + h])
+    ms(R("CV", S_(T0, T0 + 288)), 255.0)
+    for n in (288, 576, 1152):
+        dma(R("CV", S_(T0 + n, T0 + 2 * n)), R("CV", S_(T0, T0 + n)))
     ts(pc(7), pc(1), 2.0, ALU.is_ge)
     ts(pc(5), pc(1), 8.0, ALU.is_lt, pc(7), ALU.mult)
-    ts(R("SEL", ONES), R("XI", S_(0, 144)), pc(0), ALU.subtract, 11.0, ALU.is_equal)
-    act(R("SEL", OWN), R("SEL", ONES), ACT.Identity, 0.0, pc(5))
-    tt(R("SEL", KID), R("SEL", ONES), R("SEL", OWN), ALU.subtract)
-    if any(tune["fva"]):
-        ts(pc(8), pc(1), 4.0, ALU.is_lt, 2.0, ALU.mult)
-        ts(pc(9), pc(8), -1.0, ALU.add, pc(5), ALU.mult)
-        act(R("SEL", OWN2), R("SEL", ONES), ACT.Identity, 0.0, pc(9))
+    ts(R("SEL", ONES), R("XR"), 11.0, ALU.is_equal)
+    iota(R("wr", 0), [[1, 16]], 0, 0)
+    ts(R("wr", 1), R("wr", 0), pc(1), ALU.is_equal)
+    wcol = lambda j: R("wr", 1, S_(j, j + 1))
+    for j, d, q, w in ((KID, 0, 2, -DU / 32), (OWN, 2, 1, -DU / 32), (OWN2, 2, 1, DU / 32)):
+        if j != OWN2 or any(tune["fva"]):
+            ts(pc(8 + j % 3), pc(2), float(q), ALU.is_equal, w, ALU.mult)
+            lin(pc(8 + j % 3), wcol(d), pc(8 + j % 3), 1.0 / 32)
+            lin(pc(8 + j % 3), wcol(d + 1), pc(8 + j % 3))
+            lin(R("SEL", j), R("SEL", ONES), 0.0, pc(8 + j % 3))
+    lin(pc(11), wcol(0), EPS, -EPS * 31 / 32)
+    lin(pc(12), pc(11), 0.0, -1.0)
     for j, w in ((TWO, 2 * DU), (NEG, -DU), (NEG1, -1.0)):
-        if j != NEG1 or any(tune["bpos"]):
-            act(R("SEL", j), R("SEL", ONES), ACT.Identity, 0.0, w)
+        lin(R("SEL", j), R("SEL", ONES), 0.0, w)
     ts(R("BO"), R("CG"), pc(0), ALU.is_equal)
-    iota(R("FL", S_(0, 16)), [[0, 16]], 1, 0); iota(R("FM", S_(0, 16)), [[0, 16]], 1, 0)
-    act(R("cm32"), R("one"), ACT.Identity, 0.0, -1.0 / 32)
+    iota(R("FF", S_(15, 576, 288)), [[0, 2]], 1, 0)
+    iota(R("near"), [[-16383, 2], [0, 9]], 8192, 0)
+    for hf in HALVES:
+        iota(R("sc", S_(272 * hf + 128, 272 * hf + 144)), [[0, 16]], 0, 0)
+    cp(R("oW"), R("XI", S_(4, 22)))
+    lin(R("cm32"), R("one"), 0.0, -1.0 / 32)
     asel(R("ID"), R("one", S_(0, 128)), [[-1, 128]], ALU.is_equal, 0.0, 0, 1)
-    for n, w in (("ID4", 1.0), ("NID", -1.0), ("IDB", BIG), ("NIDB", -BIG), ("IDH", DU / 2), ("IDT", TIE), ("N2ID", -2.0)):
-        act(R(n), R("ID"), ACT.Identity, 0.0, w)
+    for n, w in (("ID4", 1.0), ("NID", -1.0), ("IDB", BIG), ("NIDB", -BIG), ("IDH", DU / 2), ("NIDH", -DU / 2)):
+        lin(R(n), R("ID"), 0.0, w)
     asel(R("DW"), R("BO"), [[1, 128]], ALU.is_gt, 0.0, 0, -1)
-    ts(R("thr"), R("KX"), pc(1), ALU.is_equal, 4096.0, ALU.mult)
+    ts(R("oR"), R("wr", 0), 0.0, ALU.mult, pc(1), ALU.add)
+    lin(R("tri"), IND(R("wr", 1), R("oR")), 0.0, 4096.0)
     K16 = [[0, 16], [1, 16]]
     asel(R("seg"), R("one"), K16, ALU.is_gt, 0.0, 0, 0)
-    act(R("sgm"), R("seg"), ACT.Identity, -1.0)
-    act(R("big"), R("seg"), ACT.Identity, 2 * BIG, -2 * BIG)
-    act(R("stp"), R("seg"), ACT.Identity, 4 * BIG, -4 * BIG - DU)
-    act(R("dumW"), R("XI", S_(4, 20)), ACT.Identity, pc(1), 16.0)
-    act(R("dumW"), R("dumW"), ACT.Identity, float(W))
-    ms(R("ZS"), 0.0)
-    for gq in range(8):
-        dma(RP("F", S_(16 * gq + 2, 16 * gq + 16), S_(0, W)), RP("ZS", S_(0, 112)))
-    ms(R("F", S_(NONE, NONE + 1)), 200.0)
-    iota(R("F", S_(W, W + 16)), [[0, 16]], 200, 0)
-    h0, h1 = S_(0, 120), S_(120, 240)
+    lin(R("big"), R("seg"), 2 * BIG, -2 * BIG)
+    lin(R("stp"), R("seg"), 4 * BIG, -4 * BIG - DU)
+    lin(R("dumW"), R("XI", S_(4, 20)), pc(1), 16.0)
+    lin(R("dumW"), R("dumW"), float(W))
+    ms(R("ZE"), 0.0)
+    dma(RP("F", S_(2, 16), S_(0, W)), RP("ZE", S_(0, 112), S_(0, 480)))
+    ms(RP("F", p32, S_(NONE, NONE + 1)), 200.0 / EPS)
+    h0, h1 = S_(0, 128), S_(128, 256)
     ts(RP("DJ", p32, h0), RP("DI", p32), 63, ALU.bitwise_and); ts(RP("DJ", p32, h1), RP("DI", p32), 4032, ALU.bitwise_and)
-    ts(RP("DL", p32), RP("DJ", p32), EPS, ALU.mult)
-    dma(RP("F", S_(0, 1), S_(0, W)), RP("DL", p32, h0)); dma(RP("F", S_(1, 2), S_(0, W)), RP("DL", p32, h1))
-    for gq in range(1, 8):
-        dma(RP("F", S_(16 * gq, 16 * gq + 2), S_(0, W)), RP("F", S_(0, 2), S_(0, W)))
-    dma(R("T2", S_(T0, W)), R("F", S_(T0, W)))
+    ts(RP("DL", p32, h0), RP("DJ", p32, h0), 32.0, ALU.mult); cp(RP("DL", p32, h1), RP("DJ", p32, h1))
+    dma(RP("F", S_(0, 1), S_(0, W)), RP("DL", S_(0, W // 128), h0)); dma(RP("F", S_(1, 2), S_(0, W)), RP("DL", S_(0, W // 128), h1))
+    for a, b in ((16, 32), (32, 48), (48, 64), (64, 128)):
+        dma(RP("F", S_(a, b)), RP("F", S_(0, b - a)))
+    if tune["t2g"]:
+        dma(R("T2", S_(T0, W)), R("F", S_(T0, W)), "g")["once"] = 1
+    else:
+        add("v", "copy", (RP("DF", p32), RP("DL", p32)), [RP("DL", p32)], [RP("DF", p32)])
+        for a in (2, 9):
+            dma(RP("T2", S_(a, a + 7), S_(T0, W)), RP("XI", S_(0, 126), S_(0, 128)))
+        for j, h in enumerate((h0, h1)):
+            dma(RP("T2", S_(j, j + 1), S_(T0, W)), RP("DF", S_(T0 // 128, W // 128), h))
+        for a in (16, 32, 64):
+            dma(RP("T2", S_(a, 2 * a), S_(T0, W)), RP("T2", S_(0, a), S_(T0, W)))
+
+    def scat(hf):
+        out, x = IND(R("T2"), R("o16", S_(8 * hf, 8 * hf + 8))), half("tn", hf)
+        either("a", {"a": ("act", (out, x, ACT.Silu, 0.0, 1.0)), "v": ("copy", (out, x))}, [x], out)
 
     def ys_rows(tau):
         ts(R("Yt"), R("ids", S_(128, 256)), 4096.0, ALU.mult)
         tt(R("Yc"), R("Yt"), R("ids", S_(0, 128)), ALU.add)
         for b in range(2):
             cp(R("X2", ALL, b, ALL), R("Yc"), "g")
+        bunch(2)
         tr(R("XT"), R("X2"))
         cp(R("YS", S_(tau, 512, 4)), IND(R("XT"), R("oT", S_(0, 8))), "a")
 
     def yb_rows(tau):
-        act(R("Y1"), R("dd"), ACT.Identity, 0.0, -2.0)
-        tt(R("Y1"), R("Y1"), R("apf"), ALU.add)
+        lin(R("Y1"), R("lv", S_(0, 16)), -2048.0, 2048.0)
+        tt(R("Y1"), R("Y1"), R("ai"), ALU.add)
         for b in range(2):
             ts(R("YB", b), R("Y1"), -1.0, ALU.max)
+        bunch(2)
         tr(R("YBT"), R("YB"))
         cp(R("B64", S_(tau, 64, 4)), IND(R("YBT"), R("oT", S_(0, 1))), "a")
 
     def zrep(t):
         if t < 3:
-            act(R("Zp"), IND(R("Z"), R("oP%d" % t)), ACT.Copy)
-            w = 16 // NP
-            mm([(R("p3", S_(L + w * (m // 16), L + w * (m // 16) + w)), R("SEL", NEG, S_(15 - m % 16, 143 - m % 16)), R("Zp", S_(w * m, w * m + w)), m == 0, False)
-                for m in range(16 * NP)])
+            cp(R("Zp"), IND(R("Z"), R("oP%d" % t)), "a")
+            mm([(R("p3", S_(L + 8 * (m // 16), L + 8 * (m // 16) + 8)), R("SEL", NEG, S_(15 - m % 16, 143 - m % 16)), R("Zp", S_(8 * m, 8 * m + 8)), m == 0, False)
+                for m in range(32)])
             cp(R("nz%d" % t), R("p3", S_(L, L + 16)), "a")
         for k in range(16):
             nv, na = tune["z0"] if t == 0 else (0, 0)
@@ -310,204 +357,67 @@ def build_ops(tune):
                 cp(R("zr%d" % t, S_(k, 4096, 16)), R("Zp"), "v" if k < nv else "a" if k < nv + na else "g")
             else:
                 cp(R("ZT", ALL, k, ALL), R("Z4", ALL, ALL, TILE[t]), "g")
+            if k % 2 and t:
+                bunch(2)
         if t >= 3:
             dma(R("zr%d" % (t - 3)), R("ZT"))
 
-    def diff(raw, dif, out, win, off, rep, c, nact, scale, ps, mid=False, pos=None, first=False):
-        na = min(2, max(0, nact - 2 * c))
-        b0, md, b1 = 1024 * c, 1024 * c + 512 * na, 1024 * c + 1024
-        if na:
-            act(R(raw, S_(b0, md)), IND(win, R(off, S_(b0 // 16, md // 16))), ACT.Copy)
-        for h in range(na):
-            x = S_(b0 + 512 * h, b0 + 512 * h + 512)
-            mm([(R("p%d" % h), R("ID"), R(raw, x), True, False), (R("p%d" % h), R("NID"), R(rep, x), False, True)])
-            act(R(out, x), R("p%d" % h), ACT.Abs, 0.0, scale)
-        if na < 2:
-            x = S_(md, b1)
-            tt(R(dif, x), IND(win, R(off, S_(md // 16, b1 // 16))), R(rep, x), ALU.subtract)
-            if pos and not na:
-                dpass(ps, dif, c, c + 1, NEG if scale > 1 else NEG1, first, mid)
-                ts(R(pos, x), R(dif, x), 0.0, ALU.max, 2.0 * scale, ALU.mult)
-                return dpass(ps, pos, c, c + 1, ONES, False, mid)
-            act(R(out, x), R(dif, x), ACT.Abs, 0.0, scale)
-        return dpass(ps, out, c, c + 1, ONES, first, mid)
+    def sizes(dif, out, c, ps, pos):
+        less = dpass(ps, dif, c, NEG1)
+        o = either("v" if pos else "a", {"a": ("act", (ch(out, c), ch(dif, c), ACT.Abs, 0.0, 1.0)),
+                                         "v": ("ts", (ch(out, c), ch(dif, c), 0.0, 2.0, ALU.max, ALU.mult))}, [ch(dif, c)], ch(out, c))
+        o["link"], less["only"] = less["id"], o["id"]
+        return dpass(ps, out, c, ONES)
 
-    parts = tune["parts"]
-    pbank = lambda c: "p2" if c < parts[0][1] else "p6"
-    starts = [c0 for c0, c1 in parts]
+    pbank = lambda hf: "p2" if hf == HALVES[0] else "p6"
+    half = lambda n, hf, at=0: R(n, S_(at + 128 * hf, at + 128 * hf + 128))
 
+    obank = lambda hf: "p5" if hf == HALVES[0] else "p4"
     whole = {}
 
     def first_dist(t):
-        mm([(R("p5", S_(0, L)), R("ID4"), R("Pp"), True, False)])
-        for c in range(4):
+        fb = lambda c: obank(c // 2) if t == 0 else "p5"
+        for hf in HALVES:
+            mm([(half(fb(2 * hf), hf), R("ID4"), half("Pp", hf), t == 0 or hf == HALVES[0], False)])
+        for c in (2, 3, 0, 1):
             if c in tune["fva"][t]:
-                act(ch("GR", c), IND(R("V", S_(0, T0)), oc("S%d" % t, c)), ACT.Copy)
-                for b, bank in enumerate(("p6", "p7")):
+                if tune["fvd"][t]:
+                    lin(ch("GR", c), IND(R("V", S_(0, T0)), oc("S%d" % t, c)), 0.0, -1.0)
+                    dma(ch("GR", c), zc(t, 1024 * c, 1024 * c + 1024), "g", True)
+                    lin(ch("DS", c), ch("GR", c), 0.0, 1.0, "v", True)
+                else:
+                    cp(ch("GR", c), IND(R("V", S_(0, T0)), oc("S%d" % t, c)), "a")
+                for b, bank in enumerate(() if tune["fvd"][t] else ("p6", "p7")):
                     x = S_(1024 * c + 512 * b, 1024 * c + 512 * b + 512)
-                    mm([(R(bank), R("ID"), R("zr%d" % t, x), True, False), (R(bank), R("NID"), R("GR", x), False, False)])
-                    act(R("DS", x), R(bank), ACT.Relu)
+                    mm([(R(bank), R("ID"), zc(t, x.start, x.stop), True, False), (R(bank), R("NID"), R("GR", x), False, False)])
+                    lin(R("DS", x), R(bank), 0.0, 1.0, "a", True)
             else:
-                tt(ch("DS", c), IND(R("V", S_(0, T0)), oc("S%d" % t, c)), ch("zr%d" % t, c), ALU.max)
-            whole[c] = dpass("p5", "DS", c, c + 1, TWO, False, True)["id"]
+                tt(ch("DS", c), IND(R("V", S_(0, T0)), oc("S%d" % t, c)), zc(t, 1024 * c, 1024 * c + 1024), ALU.max)
+            whole[c] = dpass(fb(c), "DS", c, TWO, True)["id"]
+        if t:
+            cp(R("Pf"), R("p5", S_(0, L)), "a")
 
-    def offspring(t):
+    def offspring(t, hf):
         top = T0 if t < 3 else W
-        for c0, c1 in parts:
-            x = S_(64 * c0, 64 * c1)
-            mm([(R(pbank(c0), x), R("ID4"), R("Pp", x), True, False), (R(pbank(c0), x), R("IDT"), R("one", x), False, False)])
-        for c in range(4):
+        mm([(half(pbank(hf), hf), R("ID4"), half("Pp", hf), True, False)])
+        if t in (1, 2):
+            mm([(half(obank(hf), hf), R("ID4"), half("Pf", hf), True, False)])
+        for c in (2 * hf, 2 * hf + 1):
             at = oc("S%d" % TILE[t], c)
-            act(ch("G2", c), IND(R("T2", S_(0, top)), at), ACT.Identity, 0.0, 1.0 / EPS)
-            tt(ch("DA", c), IND(R("CV", S_(0, top)), at), ch("zr%d" % (t % 3), c), ALU.max)
-            o = dpass(pbank(c), "DA", c, c + 1, TWO, False, t < 3)
-            dpass(pbank(c), "G2", c, c + 1, KID, False, t < 3)["after"] = o["id"]
+            cut = tune["cut"] if c == 2 * HALVES[1] + 1 else ()
+            for a, b in zip((0,) + cut, cut + (64,)):
+                cp(R("G2", S_(1024 * c + 16 * a, 1024 * c + 16 * b)), IND(R("T2", S_(0, top)), R("S%d" % TILE[t], S_(64 * c + a, 64 * c + b))), "v" if a else "a")
+            gate = tt(ch("DA", c), IND(R("CV", S_(0, top)), at), zc(t, 1024 * c, 1024 * c + 1024), ALU.max)["id"]
+            o = dpass(pbank(hf), "DA", c, TWO, t < 3)
+            dpass(pbank(hf), "G2", c, KID, t < 3)["after"] = o["id"]
             if t < 3:
-                dpass("p5", "G2", c, c + 1, OWN2 if c in tune["fva"][t] else OWN, False, True)["after"] = whole[c]
+                dpass(obank(hf), "G2", c, OWN2 if c in tune["fva"][t] else OWN, True)["after"] = whole[c]
         if t < 3:
-            cp(R("Ps"), R("p5", S_(0, L)), "a")
+            lin(half("Ps", hf), half(obank(hf), hf), -TIE)
+        return gate
 
-    if NP == 1:
-        act(pc(6), pc(1), ACT.Identity, 0.0, 64.0)
-        act(R("t1"), R("XI", S_(4, 20)), ACT.Identity, pc(6), 4.0)
-    else:
-        ts(pc(7), pc(1), 8.0, ALU.is_ge, -508.0, ALU.mult)
-        act(pc(6), pc(1), ACT.Identity, pc(7), 64.0)
-        iota(R("t2"), [[512, 2], [8, 8]], 0, 0)
-        act(R("t1"), R("t2"), ACT.Identity, pc(6))
-    for t in range(3):
-        ts(R("oP%d" % t), R("t1"), float(t), ALU.add)
-    zrep(0)
-    late = len(ops) - 1
-    dma(R("Z4"), R("zs"))["after"] = late
-    dma(R("Q", S_(0, T0)), R("nq"))["after"] = late
-    dma(R("V", S_(T0, GB)), R("V", S_(0, GB - T0)))["after"] = late
-    dma(R("Q", S_(T0, GB)), R("Q", S_(0, GB - T0)))
-    act(R("Pp"), IND(R("nz0"), R("oB")), ACT.Copy)
-    cp(R("S0"), IND(R("SN"), R("oP0")))
-    first_dist(0)
-    cp(R("B64"), R("BI"))
-    ts(R("Bt"), R("B64"), 0.0, ALU.is_lt, float(NONE + 1), ALU.mult)
-    tt(R("Bo"), R("Bt"), R("B64"), ALU.add)
-    for b in range(2):
-        cp(R("XB", ALL, b, ALL), R("Bo"), "a")
-    tr(R("XBT"), R("XB"))
-    for h in range(4):
-        cp(R("B16", S_(h, 64, 4)), IND(R("XBT", S_(32 * h, 32 * h + 32)), R("oT", S_(0, 1))))
-    act(R("VBt"), IND(R("V", S_(0, GB)), R("B16")), ACT.Copy)
-    tt(R("VB"), IND(R("F"), R("B16")), R("VBt"), ALU.add)
-    ts(R("mg"), R("KX", S_(0, 16)), pc(1), ALU.is_equal, -128.0, ALU.mult)
-    for k in range(16):
-        act(R("EXP", k), R("BO"), ACT.Identity, 0.0, R("mg", S_(k, k + 1)))
-    zrep(1)
-    ts(R("Yt"), R("SN", S_(515, 1024, 4)), 4096.0, ALU.mult)
-    tt(R("YS", S_(3, 512, 4)), R("Yt"), R("SN", S_(3, 512, 4)), ALU.add)
-
-    cp(R("S1"), IND(R("SN"), R("oP1"))); cp(R("S2"), IND(R("SN"), R("oP2")))
-    start = len(ops)
-    ends = lambda n: R(n, S_(15, L, 16))
-    for t in range(RO):
+    def books(t):
         tau = TILE[t]
-        n0 = T0 + L * t
-        top = T0 if t == 0 else GB + L * t
-        ewin = R("V", S_(0, T0 if t == 0 else GB + L * (t - 1)))
-        D1, D2, WW, H = R("p3", S_(0, L)), R("p4", S_(0, L)), R("p5", S_(0, L)), R("p6", S_(L, 2 * L))
-        nz = tune["zact"][t]
-        old = "Ps" if t < 3 else "K%d" % tau
-        offspring(t)
-        if t > 0:
-            gv = R("V", S_(GB + L * (t - 1), GB + L * t))
-            mm([(R("p4", S_(0, L)), R("ID"), gv, True, False), (R("p4", S_(0, L)), R("NID"), R("Z", S_(tau, 1024, 4)), False, True)])
-            act(R("dg"), R("p4", S_(0, L)), ACT.Abs, 0.0, DU)
-            mm([(R("p5", S_(0, 16)), R("SEL", ONES, S_(15 - m, 143 - m)), R("dg", ALL, m), m == 0, False) for m in range(16)])
-            act(R("mg"), R("dumW"), ACT.Identity, GB + L * (t - 1) - W + TIE)
-            act(R("sgn", S_(L, L + 16)), R("p5", S_(0, 16)), ACT.Sign, 0.5 - KILL * DU)
-            tt(R("Pm"), R("p5", S_(0, 16)), R("mg"), ALU.add)
-            act(R("Pmb"), IND(R("Pm"), R("oB")), ACT.Identity, TIE)
-        for (c0, c1) in parts:
-            u0, u1, w0, w1 = 64 * c0, 64 * c1, 4 * c0, 4 * c1
-            A = lambda n, at=0: R(n, S_(at + u0, at + u1))
-            Bn = lambda n: R(n, S_(w0, w1))
-            en = lambda n: R(n, S_(u0 + 15, u1, 16))
-            wide = lambda n: IND(Bn(n), R("oB", S_(0, w1 - w0)))
-            pb, yb = pbank(c0), "p4" if c0 else "p5"
-            tt(A("P1"), A(pb), A(old), ALU.min)
-            mm([(A(pb), R("ID4"), A("P1"), True, False)])
-            scan(A("sc2"), A("big"), A("P1"), 0.0, ALU.add, ALU.min)
-            ts(Bn("th3"), en("sc2"), RND, ALU.add, DU - RND, ALU.add)
-            if t == 0:
-                tt(A("nf"), wide("th3"), A("P1"), ALU.is_le)
-                mm([(A(pb), R("IDB"), A("nf"), False, False)])
-                scan(A("sc3"), A("stp"), A(pb), 0.0, ALU.add, ALU.min)
-                cp(Bn("Ri"), en("sc3"))
-            else:
-                tt(A("FM", 16), wide("th3"), A("sc2"), ALU.is_gt)
-                mm([(A(yb, L), R("ID4"), A("Pmb"), True, False)])
-                scan(A("sc1"), A("seg"), A("P1"), 0.0, ALU.mult, ALU.max)
-                ts(Bn("th1"), en("sc1"), RND, ALU.add, -RND, ALU.add)
-                tt(A("FL", 16), wide("th1"), A("sc1"), ALU.is_le)
-                mm([(A(pb), R("NIDB"), A("FM", 16), False, False), (A(pb), R("IDB"), A("FM", 15), False, False), (A(pb), R("IDB"), A("seg"), False, False)])
-                mm([(A(pb), R("IDH"), A("FL", 15), False, False), (A(pb), R("IDH"), A("sgm"), False, False)])
-                mm([(A(yb, L), R("NIDB"), A("FL", 16), False, False), (A(yb, L), R("IDB"), A("FL", 15), False, False),
-                    (A(yb, L), R("IDB"), A("seg"), False, False)])
-                tt(A("Pi"), A(yb, L), A("P1"), ALU.min)
-                act(A("sgn"), A("P1"), ACT.Sign, 0.5 - KILL * DU)
-                scan(A("sc3"), A("big"), A(pb), 0.0, ALU.add, ALU.min)
-                tt(Bn("Ri"), en("sc3"), Bn("Pm"), ALU.min)
-            ts(Bn("ai"), Bn("Ri"), 4095, ALU.bitwise_and)
-            cp(Bn("a16"), Bn("ai"))
-            if t == 0:
-                scan(A("sc1"), A("seg"), A("P1"), 0.0, ALU.mult, ALU.max)
-            cp(A("va"), IND(R("V", S_(0, top)), Bn("a16")), "a")
-            cp(A("q16"), IND(R("Q", S_(0, top)), Bn("a16")))
-            act(A("nFa"), IND(R("F"), Bn("a16")), ACT.Identity, 0.0, -1.0)
-            mm([(A(pb, L), R("BO"), A("nFa"), True, True)])
-            ts(A("ar16"), A(pb, L), -1.0 / EPS, ALU.mult)
-            nv = 16 - tune["ng"] - tune["na"][t]
-            for k in range(16):
-                cp(R("vr", S_(16 * u0 + k, 16 * u1, 16)), A("va"), "v" if k < nv else "a" if k < nv + tune["na"][t] else "g")
-        if t > 0:
-            far = R("p3", S_(L, L + 16))
-            mm([(far, R("ID"), R("sgn", S_(L, L + 16)), True, False)] + [(far, R("ID"), R("sgn", S_(k, L, 16)), False, False) for k in range(16)])
-            ts(R("dd"), far, -14.0, ALU.is_lt, 4096.0, ALU.mult)
-        else:
-            ts(R("dd"), ends("sc1"), DU * KILL, ALU.is_lt, 4096.0, ALU.mult)
-        tt(R("apf"), R("ai"), R("dd"), ALU.add)
-        ts(R("ap16"), R("apf"), float(W), ALU.min)
-        if tune["vba"]:
-            act(R("cl"), IND(R("F"), R("ap16")), ACT.Copy)
-            mm([(R("p4", S_(L, 2 * L)), R("ID"), R("va"), True, False), (R("p4", S_(L, 2 * L)), R("ID"), R("cl"), False, False)])
-            cp(R("VB", S_(tau, 1024, 4)), R("p4", S_(L, 2 * L)), "a")
-        else:
-            tt(R("VB", S_(tau, 1024, 4)), IND(R("F"), R("ap16")), R("va"), ALU.add)
-        if t < RO - 1:
-            cp(R("Q", S_(n0, n0 + L)), R("q16"))
-            send("Q", t, n0, "aq%d" % t)
-        if t < 2:
-            act(R("tk"), IND(R("T2", S_(0, top)), R("a16")), ACT.Identity, 0.0, pc(5))
-        if t < 3:
-            zrep(t + 2)
-        wide_v = []
-        for h in range(16):
-            ts(R("E", h, S_(0, L - 16 * h)), R("ar16", S_(16 * h, L)), R("apf", S_(h, h + 1)), ALU.is_equal)
-        last_e = len(ops) - 1
-        mm([(WW, R("DW"), R("E", ALL, S_(0, 16)), True, False)] +
-           [(R("p5", S_(16 * h + 16, L)), R("BO"), R("E", h, S_(16, L - 16 * h)), False, False) for h in range(15)])
-        tt(R("fl"), WW, R("thr"), ALU.mult)
-        if tune["lowv"][t]:
-            scan(R("cnt"), R("seg"), R("fl"), 0.0, ALU.mult, ALU.max)
-            tt(R("t2"), ends("cnt"), R("apf"), ALU.max)
-            tt(R("t1"), R("t2"), R("dumW"), ALU.min)
-        else:
-            low = R("p5", S_(L, L + 16))
-            mm([(low, R("ID4"), R("apf"), True, False)] + [(low, R("ID"), R("fl", S_(m, L, 16)), False, False) for m in range(16)])
-            tt(R("t1"), low, R("dumW"), ALU.min)
-        cp(R("o16"), R("t1"))
-        if t == RO - 1:
-            cp(IND(R("T2"), R("o16")), R("F", S_(n0, n0 + L)))
-        else:
-            act(R("Pp"), IND(R("nz%d" % TILE[t + 1]), R("oB")), ACT.Copy)
-        scat = len(ops) - 1
         if t == 0:
             cp(R("Pi"), R("P1"))
         ts(R("ids"), R("Pi"), 4095, ALU.bitwise_and)
@@ -517,86 +427,223 @@ def build_ops(tune):
         else:
             ys_rows(tau)
             yb_rows(tau)
+
+    ts(pc(7), pc(1), 8.0, ALU.is_ge, -508.0, ALU.mult)
+    lin(pc(6), pc(1), pc(7), 64.0)
+    iota(R("t2"), [[512, 2], [8, 8]], 0, 0)
+    lin(R("t1"), R("t2"), pc(6))
+    for t in range(3):
+        ts(R("oP%d" % t), R("t1"), float(t), ALU.add)
+    zrep(0)
+    late = len(ops) - 1
+    dma(R("Z4"), R("zs"))["after"] = late
+    dma(R("Q", S_(0, T0)), R("nq"))["after"] = late
+    dma(R("V", S_(T0, GB)), R("V", S_(0, GB - T0)))["after"] = late
+    dma(R("Q", S_(T0, GB)), R("Q", S_(0, GB - T0)))
+    lin(R("Pp"), IND(R("nz0"), R("oB")), TIE)
+    cp(R("S0"), IND(R("SN"), R("oP0")))
+    first_dist(0)
+    cp(R("B64"), R("BI"))
+    ts(R("YK", S_(0, 64)), R("B64"), 0.0, ALU.is_lt, float(NONE + 1), ALU.mult)
+    tt(R("Bo"), R("YK", S_(0, 64)), R("B64"), ALU.add)
+    for b in range(2):
+        cp(R("XB", ALL, b, ALL), R("Bo"), "a")
+    bunch(2)
+    tr(R("XBT"), R("XB"))
+    for h in range(4):
+        cp(R("B16", S_(h, 64, 4)), IND(R("XBT", S_(32 * h, 32 * h + 32)), R("oT", S_(0, 1))))
+    bunch(4)
+    lin(R("VBt"), IND(R("F"), R("B16")), 0.0, pc(11))
+    tt(R("VB"), IND(R("V", S_(0, GB)), R("B16")), R("VBt"), ALU.add)
+    lin(R("MB"), R("BO"), 0.0, -128.0)
+    dma(R("EXP", S_(0, 4)), R("ZE")); dma(R("EXP", S_(4, 8)), R("ZE")); dma(R("EXP", S_(8, 16)), R("EXP", S_(0, 8)))
+    for k in range(16):
+        dma(RP("EXP", S_(k, 128, 16), k), RP("MB", S_(k, 128, 16)))
+    zrep(1)
+    ts(R("Yt"), R("SN", S_(515, 1024, 4)), 4096.0, ALU.mult)
+    tt(R("YS", S_(3, 512, 4)), R("Yt"), R("SN", S_(3, 512, 4)), ALU.add)
+
+    cp(R("S1"), IND(R("SN"), R("oP1"))); cp(R("S2"), IND(R("SN"), R("oP2")))
+    start = len(ops)
+    for t in range(RO):
+        tau = TILE[t]
+        n0 = T0 + L * t
+        top = T0 if t == 0 else GB + L * t
+        old = "Ps" if t < 3 else "K%d" % tau
+        gate = offspring(t, HALVES[0])
+        offspring(t, HALVES[1])
+        if t > 0:
+            at = len(ops)
+            books(t - 1)
+            for o in ops[at:]:
+                if o["eng"] == "v":
+                    o["after"] = gate
+            gv = R("V", S_(GB + L * (t - 1), GB + L * t))
+            gd = R("p3", S_(0, 16))
+            mm([(R("p3", S_(0, L)), R("ID"), gv, True, False), (R("p3", S_(0, L)), R("NID"), R("Z", S_(tau, 1024, 4)), False, True)])
+            act(R("dg"), R("p3", S_(0, L)), ACT.Abs, 0.0, DU)
+            mm([(gd, R("ID4"), R("dumW"), True, False)])
+            mm([(gd, R("SEL", ONES, S_(15 - m, 143 - m)), R("dg", ALL, m), False, False) for m in range(16)])
+            lin(R("Pm"), gd, GB + L * (t - 1) - W + TIE)
+            act(R("sgn", S_(L, L + 16)), R("Pm"), ACT.Sign, 0.5 - KILL * DU)
+            lin(R("Pmb"), IND(R("Pm"), R("oB")), TIE)
+        for hf in HALVES:
+            u0, u1, w0, w1 = 128 * hf, 128 * hf + 128, 8 * hf, 8 * hf + 8
+            A = lambda n, at=0: half(n, hf, at)
+            Bn = lambda n: R(n, S_(w0, w1))
+            sc = lambda j: R("sc", S_(272 * hf + 144 * j, 272 * hf + 144 * j + 128))
+            FF = lambda j, at: R("FF", S_(288 * hf + 144 * j + at, 288 * hf + 144 * j + at + 128))
+            th = lambda n: R("th", S_(24 * hf, 24 * hf + n))
+            pb, yb = pbank(hf), "p3" if hf == HALVES[0] else "p4"
+            tt(A("P1"), A(pb), A(old), ALU.min)
+            mm([(A(pb), R("ID4"), A("P1"), True, False)])
+            scan(sc(0), A("big"), A("P1"), 0.0, ALU.add, ALU.min)
+            if t == 0:
+                lin(th(8), R("sc", S_(272 * hf + 15, 272 * hf + 128, 16)), DU / 2, 1.0, "v")
+                tt(A("nf"), IND(th(8), R("oB", S_(0, 8))), A("P1"), ALU.is_le)
+                mm([(A(pb), R("IDB"), A("nf"), False, False)])
+                scan(A("sc3"), A("stp"), A(pb), 0.0, ALU.add, ALU.min)
+                cp(Bn("Ri"), R("sc3", S_(u0 + 15, u1, 16)))
+            else:
+                yp = R(yb, S_(L, L + 128))
+                mm([(yp, R("ID4"), A("Pmb"), True, False)])
+                scan(sc(1), A("seg"), A("P1"), 0.0, ALU.mult, ALU.max)
+                tt(th(17), R("sc", S_(272 * hf + 15, 272 * hf + 272, 16)), R("near", S_(1, 18)), ALU.add)
+                tt(R("FF", S_(288 * hf + 16, 288 * hf + 288)), IND(th(17), R("oW", S_(0, 17))), R("sc", S_(272 * hf, 272 * hf + 272)), ALU.is_gt)
+                mm([(A(pb), R("NIDB"), FF(0, 16), False, False), (A(pb), R("IDB"), FF(0, 15), False, False),
+                    (A(pb), R("IDB"), A("seg"), False, False), (A(pb), R("NIDH"), FF(1, 15), False, False), (A(pb), R("IDH"), A("seg"), False, False)])
+                mm([(yp, R("NIDB"), FF(1, 15), False, False), (yp, R("IDB"), FF(1, 16), False, False), (yp, R("IDB"), A("seg"), False, False)])
+                tt(A("Pi"), yp, A("P1"), ALU.min)
+                act(A("sgn"), A("P1"), ACT.Sign, 0.5 - KILL * DU)
+                scan(A("sc3"), A("big"), A(pb), 0.0, ALU.add, ALU.min)
+                tt(Bn("Ri"), R("sc3", S_(u0 + 15, u1, 16)), Bn("Pm"), ALU.min)
+            ts(Bn("ai"), Bn("Ri"), 4095, ALU.bitwise_and)
+            cp(Bn("a16"), Bn("ai"))
+            if t == 0:
+                scan(sc(1), A("seg"), A("P1"), 0.0, ALU.mult, ALU.max)
+                act(R("lv", S_(w0, w1)), R("sc", S_(272 * hf + 159, 272 * hf + 272, 16)), ACT.Sign, 0.5 - KILL * DU)
+            cp(A("va"), IND(R("V", S_(0, top)), Bn("a16")), "a")
+            cp(A("q16"), IND(R("Q", S_(0, top)), Bn("a16")))
+        lin(R("nFa"), IND(R("F"), R("a16")), 0.0, pc(12))
+        for k in range(16):
+            if k < tune["vrw"]:
+                cp(R("vr", S_(k, 4096, 16)), R("va"), tune["vr"][0][k])
+            else:
+                for x, hf in enumerate(HALVES):
+                    cp(R("vr", S_(2048 * hf + k, 2048 * hf + 2048, 16)), half("va", hf), tune["vr"][x][k])
+        if t > 0:
+            far = R("p5", S_(L, L + 16))
+            mm([(far, R("ID"), R("sgn", S_(L, L + 16)), True, False)] + [(far, R("ID"), R("sgn", S_(k, L, 16)), False, False) for k in range(16)])
+            act(R("lv", S_(0, 16)), far, ACT.Sign, 14.0)
+        vb = R("p5", S_(0, L))
+        mm([(R("p5", S_(m, L, 16)), R("EXP", m), R("lv"), m == 0, False) for m in range(16)])
+        for hf in HALVES:
+            mm([(half("p5", hf), R("ID"), half("va", hf), False, False)])
+        mm([(vb, R("NID"), R("nFa"), False, False)])
+        lin(R("VB", S_(tau, 1024, 4)), vb, 128.0)
+        if t < RO - 1:
+            cp(R("Q", S_(n0, n0 + L)), R("q16"))
+            send("Q", t, n0, "aq%d" % t)
+        if t < 2:
+            lin(R("tk"), IND(R("T2", S_(0, top)), R("a16")), 0.0, pc(5))
+        if t < 3:
+            zrep(t + 2)
+        WW = R("p5", S_(0, L))
+        mm([(R("p6", S_(L, 2 * L)), R("BO"), R("nFa"), True, True)])
+        ts(R("ar16"), R("p6", S_(L, 2 * L)), -1.0 / EPS, ALU.mult)
+        lin(R("dd"), R("lv"), 2048.0, -2048.0)
+        tt(R("apf"), R("ai"), R("dd"), ALU.add)
+        for h in range(16):
+            e = 128 * (h // 8 + 1)
+            ts(R("E", h, S_(0, e - 16 * h)), R("ar16", S_(16 * h, e)), R("apf", S_(h, h + 1)), ALU.is_equal)
+            if h % 4 == 3:
+                bunch(4)
+        mm([(WW, R("DW"), R("E", ALL, S_(0, 16)), True, False)] +
+           [(R("p5", S_(16 * h + 16, 128 * (h // 8 + 1))), R("BO"), R("E", h, S_(16, 128 - 16 * (h % 8))), False, False) for h in range(16) if h % 8 < 7])
+        tt(R("fl"), WW, R("tri"), ALU.mult)
+        scan(R("cnt"), R("seg"), R("fl"), 0.0, ALU.mult, ALU.max)
+        tt(R("t2"), R("cnt", S_(15, L, 16)), R("apf"), ALU.max)
+        tt(R("t1"), R("t2"), R("dumW"), ALU.min)
+        cp(R("o16"), R("t1"))
+        if t == RO - 1:
+            cp(R("tn"), R("F", S_(n0, n0 + L)), "a")
+            for hf in HALVES:
+                scat(hf)
+            books(t)
+        else:
+            lin(R("Pp"), IND(R("nz%d" % TILE[t + 1]), R("oB")), TIE)
         if t < 2:
             first_dist(t + 1)
-        for hf in range(2):
-            banks = ("p0", "p1", "p2", "p7")
+        banks = ("p0", "p1", "p2", "p7")
+        how = dict(zip([c for hf in HALVES for c in (2 * hf, 2 * hf + 1)], tune["zq"][t]))
+        for x, hf in enumerate(HALVES):
             h = lambda n, *ix: R(n, *ix, S_(128 * hf, 128 * hf + 128))
             q4 = lambda n, j: R(n, S_(128 * j, 128 * j + 128))
-            dk = lambda k: R("DC", S_(2048 * hf + k, 2048 * hf + 2048, 16))
-            nq = (2, tune["zq"][t])
-            w = 64 * nq[hf]
-            sub = lambda b: [x for j in range(4) for x in [(q4(banks[b], j), R("ID"), dk(4 * b + j), j == 0, False)] +
-                             [(R(banks[b], S_(128 * j, 128 * j + w)), R("NID"), R("va", S_(128 * hf, 128 * hf + w)), False, False)] * (w > 0)]
-            mm([(h("p4"), R("BO"), h("cm32"), True, False)])
-            mm([(h("p3"), R("BO"), h("nFa"), True, False)])
+            D1, D2 = h("p3"), h("p4")
+            mm([(D2, R("BO"), h("cm32"), True, False)])
+            mm([(D1, R("BO"), h("nFa"), True, False)])
+            for c in (c for c in how if x == 0 and how[c] != "f"):
+                lin(ch("DC", c), IND(R("Z"), oc("q16", c)), 0.0, -1.0 if how[c] == "d" else 1.0)
+                if how[c] == "d":
+                    dma(ch("DC", c), ch("vr", c), "g", True)
             for c in (2 * hf, 2 * hf + 1):
-                diff(None, "DB", "DB", R("VB"), "q16", "vr", c, 0, 1.0, "p3", False, "DA" if c >= 4 - tune["bpos"][t] else None)
-                wide_v.append(len(ops) - 3)
-                if c - 2 * hf >= nq[hf]:
-                    diff(None, "DC", "GR", R("Z"), "q16", "vr", c, 0, 1.0, "p4")
-                    wide_v.append(len(ops) - 3)
-            for x in ((0, 1) if hf == 0 else ()):
-                for c in range(2 * x, 2 * x + nq[x]):
-                    act(ch("DC", c), IND(R("Z"), oc("q16", c)), ACT.Copy)
-                    for b in range(2):
-                        bank = banks[2 * (c % 2) + b]
-                        mm([y for j in range(8) for y in ((oc(bank, j), R("ID"), R("DC", S_(1024 * c + 8 * b + j, 1024 * c + 1024, 16)), j == 0, False),
-                                                          (oc(bank, j), R("NID"), oc("va", c), False, False))])
-                        act(R("AC", x, S_(8 * b, 8 * b + 8), S_(64 * (c % 2), 64 * (c % 2) + 64)), R(bank), ACT.Abs)
-                        if tune["dd"][t] and x == 0:
-                            cp(R("DD", S_(8 * b, 8 * b + 8), S_(64 * c, 64 * c + 64)), R(bank), "a")
+                tt(ch("DB", c), IND(R("VB"), oc("q16", c)), ch("vr", c), ALU.subtract)
+                sizes("DB", "DA", c, "p3", 2 * x + c % 2 in tune["bpos"][t])
+                if how[c] == "f":
+                    tt(ch("DC", c), IND(R("Z"), oc("q16", c)), ch("vr", c), ALU.subtract)
+                if how[c] != "p":
+                    sizes("DC", "GR", c, "p4", 2 * x + c % 2 in tune["gpos"][t])
+                for b in range(2 if how[c] == "p" else 0):
+                    bank = banks[2 * (c % 2) + b]
+                    mm([y for j in range(8) for y in ((oc(bank, j), R("ID"), R("DC", S_(1024 * c + 8 * b + j, 1024 * c + 1024, 16)), j == 0, False),
+                                                      (oc(bank, j), R("NID"), oc("va", c), False, False))])
+                    act(R("AC", 2 * c + b), R(bank), ACT.Abs)
+                    mm([(oc("p4", c), R("SEL", ONES, S_(15 - 8 * b - j, 143 - 8 * b - j)), R("AC", 2 * c + b, S_(64 * j, 64 * j + 64)), False, False) for j in range(8)])
+            runs = [(2 * hf, 2 * hf + 2)] if how[2 * hf] == how[2 * hf + 1] else [(2 * hf, 2 * hf + 1), (2 * hf + 1, 2 * hf + 2)]
             for b in range(4):
-                if w:
-                    mm([(R("p4", S_(128 * hf, 128 * hf + w)), R("SEL", ONES, S_(15 - k, 143 - k)), R("AC", hf, k, S_(0, w)), False, False)
-                        for k in range(4 * b, 4 * b + 4)])
-                if tune["dd"][t] and hf == 0:
-                    mm([(R(banks[b]), R("ID"), R("DD", S_(4 * b, 4 * b + 4)), True, False)])
-                else:
-                    mm(sub(b))
-            act(h("A1"), h("p3"), ACT.Abs)
-            act(h("wx", 0), h("p3"), ACT.Relu, -8800.0, 8.0)
-            if tune["eqv"]:
-                ts(h("wx", 1), h("A1"), 0.0, ALU.is_equal, 2048.0, ALU.mult)
-            else:
-                act(h("wx", 1), h("A1"), ACT.Relu, 2048.0, -2.0 ** 26)
-            mm([(h("p4"), R("ID"), h("wx", 0), False, False), (h("p4"), R("NID"), h("wx", 1), False, False)])
-            tt(h("att"), h("p4"), h("A1"), ALU.is_ge)
+                lst = []
+                for j in range(4):
+                    for c0, c1 in runs:
+                        out = R(banks[b], S_(128 * j + 64 * (c0 % 2), 128 * j + 64 * (c1 - 2 * hf)))
+                        lst.append((out, R("NID" if how[c0] == "d" else "ID"), R("DC", S_(1024 * c0 + 4 * b + j, 1024 * c1, 16)), not lst, False))
+                        if how[c0] == "p":
+                            lst.append((out, R("NID"), R("va", S_(64 * c0, 64 * c1)), False, False))
+                mm(lst)
+            act(h("A1"), D1, ACT.Abs)
+            either("a", {"a": ("act", (h("wx", 0), h("A1"), ACT.Relu, -8800.0, 8.0)),
+                         "v": ("ts", (h("wx", 0), h("A1"), 1100.0, 8192.0, ALU.is_gt, ALU.mult))}, [h("A1")], h("wx", 0))
+            either("a", {"a": ("act", (h("wx", 1), h("A1"), ACT.Relu, 2048.0, -2.0 ** 26)),
+                         "v": ("ts", (h("wx", 1), h("A1"), 0.0, 2048.0, ALU.is_equal, ALU.mult))}, [h("A1")], h("wx", 1))
+            mm([(D2, R("ID"), h("wx", 0), False, False), (D2, R("NID"), h("wx", 1), False, False)], True)
+            tt(h("att"), D2, h("A1"), ALU.is_ge)
             H, X = q4("p6", 2 + hf), q4("p6", hf)
-            if tune["lohi"]:
-                mm([(H, R("ID"), h("va"), True, False)])
-            mm([(H, R("BO"), h("att"), not tune["lohi"], False)])
-            for b in range(4):
-                mm([(q4(banks[b], j), R("EXP", 4 * b + j), h("att"), False, False) for j in range(4)], not hf and tune["keep"])
-                if 4 * hf + b in tune["sact"][t]:
-                    act(R("U", 4 * hf + b), R(banks[b]), ACT.Sign)
-                else:
-                    ts(R("U", 4 * hf + b), R(banks[b]), -1.0, ALU.max, 1.0, ALU.min)
-                mm([(H, R("ID"), R("U", 4 * hf + b, S_(128 * j, 128 * j + 128)), False, False) for j in range(4)])
-            if tune["lohi"]:
-                if not hf and tune["lohi"] == 1:
-                    ts(R("lo"), R("va"), -2.0, ALU.add, 0.0, ALU.max)
-                    ts(R("hi"), R("va"), 2.0, ALU.add, 63.0, ALU.min)
-                elif not hf:
-                    act(R("lo"), R("va"), ACT.Relu, -2.0)
-                    act(R("hi"), R("va"), ACT.Relu, 61.0, -1.0)
-                    act(R("hi"), R("hi"), ACT.Identity, 63.0, -1.0)
+            mm([(H, R("ID"), h("va"), True, False)])
+            mm([(H, R("BO"), h("att"), False, False)])
+            for u in range(4):
+                mm([(q4(banks[u], j), R("EXP", 4 * u + j), h("att"), False, False) for j in range(4)])
+                sg = R("U", 4 * hf + u)
+                either("a" if 4 * x + u in tune["sact"][t] else "v", {"a": ("act", (sg, R(banks[u]), ACT.Sign, 0.0, 1.0)),
+                       "v": ("ts", (sg, R(banks[u]), -1.0, 1.0, ALU.max, ALU.min))}, [R(banks[u])], sg)
+                mm([(H, R("ID"), R("U", 4 * hf + u, S_(128 * j, 128 * j + 128)), False, False) for j in range(4)])
+            if not x:
+                lin(R("lo"), R("va"), -2.0, 1.0, "v", True)
+                ts(R("hi"), R("va"), 2.0, ALU.add, 63.0, ALU.min)
             new = S_(n0 + 128 * hf, n0 + 128 * hf + 128)
             tt(X, H, h("lo"), ALU.max)
             tt(R("V", new), X, h("hi"), ALU.min)
             if t < RO - 1:
-                to = R("o16", S_(8 * hf, 8 * hf + 8))
-                cp(IND(R("CV"), to), R("V", new))
-                mm([(X, R("QC"), R("V", new), True, False)] + [(X, R("N2ID"), h("tk"), False, False)] * (t < 2))
-                act(h("tn"), X, ACT.Identity, 0.0, -DU * EPS)
-                tt(IND(R("T2"), to), h("tn"), R("F", new), ALU.add)
+                cp(IND(R("CV"), R("o16", S_(8 * hf, 8 * hf + 8))), R("V", new))
+                mm([(X, R("ID"), R("F", new), True, False), (X, R("QC"), R("V", new), False, False)] + [(X, R("ID"), h("tk"), False, False)] * (t < 2))
+                cp(h("tn"), X, "a")
+                scat(hf)
         if t < RO - 1:
             send("V", t, n0, "av%d" % t)
         dma(R("yv", S_(L * t, L * t + L)), R("V", S_(n0, n0 + L)))
     dma(R("ys"), R("YS")); dma(R("yb"), R("B64"))
     dma(R("YL"), RP("T2", S_(0, 128, 16), S_(0, W))); dma(R("YH"), RP("T2", S_(1, 128, 16), S_(0, W)))
-    tt(R("YK"), R("YL"), R("YH"), ALU.add)
-    act(R("YK"), R("YK"), ACT.Identity, 0.0, 1.0 / EPS)
+    lin(R("YL"), R("YL"), 0.0, 1.0 / 32)
+    tt(R("YI"), R("YL"), R("YH"), ALU.add)
+    cp(R("YK"), R("YI"))
     dma(R("yk"), R("YK"))
 
     hist = {}
@@ -610,9 +657,9 @@ def build_ops(tune):
                 if j == o["id"]:
                     continue
                 if ps and o["eng"] == "p" and ops[j]["eng"] == "p":
-                    if ops[j]["group"] != o["group"] or j == o["group"] or "seq" in ops[j]:
+                    if ops[j]["group"] != o["group"] or j == o["group"]:
                         dep.add(j)
-                elif (ps and ops[j]["eng"] != o["eng"]) or ((wr or wr2) and (fb & fb2) and (pb & pb2)):
+                elif (ps and (ops[j]["eng"] != o["eng"] or "alt" in o or "alt" in ops[j])) or ((wr or wr2) and (fb & fb2) and (pb & pb2)):
                     dep.add(j)
         for r, wr in acc:
             fb, pb = _foot(r)[:2]
@@ -621,7 +668,7 @@ def build_ops(tune):
             dep.add(o["after"])
         o["dep"] = dep
     first = lambda e, n, k=0: [o["id"] for o in ops if o["eng"] == e and o["wr"] and o["wr"][0]["n"] == n][k]
-    behind = {"g": first("g", "zr0", -1), "v": first("v", "DS", tune["late"][0]), "a": first("a", "G2", tune["late"][1])}
+    behind = {"g": first("g", "zr0", 3), "v": first("v", "DS", tune["late"][0]), "a": first("a", "G2", tune["late"][1])}
     for o in ops[:start]:
         if o["wr"] and (o["eng"], o["wr"][0]["n"]) in LATE:
             o["dep"].add(behind[o["eng"]])
@@ -638,30 +685,37 @@ def build_ops(tune):
         put(i)
     at = {i: k for k, i in enumerate(new)}
     for o in ops:
-        o.update({x: at[o[x]] for x in ("id", "group", "after") if x in o})
+        o.update({x: at[o[x]] for x in ("id", "group", "after", "link", "only") if x in o})
         o["dep"] = {at[j] for j in o["dep"]}
     return [ops[i] for i in new]
 
 
-def cost(o, m):
+def cost(o, m, e=None):
     cyc = 0.83 * m["f"]
-    k, a = o["kind"], o["args"]
+    k, a = o["alt"][e] if e else (o["kind"], o["args"])
+    if k == "many":
+        d = sum(cost({"kind": x, "args": y}, m)[0] for x, y in a)
+        return d, d
     if k == "recv":
         return 0.0, m["rem"]
     if k == "send":
-        return 800.0, 1500.0
+        d = m["snd"] + m["snd1"] * (a[2] == "aq0")
+        return d, d + 700.0
     if k == "dma":
         fo, fi = _foot(a[0]), _foot(a[1])
         by = fo[2] * fo[3] * (2 if _dtype(a[0]["n"]) in (B, U2) else 4)
-        return 60.0 + by / 300.0, m["dma"] + by / 200.0 + 5.0 * max(fo[3], fi[3])
+        if o["eng"] == "g":
+            d = m["gd"] + m["gd1"] * o.get("once", 0)
+            return d, d + 0.6 * m["dma"] + by / (150.0 if o["acc"] else 200.0)
+        return m["dh"] + by / 300.0, m["dma"] + by / 200.0 + 5.0 * max(fo[3], fi[3])
     if k == "mm":
-        d = sum(max(64, _foot(x[2])[2]) * (4 if _dtype(x[2]["n"]) == F4 else 1) for x in a) * m["pe"] * m["f"]
+        d = sum(max(64, _foot(x[2])[2]) * (4 if _dtype(x[2]["n"]) == F4 else 1) for x in a) * m["pe"] * m["f"] + m["po"] * len(a)
         return d, d + 100.0
     n = _count(a[0])
     if k == "iota":
-        d = 130.0 + 2 * n * cyc
+        d = 130.0 * m["f"] + m["gx"] + 2 * n * cyc
     elif k == "asel":
-        d = 170.0 + 2 * n * cyc
+        d = 170.0 * m["f"] + m["gx"] + 2 * n * cyc
     elif a[0]["off"] is not None:
         d = 50.0 + n * m["sca"] * cyc
     elif isinstance(a[1], dict) and a[1]["off"] is not None:
@@ -671,12 +725,16 @@ def cost(o, m):
         two = all(_dtype(x["n"]) in (B, U2) for x in big)
         if k == "tt":
             c = 2.0 if _where(a[1]["n"]) == "sbuf" and _where(a[2]["n"]) == "sbuf" else 1.0
-        elif k in ("act", "red"):
+        elif k == "act":
             c = 1.0
         else:
             c = 0.5 if two else 1.0
-        d = max(64.0, n * c) * cyc + m["ov"]
+        d = max(64.0, n * c) * cyc + m["ov"] + o.get("once", 0.0)
     return d, d
+
+
+def idle(ops, o):
+    return "only" in o and ops[o["only"]]["eng"] != "v"
 
 
 def _pass(ops, cs, nxt, nprev, pr, m, back, hold):
@@ -719,9 +777,9 @@ def _pass(ops, cs, nxt, nprev, pr, m, back, hold):
     return order, start, end
 
 
-def schedule(ops, m, turns=3, moves=250000):
+def schedule(ops, m, turns=3):
     n = len(ops)
-    cs = [cost(o, m) for o in ops]
+    cs = [(0.0, 0.0) if idle(ops, o) else cost(o, m) for o in ops]
     anc = [0] * n
     pred = []
     for o in ops:
@@ -747,112 +805,215 @@ def schedule(ops, m, turns=3, moves=250000):
                 best = (end, order)
             _o, bs, _e = _pass(ops, cs, pred, [len(x) for x in succ], [st[i] + cs[i][0] for i in range(n)], m, True, hold)
             pr = [bs[i] + cs[i][0] for i in range(n)]
-    return _polish(ops, best[1], m, moves, anc, pred) if moves else best[1]
+    lead = [i for i in range(n) if "lead" in ops[i]]
+    for k in range(1, len(lead)):
+        anc[lead[k]] |= anc[lead[k - 1]] | 1 << lead[k - 1]
+    order = lead + [i for i in best[1] if i not in lead]
+    order = _polish(ops, order, m, anc, pred) if m["moves"] else order
+    for o in ops:
+        if "alt" in o:
+            o["kind"], o["args"] = o["alt"][o["eng"]]
+    return [i for i in order if not idle(ops, ops[i])]
 
 
-def _polish(ops, order, m, moves, anc, pred):
+def _polish(ops, order, m, anc, pred):
     n = len(ops)
-    eng = [o["eng"] for o in ops]
-    tabs = []
-    for ch in m["also"]:
-        x = dict(m, **ch)
-        cs = [cost(o, x) for o in ops]
-        tabs.append((cs, [[(j, cs[j][1] + ((0.0 if eng[i] == "p" else x["lat0"]) if eng[j] == eng[i] else x["lat"])) for j in pred[i]] for i in range(n)]))
+    QS = "vapgs-"
+    mixes = [dict(m, **ch) for ch in m["also"]]
+    price = [[{e: cost(o, x, e) for e in o["alt"]} if "alt" in o else {o["eng"]: cost(o, x)} for o in ops] for x in mixes]
 
-    def run(od, a, cs, pl, out, last, was):
+    def gap(x, e, f):
+        return (0.0 if e == "p" else x["lat0"]) if e == f else x["lat"]
+
+    def starts(order, z):
+        x, free, st = mixes[z], {}, [0.0] * n
+        cs = [(0.0, 0.0) if idle(ops, o) else price[z][i][o["eng"]] for i, o in enumerate(ops)]
+        for i in order:
+            e = ops[i]["eng"]
+            st[i] = max([free.get(e, 0.0)] + [st[j] + cs[j][1] + gap(x, e, ops[j]["eng"]) for j in pred[i]])
+            if e:
+                free[e] = st[i] + cs[i][0]
+        return st, cs
+
+    def run(od, a, q, F, was, lim):
+        rel, pl, hold, tail, last = F
         a -= a % 8
         st, by, marks = was[1][:], was[2][:], was[4][:a // 8 + 1]
-        free, end, at = marks[-1]
-        free = dict(free)
-        for k in range(a, len(od)):
-            i = od[k]
-            e = eng[i]
-            s, w = free[e]
+        free, who, end, at = marks[-1]
+        free, who = free[:], who[:]
+        k = a
+        for i in od[a:]:
+            e = q[i]
+            s, w = free[e], who[e]
+            if rel[i] > s:
+                s, w = rel[i], -1
             for j, d in pl[i]:
                 if st[j] + d > s:
                     s, w = st[j] + d, j
             st[i], by[i] = s, w
-            if e:
-                free[e] = (s + cs[i][0], i)
-            if s + out[i] > end:
-                end, at = s + out[i], i
-            if k % 8 == 7:
-                marks.append((dict(free), end, at))
-        for e, d in last.items():
-            if free[e][0] + d > end:
-                end, at = free[e][0] + d, free[e][1]
-        return end, st, by, at, marks, free
-
-    def frame(order, lo, hi, cs, pl):
-        zero = [0.0] * n
-        was = run(order[:lo], 0, cs, pl, zero, {}, (0, zero, [-1] * n, 0, [({e: (0.0, -1) for e in eng}, 0.0, -1)]))
-        out = [c[1] for c in cs]
-        last = {}
-        for i in reversed(order[hi:]):
-            if eng[i]:
-                out[i] = max(out[i], cs[i][0] + last.get(eng[i], 0.0))
-                last[eng[i]] = out[i]
-            for j, d in pl[i]:
-                out[j] = max(out[j], d + out[i])
-        return (cs, pl, out, last), (0, was[1], was[2], 0, [(was[5], 0.0, -1)])
+            if e < 5:
+                free[e], who[e] = s + hold[i], i
+            s += tail[i]
+            if s > end:
+                if s > lim:
+                    return None
+                end, at = s, i
+            k += 1
+            if not k & 7:
+                marks.append((free[:], who[:], end, at))
+        for e in range(5):
+            if free[e] + last[e] > end:
+                end, at = free[e] + last[e], who[e]
+        return (end, st, by, at, marks) if end <= lim else None
 
     rng = np.random.default_rng(m["seed"])
-    spans = [(lo, min(n, lo + span)) for span in m["spans"] for lo in range(0, n - span // 2, span // 2)]
+    spans = m.get("only") or [(lo, min(n, lo + span)) for span in m["spans"] for lo in range(0, n - span // 2, span // 2)]
+    Z = range(len(mixes))
     for lo, hi in spans:
-        st = frame(order, n, n, *tabs[0])[1][1]
+        st = starts(order, 0)[0]
         order = [i for _s, _k, i in sorted((st[i], k, i) for k, i in enumerate(order))]
-        frames = [frame(order, lo, hi, cs, pl) for cs, pl in tabs]
-        od = order[lo:hi]
-        inside = set(od)
-        base = [run(od, 0, *f, was) for f, was in frames]
+        ids = order[lo:hi]
+        w = len(ids)
+        loc = {i: k for k, i in enumerate(ids)}
+        q = [QS.index(ops[i]["eng"] or "-") for i in ids]
+        inner = [[loc[j] for j in pred[i] if j in loc] for i in ids]
+        nxt = [[] for _ in ids]
+        for k in range(w):
+            for j in inner[k]:
+                nxt[j].append(k)
+        up = [sum(1 << y for y in range(k) if (anc[i] >> ids[y]) & 1) for k, i in enumerate(ids)]
+        flex = {k for k, i in enumerate(ids) if "alt" in ops[i] and ops[i].get("link", i) in loc}
+        frames, beyond, full, base = [], [], [], []
+        for z in Z:
+            st, cs = starts(order, z)
+            free = [0.0] * 6
+            for i in order[:lo]:
+                if ops[i]["eng"]:
+                    free[QS.index(ops[i]["eng"])] = st[i] + cs[i][0]
+            out, last = [c[1] for c in cs], [0.0] * 5
+            for i in reversed(order[hi:]):
+                e = ops[i]["eng"]
+                if e:
+                    out[i] = max(out[i], cs[i][0] + last[QS.index(e)])
+                    last[QS.index(e)] = out[i]
+                for j in pred[i]:
+                    out[j] = max(out[j], cs[j][1] + gap(mixes[z], e, ops[j]["eng"]) + out[i])
+            rel = [max([0.0] + [st[j] + cs[j][1] + gap(mixes[z], ops[i]["eng"], ops[j]["eng"]) for j in pred[i] if j not in loc]) for i in ids]
+            beyond.append([out[i] - cs[i][1] for i in ids])
+            full.append([cs[i][1] for i in ids])
+            frames.append((rel, [None] * w, [cs[i][0] for i in ids], [0.0] * w, last))
+            base.append((0, [0.0] * w, [-1] * w, 0, [(free, [-1] * 6, 0.0, -1)]))
+
+        def links(ks):
+            for z in Z:
+                x, pl, tail, fu = mixes[z], frames[z][1], frames[z][3], full[z]
+                for k in ks:
+                    pl[k] = [(j, fu[j] + ((0.0 if q[k] == 2 else x["lat0"]) if q[j] == q[k] else x["lat"])) for j in inner[k]]
+                tail[:] = [a + b for a, b in zip(fu, beyond[z])]
+                for k in range(w - 1, -1, -1):
+                    t = tail[k]
+                    for j, d in pl[k]:
+                        if d + t > tail[j]:
+                            tail[j] = d + t
+
+        def turn(pairs):
+            undo, ks = [], set()
+            for k, e in pairs:
+                o = ops[ids[k]]
+                undo.append((k, o["eng"]))
+                o["eng"], q[k] = e, QS.index(e)
+                ks.update([k] + nxt[k])
+                for z in Z:
+                    frames[z][2][k], full[z][k] = price[z][ids[k]][e]
+                    if "link" in o:
+                        y = loc[o["link"]]
+                        frames[z][2][y], full[z][y] = price[z][o["link"]]["p"] if e == "v" else (0.0, 0.0)
+                        ks.update(nxt[y])
+            links(ks)
+            return undo
+
+        links(range(w))
+        od = list(range(w))
+        base = [run(od, 0, q, frames[z], base[z], 1e30) for z in Z]
         cur = sum(b[0] for b in base)
-        best = (cur, od)
-        turns = moves // len(spans)
-        rnd = rng.random((turns, 5)).tolist()
+        best = (cur, od, q[:])
+        way = [(None,)] * len(mixes)
+        turns = m["moves"] // len(spans)
+        rnd = rng.random((turns, 7)).tolist()
         for it in range(turns):
+            if it % 200 == 199:
+                st = base[it // 200 % len(mixes)][1]
+                od = [i for _s, _k, i in sorted((st[i], k, i) for k, i in enumerate(od))]
+                base = [run(od, 0, q, frames[z], base[z], 1e30) for z in Z]
             r = rnd[it]
-            z = int(r[0] * len(tabs))
-            by, i = base[z][2], base[z][3]
-            pairs = []
-            while i in inside and by[i] in inside:
-                if eng[by[i]] == eng[i] and not (anc[i] >> by[i]) & 1:
-                    pairs.append((by[i], i))
-                i = by[i]
-            if not pairs:
-                continue
-            p, i = pairs[int(r[1] * len(pairs))]
-            a, b = od.index(p), od.index(i)
-            if r[2] < 0.5:
-                for _ in range(int(r[3] ** 2 * 8)):
-                    c = a - 1
-                    while c >= 0 and eng[od[c]] != eng[i]:
-                        c -= 1
-                    if c < 0 or (anc[i] >> od[c]) & 1:
-                        break
-                    a = c
-                mid = od[a:b + 1]
-                new = od[:a] + [x for x in mid if x == i or (anc[i] >> x) & 1] + [x for x in mid if x != i and not (anc[i] >> x) & 1] + od[b + 1:]
+            z = int(r[0] * len(mixes))
+            if way[z][0] is not base[z]:
+                by, i = base[z][2], base[z][3]
+                pairs, can = [], []
+                while i >= 0:
+                    j = by[i]
+                    if j >= 0 and q[j] == q[i] and not (up[i] >> j) & 1:
+                        pairs.append((j, i))
+                    if i in flex:
+                        can.append(i)
+                    i = j
+                way[z] = (base[z], pairs, can)
+            pairs, can = way[z][1:]
+            undo = None
+            if r[5] < m["flip"]:
+                if not can:
+                    continue
+                k = can[int(r[1] * len(can))]
+                es = [e for e in ops[ids[k]]["alt"] if e != QS[q[k]]]
+                ch = [(k, es[int(r[2] * len(es))])]
+                if r[6] < 0.5:
+                    at = od.index(k)
+                    can = [y for y in od[max(0, at - 40):at + 40] if y in flex and QS[q[y]] == ch[0][1] and QS[q[k]] in ops[ids[y]]["alt"]]
+                    if can:
+                        ch.append((can[int(r[3] * len(can))], QS[q[k]]))
+                undo = turn(ch)
+                new, a = od, 0
             else:
-                for _ in range(int(r[3] ** 2 * 16)):
-                    c = b + 1
-                    while c < len(od) and eng[od[c]] != eng[i]:
-                        c += 1
-                    if c >= len(od) or (anc[od[c]] >> p) & 1:
-                        break
-                    b = c
-                mid = od[a:b + 1]
-                new = od[:a] + [x for x in mid if x != p and not (anc[x] >> p) & 1] + [x for x in mid if x == p or (anc[x] >> p) & 1] + od[b + 1:]
-            room = m["heat"] * len(tabs) * (1.0 - it / turns) * r[4]
-            first = run(new, a, *frames[z][0], base[z])
-            if first[0] > base[z][0] + room:
-                continue
-            res = [first if y == z else run(new, a, *frames[y][0], base[y]) for y in range(len(tabs))]
-            val = sum(x[0] for x in res)
-            if val <= cur + room:
-                od, base, cur = new, res, val
-                if val < best[0]:
-                    best = (val, new)
-        order = order[:lo] + best[1] + order[hi:]
+                if not pairs:
+                    continue
+                p, i = pairs[int(r[1] * len(pairs))]
+                a, b = od.index(p), od.index(i)
+                if r[2] < 0.5:
+                    for _ in range(int(r[3] ** 2 * 8)):
+                        c = a - 1
+                        while c >= 0 and q[od[c]] != q[i]:
+                            c -= 1
+                        if c < 0 or (up[i] >> od[c]) & 1:
+                            break
+                        a = c
+                    mid, u = od[a:b + 1], up[i] | 1 << i
+                    new = od[:a] + [x for x in mid if (u >> x) & 1] + [x for x in mid if not (u >> x) & 1] + od[b + 1:]
+                else:
+                    for _ in range(int(r[3] ** 2 * 16)):
+                        c = b + 1
+                        while c < w and q[od[c]] != q[i]:
+                            c += 1
+                        if c >= w or (up[od[c]] >> p) & 1:
+                            break
+                        b = c
+                    mid = od[a:b + 1]
+                    new = od[:a] + [x for x in mid if x != p and not (up[x] >> p) & 1] + [x for x in mid if x == p or (up[x] >> p) & 1] + od[b + 1:]
+            room = m["heat"] * len(mixes) * (1.0 - it / turns) * r[4]
+            res = [None] * len(mixes)
+            for y in [z] + [y for y in Z if y != z]:
+                res[y] = run(new, a, q, frames[y], base[y], base[y][0] + (room if y == z else 1e9))
+                if res[y] is None:
+                    break
+            if res[y] is not None and sum(x[0] for x in res) <= cur + room:
+                od, base, cur = new, res, sum(x[0] for x in res)
+                if cur < best[0]:
+                    best = (cur, new, q[:])
+            elif undo:
+                turn(undo)
+        for k, i in enumerate(ids):
+            if "alt" in ops[i]:
+                ops[i]["eng"] = QS[best[2][k]]
+        order = order[:lo] + [ids[k] for k in best[1]] + order[hi:]
     return order
 
 
@@ -876,13 +1037,37 @@ def rank_program(g, core, T, topo):
     done = {}
     cnt = {e: 0 for e in CNT}
     ndma = [0]
-    final = {}
+    final, seen = {}, {}
     nr = len(T.cores)
     closes = {ops[i]["group"]: i for i in order if ops[i]["eng"] == "p"}
 
     def lanes(src, dst):
         en = topo.engines(src, dst)
         return sum(1 << x for x in en), len(en)
+
+    def issue(q, k, a, last):
+        if k == "mm":
+            for z, (po, lt, rh, st, sp) in enumerate(a):
+                ins = q.matmul(_ap(T, po), _ap(T, lt), _ap(T, rh), st, last and z == len(a) - 1)
+            return ins
+        x = [_ap(T, r) for r in a]
+        if k == "copy":
+            return q.tensor_copy(x[0], x[1])
+        if k == "tt":
+            return q.tensor_tensor(x[0], x[1], x[2], x[3])
+        if k == "ts":
+            return q.tensor_scalar(x[0], x[1], x[2], None, x[4]) if x[5] is None else q.tensor_scalar(x[0], x[1], x[2], x[3], x[4], x[5])
+        if k == "scan":
+            return q.tensor_tensor_scan(x[0], x[1], x[2], x[3], x[4], x[5])
+        if k == "tr":
+            return q.transpose(x[0], x[1])
+        if k == "ms":
+            return q.memset(x[0], x[1])
+        if k == "act":
+            return q.activation(x[0], x[1], x[2]) if a[0]["off"] is not None else q.activation(x[0], x[1], x[2], bias=x[3], scale=x[4])
+        if k == "iota":
+            return q.iota(x[0], x[1], x[2], x[3]) if _dtype(a[0]["n"]) == I4 else q.iota(x[0], x[1], x[2], x[3], allow_small_or_imprecise_dtypes=True)
+        return q.affine_select(x[0], x[1], x[2], x[3], x[4], x[5], x[6])
 
     for i in order:
         o = ops[i]
@@ -896,7 +1081,7 @@ def rank_program(g, core, T, topo):
         kn = known[e]
         need = {}
         for j in o["dep"]:
-            if e == "p" and ops[j]["eng"] == "p":
+            if (e == "p" and ops[j]["eng"] == "p") or idle(ops, ops[j]):
                 continue
             need[j] = done[j]
         for j in sorted(need, reverse=True):
@@ -905,9 +1090,10 @@ def rank_program(g, core, T, topo):
             if kn.get(s, 0) < v and v == top:
                 q.wait_ge(T.sem[s], v)
                 kn[s] = v
+                seen[s] = max(seen.get(s, 0), v)
                 for s2, v2 in imp.items():
                     kn[s2] = max(kn.get(s2, 0), v2)
-        x = [_ap(T, r) for r in a] if k != "mm" else None
+        x = [_ap(T, r) for r in a] if k in ("send", "dma") else None
         if k == "send":
             dst = T.cores[(rank + a[3]) % nr]
             rid, pid, _ = topo.addr(dst)
@@ -919,41 +1105,17 @@ def rank_program(g, core, T, topo):
         if k == "dma":
             s = "d%d" % ndma[0]
             ndma[0] += 1
-            q.dma_start(x[0], x[1]).then_inc(T.sem[s], 16)
+            (q.dma_start(x[0], x[1], accum_op=ALU.add) if o["acc"] else q.dma_start(x[0], x[1])).then_inc(T.sem[s], 16)
             done[i] = (s, 16, dict(kn))
             final[s] = 16
             continue
-        if k == "copy":
-            ins = q.tensor_copy(x[0], x[1])
-        elif k == "tt":
-            ins = q.tensor_tensor(x[0], x[1], x[2], x[3])
-        elif k == "ts":
-            ins = q.tensor_scalar(x[0], x[1], x[2], None, x[4]) if x[5] is None else q.tensor_scalar(x[0], x[1], x[2], x[3], x[4], x[5])
-        elif k == "scan":
-            ins = q.tensor_tensor_scan(x[0], x[1], x[2], x[3], x[4], x[5])
-        elif k == "tr":
-            ins = q.transpose(x[0], x[1])
-        elif k == "ms":
-            ins = q.memset(x[0], x[1])
-        elif k == "red":
-            ins = q.tensor_reduce(x[0], x[1], AxisListType.X, ALU.add)
-        elif k == "act":
-            ins = q.activation(x[0], x[1], x[2], bias=x[3], scale=x[4])
-        elif k == "iota":
-            if _dtype(a[0]["n"]) == I4:
-                ins = q.iota(x[0], x[1], x[2], x[3])
-            else:
-                ins = q.iota(x[0], x[1], x[2], x[3], allow_small_or_imprecise_dtypes=True)
-        elif k == "asel":
-            ins = q.affine_select(x[0], x[1], x[2], x[3], x[4], x[5], x[6])
-        else:
-            for z, (po, lt, rh, st, sp) in enumerate(a):
-                ins = q.matmul(_ap(T, po), _ap(T, lt), _ap(T, rh), st, closes[o["group"]] == i and z == len(a) - 1)
-        cnt[e] += 1
-        ins.then_inc(T.sem[CNT[e]], 1)
+        for k, a in (a if k == "many" else [(k, a)]):
+            issue(q, k, a, closes.get(o.get("group")) == i).then_inc(T.sem[CNT[e]], 1)
+            cnt[e] += 1
         imp = dict(kn)
         imp[CNT[e]] = cnt[e]
         done[i] = (CNT[e], cnt[e], imp)
         final[CNT[e]] = cnt[e]
     for s, v in final.items():
-        g.sync.wait_ge(T.sem[s], v)
+        if seen.get(s, 0) < v:
+            g.sync.wait_ge(T.sem[s], v)

import numpy as np
from concourse.bass import DstId, RemoteDMATransfer
from concourse.mybir import dt, AluOpType, AxisListType, ActivationFunctionType

T0, L, RO, KILL = 1536, 256, 5, 200
TILE = [0, 1, 2, 1, 2]
HOPS = [1, 1, 1, 1]
GB, W = T0 + L * RO, T0 + L * (2 * RO - 1)
NONE = GB - 1
EPS = 2.0 ** -15
DU, TIE, BIG = 16384.0, 4096.0, 2.0 ** 24
ALU = AluOpType
ACT = ActivationFunctionType

B, F4, I4, U2 = "bfloat16", "float32", "int32", "uint16"


def _s(shape, d):
    return ("sbuf", [128] + list(shape), d)


CUBE = [4096]
NARROW = (("Pm", "dd", "apf", "t1", "t2", "Y1", "dumW", "nz0", "nz1", "nz2"), ("Ri", "ai", "pI", "pJ"),
          ("a16", "o16", "oR", "oT", "oB", "oP0", "oP1", "oP2"))
AT = {n: (b, 16 * i) for b, ns in zip(("nf4", "ni4", "nu2"), NARROW) for i, n in enumerate(ns)}
SCRATCH = {
    "V": _s([W], B), "F": _s([W], B), "T2": _s([W + L], F4), "Q": _s([W], I4),
    "Z": _s([1024], B), "VB": _s([1024], F4), "VBt": _s([1024], B), "ZE": _s([512], B), "MB": _s([128], B),
    "SN": _s([1024], I4), "KI": _s([2, 96], I4), "KJ": _s([2, 96], I4), "KK": _s([2, 96], I4), "KL": _s([2, 96], B), "KH": _s([2, 96], B),
    "DI": _s([128], I4), "DJ": _s([256], I4), "DL": _s([256], B), "DF": _s([256], F4),
    "BI": _s([64], I4), "B64": _s([64], F4), "Bo": _s([4, 16], F4), "B16": _s([64], U2),
    "XB": _s([4, 2, 16], F4), "XBT": _s([128], F4), "YB": _s([2, 16], F4), "YBT": _s([32], F4),
    "X2": _s([8, 2, 16], F4), "XT": _s([256], F4), "YS": _s([512], F4), "Yt": _s([128], F4), "Yc": _s([8, 16], F4),
    "YL": _s([240], F4), "YH": _s([240], F4), "YI": _s([240], I4), "YK": _s([240], F4),
    "zr0": _s(CUBE, B), "zr1": _s(CUBE, B), "zr2": _s(CUBE, B), "ZT": _s([16, 16, 16], B), "Z4": _s([16, 16, 4], B),
    "Zp": _s([L], B), "Pp": _s([L], F4),
    "S0": _s([L], U2), "S1": _s([L], U2), "S2": _s([L], U2), "Ps": _s([L], F4), "Pf": _s([L], F4), "K1": _s([L], I4), "K2": _s([L], I4),
    "G2": _s(CUBE, B), "DA": _s(CUBE, B), "DS": _s(CUBE, B), "DB": _s(CUBE, B),
    "DC": _s(CUBE, B), "AC": _s([8, 512], B), "U": _s([8, 2 * L], B), "vr": _s(CUBE, B), "GR": _s(CUBE, B),
    "E": _s([16, 128], B), "k16": _s([96], U2), "CV": _s([W + L], B), "tn": _s([L], F4), "q16": _s([L], U2), "ar16": _s([L], U2), "fl": _s([L], B),
    "P1": _s([L], F4), "Pi": _s([L], I4), "ids": _s([L], I4), "Pmb": _s([L], F4),
    "sc": _s([544], F4), "sc3": _s([L], F4), "th": _s([48], F4), "near": _s([18], F4), "oW": _s([18], U2),
    "FF": _s([576], B), "lo": _s([L], B), "hi": _s([L], B), "cnt": _s([L], B), "nf": _s([L], B),
    "nf4": _s([16 * len(NARROW[0])], F4), "ni4": _s([16 * len(NARROW[1])], I4), "nu2": _s([16 * len(NARROW[2])], U2),
    "sgn": _s([L + 16], B), "IDH": _s([128], B), "NIDH": _s([128], B),
    "va": _s([L], B), "nFa": _s([L], B), "tk": _s([L], B), "lv": _s([16], B), "dg": _s([16, 16], B), "att": _s([L], B),
    "A1": _s([L], F4), "wx": _s([2, L], B),
    "pc": _s([16], F4), "XI": _s([148], F4), "XR": _s([144], F4), "CG": _s([128], F4),
    "SEL": _s([7, 144], B), "BO": _s([128], B), "ID": _s([128], B), "NID": _s([128], B),
    "IDB": _s([128], B), "NIDB": _s([128], B), "QN": _s([128], B), "MAP": _s([128], B), "QC": _s([128], B), "ID4": _s([128], F4),
    "EXP": _s([16, 128], B), "tri": _s([L], B), "DW": _s([128], B), "seg": _s([L], B), "big": _s([L], B), "stp": _s([L], B),
    "cm32": _s([L], B), "one": _s([L], B), "oI": _s([3, 16], I4), "wr": _s([2, 16], F4),
}
SCRATCH.update({"p%d" % i: ("psum", [128, 512], F4) for i in range(8)})
IO = {"vn": ([128, T0], B), "zs": ([128, 1024], B), "sn": ([128, 1024], I4), "nq": ([128, T0], I4), "kid": ([8, T0], I4),
      "bst": ([8, 1024], I4), "yv": ([128, L * RO], B), "ys": ([128, 512], F4), "yk": ([8, W], F4), "yb": ([8, 1024], F4)}
NDMA = 90
SEMAPHORES = ["cv", "ca", "cp", "cg", "snt"] + ["d%d" % i for i in range(NDMA)] + ["av%d" % i for i in range(4)] + ["aq%d" % i for i in range(4)]
CNT = {"v": "cv", "a": "ca", "p": "cp", "g": "cg"}
S_ = slice
ALL = slice(None)
HALVES = (1, 0)
TUNE = {"bpos": [(), (), (), (), ()], "gpos": [(), (), (), (), ()], "sact": [(0, 1, 2, 3, 5, 7)] * 5,
        "vr": ["vvvvvvvvvvaagggg", "gggggggggggggggg"], "cv0": "aavaav", "zq": ["ppff"] * 5, "fvd": [0, 0, 0], "t2g": 0, "fva": [(3,), (), ()],
        "late": (0, 3), "z0": (7, 5), "keep": 0, "open": 0, "vrw": 12, "cut": ()}
LATE = ([("g", n) for n in ("DW", "FF", "zr1")] +
        [("v", n) for n in ("B64", "YK", "Bo", "S1", "S2", "Yt", "YS", "XBT", "B16")] +
        [("a", n) for n in ("tri", "big", "stp", "cm32", "IDH", "NIDH", "NIDB", "IDB", "XB", "VBt")])
NOM = {"f": 1.1, "ga": 1.4, "sca": 3.5, "pe": 0.42, "ov": 50.0, "lat": 200.0, "lat0": 200.0, "dma": 2000.0, "rem": 3000.0, "snd": 1500.0, "snd1": 3000.0,
       "gx": 50.0, "dh": 100.0, "po": 0.0, "gd": 1000.0, "gd1": 2000.0, "holds": (0.3, 0.7, 1.0), "spans": (240, 160, 240, 160), "heat": 250.0, "flip": 0.08, "seed": 11, "moves": 600000,
       "also": ({"f": 1.0, "ga": 1.45, "lat": 200.0, "lat0": 200.0, "dma": 1500.0},
                {"f": 1.15, "ga": 1.8, "sca": 2.5, "lat": 280.0, "lat0": 280.0, "snd": 2000.0, "gx": 100.0},
                {"f": 1.45, "ga": 1.2, "pe": 0.5, "sca": 5.0, "rem": 4000.0, "dma": 3000.0, "snd": 2500.0, "snd1": 6000.0, "gx": 100.0, "dh": 300.0,
                 "gd": 1800.0, "gd1": 5000.0})}


def _shape(n):
    return SCRATCH[n][1] if n in SCRATCH else IO[n][0]


def _dtype(n):
    return SCRATCH[n][2] if n in SCRATCH else IO[n][1]


def _where(n):
    return SCRATCH[n][0] if n in SCRATCH else "dram"


def R(n, *ix):
    if n in AT:
        a, b = ix[0].indices(16)[:2] if ix else (0, 16)
        n, ix = AT[n][0], (S_(AT[n][1] + a, AT[n][1] + b),)
    return {"n": n, "p": ALL, "ix": ix, "off": None}


def RP(n, p, *ix):
    return {"n": n, "p": p, "ix": ix, "off": None}


def IND(win, off):
    return {"n": win["n"], "p": ALL, "ix": win["ix"], "off": off}


_FOOT = {}


def _foot(r):
    key = (r["n"], repr(r["p"]), repr(r["ix"]))
    if key not in _FOOT:
        sh = _shape(r["n"])
        m = np.zeros(sh[1:], dtype=bool)
        m[tuple(r["ix"])] = True
        pm = np.zeros(sh[0], dtype=bool)
        pm[r["p"]] = True
        fb = int.from_bytes(np.packbits(m.reshape(-1), bitorder="little").tobytes(), "little")
        pb = int.from_bytes(np.packbits(pm, bitorder="little").tobytes(), "little")
        _FOOT[key] = (fb, pb, int(m.sum()), int(pm.sum()))
    return _FOOT[key]


def _count(r):
    return 16 * _foot(r["off"])[2] if r["off"] is not None else _foot(r)[2]


def _ap(T, r):
    if not isinstance(r, dict):
        return r
    a = T[r["n"]][(r["p"],) + tuple(r["ix"])]
    return a.indirect(_ap(T, r["off"])) if r["off"] is not None else a


def build_ops(tune):
    ops = []
    group = {}

    def add(eng, kind, args, reads, writes, **kw):
        rd = [r for r in reads if isinstance(r, dict)]
        rd += [r["off"] for r in rd + list(writes) if r["off"] is not None]
        o = {"eng": eng, "kind": kind, "args": args, "rd": rd, "wr": list(writes), "id": len(ops)}
        o.update(kw)
        ops.append(o)
        return o

    real = lambda *x: all(_dtype(r["n"]) in (B, F4) for r in x if isinstance(r, dict))

    def either(eng, alt, reads, out):
        return add(eng, alt[eng][0], alt[eng][1], reads, [out], **({"alt": alt} if len(alt) > 1 else {}))

    def cp(out, a, eng="v"):
        alt = {"v": ("copy", (out, a))}
        if real(out, a) and out["off"] is None:
            alt["a"] = ("act", (out, a, ACT.Copy, 0.0, 1.0))
            if a["off"] is None and _where(a["n"]) == "sbuf" and _where(out["n"]) == "sbuf":
                alt["g"] = ("asel", (out, a, [[0, _count(out)]], ALU.is_ge, 0.0, 0, 0))
        return either(eng, alt, [a], out)

    def lin(out, a, bias, scale=1.0, eng="a", floor=False):
        alt = {"a": ("act", (out, a, ACT.Relu if floor else ACT.Identity, bias, scale))}
        if not floor:
            alt["v"] = ("ts", (out, a, scale, bias, ALU.mult, ALU.add))
        elif scale == 1.0:
            alt["v"] = ("ts", (out, a, bias, 0.0, ALU.add, ALU.max))
        return either(eng, alt, [a, bias, scale], out)

    def bunch(n):
        part = ops[-n:]
        del ops[-n:]
        alts = [o.get("alt", {o["eng"]: (o["kind"], o["args"])}) for o in part]
        alt = {e: ("many", [x[e] for x in alts]) for e in alts[0] if all(e in x for x in alts)}
        o = either(part[0]["eng"], alt, [], part[0]["wr"][0])
        o["rd"], o["wr"] = [r for x in part for r in x["rd"]], [r for x in part for r in x["wr"]]
        return o

    def tt(out, a, b, op):
        return add("v", "tt", (out, a, b, op), [a, b], [out])

    def ts(out, a, s1, op0, s2=None, op1=None):
        return add("v", "ts", (out, a, s1, s2, op0, op1), [a, s1, s2], [out])

    def scan(out, d0, d1, init, op0, op1):
        return add("v", "scan", (out, d0, d1, init, op0, op1), [d0, d1], [out])

    def tr(out, a):
        return add("v", "tr", (out, a), [a], [out])

    def ms(out, c):
        return add("v", "ms", (out, c), [], [out])

    def act(out, a, fn, bias=0.0, scale=1.0):
        return add("a", "act", (out, a, fn, bias, scale), [a, bias, scale], [out])

    def mm(lst, more=False):
        bank = lst[0][0]["n"]
        if lst[0][3]:
            group[bank] = len(ops)
        return add("p", "mm", lst, [x for m in lst for x in m[1:3]], [m[0] for m in lst], group=group[bank])

    def iota(out, pat, base, cm):
        return add("g", "iota", (out, pat, base, cm), [], [out])

    def asel(out, a, pat, op, fill, base, cm):
        return add("g", "asel", (out, a, pat, op, fill, base, cm), [a], [out])

    def dma(out, a, eng="s", acc=False):
        return add(eng, "dma", (out, a), [a] + [out] * acc, [out], acc=acc)

    def send(name, t, c0, sem):
        land = R(name, S_(GB + L * t, GB + L * t + L))
        add("g", "send", (land, R(name, S_(c0, c0 + L)), sem, HOPS[t]), [R(name, S_(c0, c0 + L))], [])
        add(None, "recv", sem, [], [land], after=len(ops) - 1)

    def dpass(ps, src, c, sel, mid=False, more=False, at=None):
        if mid:
            return mm([(R(ps, S_(128 * (m // 16), 128 * (m // 16) + 128)), R("SEL", sel, S_(15 - m % 16, 143 - m % 16)), R(src, S_(128 * m, 128 * m + 128)), False, False)
                       for m in range(8 * c, 8 * c + 8)], more)
        at = 64 * c if at is None else at
        return mm([(R(ps, S_(at, at + 64)), R("SEL", sel, S_(15 - m, 143 - m)), R(src, S_(1024 * c + m, 1024 * c + 1024, 16)), False, False)
                   for m in range(16)], more)

    ch = lambda n, c: R(n, S_(1024 * c, 1024 * c + 1024))
    oc = lambda n, c: R(n, S_(64 * c, 64 * c + 64))
    zc = lambda t, a, b: R("zr%d" % (t % 3), S_(a, b))
    ONES, KID, OWN, TWO, NEG, NEG1, OWN2 = range(7)

    for out, n in ((R("KI", 0), "kid"), (R("Z"), "zs"), (R("V", S_(0, T0)), "vn"), (R("SN"), "sn"), (R("BI"), "bst")):
        dma(out, R(n))["lead"] = 1
    pc = lambda i: R("pc", S_(i, i + 1))
    iota(R("pI"), [[0, 16]], 0, 1)
    iota(R("XI"), [[1, 148]], -4, 0)
    iota(R("oI", 0), [[32, 16]], 0, 0); iota(R("oI", 1), [[1, 16]], 0, 0)
    iota(R("CG"), [[16, 8], [0, 16]], 0, 0)
    iota(RP("DI", S_(0, 32)), [[1, 128]], 0, 128)
    ts(R("oI", 2, S_(0, 1)), R("pI", S_(0, 1)), 112, ALU.bitwise_and)
    ts(R("oI", 2, S_(1, 2)), R("pI", S_(0, 1)), 15, ALU.bitwise_and)
    ts(R("oI", 2, S_(2, 3)), R("pI", S_(0, 1)), 12, ALU.bitwise_and, 2, ALU.arith_shift_right)
    cp(R("pc", S_(0, 3)), R("oI", 2, S_(0, 3)))
    ts(R("XR"), R("XI", S_(0, 144)), pc(0), ALU.subtract)
    ts(R("QN"), R("XR", S_(0, 128)), pc(2), ALU.is_equal, 32.0, ALU.mult)
    act(pc(4), pc(1), ACT.Silu, 0.0, 96.0)["once"] = 1300.0
    ts(R("KI", 1), R("XI", S_(4, 100)), pc(4), ALU.add)
    ts(R("KJ"), R("KI"), 63, ALU.bitwise_and); ts(R("KK"), R("KI"), 4032, ALU.bitwise_and)
    ts(R("KL"), R("KJ"), 32.0, ALU.mult); cp(R("KH"), R("KK"))
    for j, (n, b) in enumerate((("KL", 0), ("KH", 0), ("KL", 1), ("KH", 1))):
        dma(RP("GR", S_(j, 32, 4), S_(0, T0)), R(n, b), "sa"[j % 2])
    p32 = S_(0, 32)
    iota(R("one"), [[0, L]], 1, 0)
    asel(RP("MAP", p32), RP("one", p32, S_(0, 128)), [[-4, 8], [-1, 16]], ALU.is_equal, 0.0, 0, 1)
    asel(RP("MAP", p32), RP("MAP", p32), [[0, 8], [-1, 16]], ALU.is_ge, 0.0, 3, 0)
    ts(R("pJ"), R("pI"), 31, ALU.bitwise_and)
    tt(R("pJ"), R("pJ"), R("oI", 0), ALU.add)
    cp(R("oT"), R("pJ")); cp(R("oB"), R("oI", 1))
    for b in range(2):
        cp(R("X2", S_(0, 6), b, ALL), R("KI", 0))
    bunch(2)
    tr(R("XT", S_(0, 192)), R("X2", S_(0, 6)))
    for u in range(6):
        cp(R("k16", S_(u, 96, 6)), IND(R("XT", S_(32 * u, 32 * u + 32)), R("oT", S_(0, 1))))
    bunch(6)
    lin(pc(3), pc(2), 4.0)
    ts(R("QC"), R("XR", S_(0, 128)), pc(3), ALU.is_equal, 32.0, ALU.mult)
    for h, bank in enumerate(("p0", "p1", "p6")):
        x = S_(512 * h, 512 * h + 512)
        cp(R("CV", x), IND(R("V", S_(0, T0)), R("k16", S_(32 * h, 32 * h + 32))), tune["cv0"][h])
        mm([(R(bank), R("QN"), R("V", x), True, False)])
        mm([(R(bank), RP("MAP", p32), RP("GR", p32, x), False, False)])
        mm([(R(bank), R("QC"), R("CV", x), False, False)])
        cp(R("T2", x), R(bank), tune["cv0"][3 + h])
    ms(R("CV", S_(T0, T0 + 288)), 255.0)
    for n in (288, 576, 1152):
        dma(R("CV", S_(T0 + n, T0 + 2 * n)), R("CV", S_(T0, T0 + n)))
    ts(pc(7), pc(1), 2.0, ALU.is_ge)
    ts(pc(5), pc(1), 8.0, ALU.is_lt, pc(7), ALU.mult)
    ts(R("SEL", ONES), R("XR"), 11.0, ALU.is_equal)
    iota(R("wr", 0), [[1, 16]], 0, 0)
    ts(R("wr", 1), R("wr", 0), pc(1), ALU.is_equal)
    wcol = lambda j: R("wr", 1, S_(j, j + 1))
    for j, d, q, w in ((KID, 0, 2, -DU / 32), (OWN, 2, 1, -DU / 32), (OWN2, 2, 1, DU / 32)):
        if j != OWN2 or any(tune["fva"]):
            ts(pc(8 + j % 3), pc(2), float(q), ALU.is_equal, w, ALU.mult)
            lin(pc(8 + j % 3), wcol(d), pc(8 + j % 3), 1.0 / 32)
            lin(pc(8 + j % 3), wcol(d + 1), pc(8 + j % 3))
            lin(R("SEL", j), R("SEL", ONES), 0.0, pc(8 + j % 3))
    lin(pc(11), wcol(0), EPS, -EPS * 31 / 32)
    lin(pc(12), pc(11), 0.0, -1.0)
    for j, w in ((TWO, 2 * DU), (NEG, -DU), (NEG1, -1.0)):
        lin(R("SEL", j), R("SEL", ONES), 0.0, w)
    ts(R("BO"), R("CG"), pc(0), ALU.is_equal)
    iota(R("FF", S_(15, 576, 288)), [[0, 2]], 1, 0)
    iota(R("near"), [[-16383, 2], [0, 9]], 8192, 0)
    for hf in HALVES:
        iota(R("sc", S_(272 * hf + 128, 272 * hf + 144)), [[0, 16]], 0, 0)
    cp(R("oW"), R("XI", S_(4, 22)))
    lin(R("cm32"), R("one"), 0.0, -1.0 / 32)
    asel(R("ID"), R("one", S_(0, 128)), [[-1, 128]], ALU.is_equal, 0.0, 0, 1)
    for n, w in (("ID4", 1.0), ("NID", -1.0), ("IDB", BIG), ("NIDB", -BIG), ("IDH", DU / 2), ("NIDH", -DU / 2)):
        lin(R(n), R("ID"), 0.0, w)
    asel(R("DW"), R("BO"), [[1, 128]], ALU.is_gt, 0.0, 0, -1)
    ts(R("oR"), R("wr", 0), 0.0, ALU.mult, pc(1), ALU.add)
    lin(R("tri"), IND(R("wr", 1), R("oR")), 0.0, 4096.0)
    K16 = [[0, 16], [1, 16]]
    asel(R("seg"), R("one"), K16, ALU.is_gt, 0.0, 0, 0)
    lin(R("big"), R("seg"), 2 * BIG, -2 * BIG)
    lin(R("stp"), R("seg"), 4 * BIG, -4 * BIG - DU)
    lin(R("dumW"), R("XI", S_(4, 20)), pc(1), 16.0)
    lin(R("dumW"), R("dumW"), float(W))
    ms(R("ZE"), 0.0)
    dma(RP("F", S_(2, 16), S_(0, W)), RP("ZE", S_(0, 112), S_(0, 480)))
    ms(RP("F", p32, S_(NONE, NONE + 1)), 200.0 / EPS)
    h0, h1 = S_(0, 128), S_(128, 256)
    ts(RP("DJ", p32, h0), RP("DI", p32), 63, ALU.bitwise_and); ts(RP("DJ", p32, h1), RP("DI", p32), 4032, ALU.bitwise_and)
    ts(RP("DL", p32, h0), RP("DJ", p32, h0), 32.0, ALU.mult); cp(RP("DL", p32, h1), RP("DJ", p32, h1))
    dma(RP("F", S_(0, 1), S_(0, W)), RP("DL", S_(0, W // 128), h0)); dma(RP("F", S_(1, 2), S_(0, W)), RP("DL", S_(0, W // 128), h1))
    for a, b in ((16, 32), (32, 48), (48, 64), (64, 128)):
        dma(RP("F", S_(a, b)), RP("F", S_(0, b - a)))
    if tune["t2g"]:
        dma(R("T2", S_(T0, W)), R("F", S_(T0, W)), "g")["once"] = 1
    else:
        add("v", "copy", (RP("DF", p32), RP("DL", p32)), [RP("DL", p32)], [RP("DF", p32)])
        for a in (2, 9):
            dma(RP("T2", S_(a, a + 7), S_(T0, W)), RP("XI", S_(0, 126), S_(0, 128)))
        for j, h in enumerate((h0, h1)):
            dma(RP("T2", S_(j, j + 1), S_(T0, W)), RP("DF", S_(T0 // 128, W // 128), h))
        for a in (16, 32, 64):
            dma(RP("T2", S_(a, 2 * a), S_(T0, W)), RP("T2", S_(0, a), S_(T0, W)))

    def scat(hf):
        out, x = IND(R("T2"), R("o16", S_(8 * hf, 8 * hf + 8))), half("tn", hf)
        either("a", {"a": ("act", (out, x, ACT.Silu, 0.0, 1.0)), "v": ("copy", (out, x))}, [x], out)

    def ys_rows(tau):
        ts(R("Yt"), R("ids", S_(128, 256)), 4096.0, ALU.mult)
        tt(R("Yc"), R("Yt"), R("ids", S_(0, 128)), ALU.add)
        for b in range(2):
            cp(R("X2", ALL, b, ALL), R("Yc"), "g")
        bunch(2)
        tr(R("XT"), R("X2"))
        cp(R("YS", S_(tau, 512, 4)), IND(R("XT"), R("oT", S_(0, 8))), "a")

    def yb_rows(tau):
        lin(R("Y1"), R("lv", S_(0, 16)), -2048.0, 2048.0)
        tt(R("Y1"), R("Y1"), R("ai"), ALU.add)
        for b in range(2):
            ts(R("YB", b), R("Y1"), -1.0, ALU.max)
        bunch(2)
        tr(R("YBT"), R("YB"))
        cp(R("B64", S_(tau, 64, 4)), IND(R("YBT"), R("oT", S_(0, 1))), "a")

    def zrep(t):
        if t < 3:
            cp(R("Zp"), IND(R("Z"), R("oP%d" % t)), "a")
            mm([(R("p3", S_(L + 8 * (m // 16), L + 8 * (m // 16) + 8)), R("SEL", NEG, S_(15 - m % 16, 143 - m % 16)), R("Zp", S_(8 * m, 8 * m + 8)), m == 0, False)
                for m in range(32)])
            cp(R("nz%d" % t), R("p3", S_(L, L + 16)), "a")
        for k in range(16):
            nv, na = tune["z0"] if t == 0 else (0, 0)
            if t < 3:
                cp(R("zr%d" % t, S_(k, 4096, 16)), R("Zp"), "v" if k < nv else "a" if k < nv + na else "g")
            else:
                cp(R("ZT", ALL, k, ALL), R("Z4", ALL, ALL, TILE[t]), "g")
            if k % 2 and t:
                bunch(2)
        if t >= 3:
            dma(R("zr%d" % (t - 3)), R("ZT"))

    def sizes(dif, out, c, ps, pos):
        less = dpass(ps, dif, c, NEG1)
        o = either("v" if pos else "a", {"a": ("act", (ch(out, c), ch(dif, c), ACT.Abs, 0.0, 1.0)),
                                         "v": ("ts", (ch(out, c), ch(dif, c), 0.0, 2.0, ALU.max, ALU.mult))}, [ch(dif, c)], ch(out, c))
        o["link"], less["only"] = less["id"], o["id"]
        return dpass(ps, out, c, ONES)

    pbank = lambda hf: "p2" if hf == HALVES[0] else "p6"
    half = lambda n, hf, at=0: R(n, S_(at + 128 * hf, at + 128 * hf + 128))

    obank = lambda hf: "p5" if hf == HALVES[0] else "p4"
    whole = {}

    def first_dist(t):
        fb = lambda c: obank(c // 2) if t == 0 else "p5"
        for hf in HALVES:
            mm([(half(fb(2 * hf), hf), R("ID4"), half("Pp", hf), t == 0 or hf == HALVES[0], False)])
        for c in (2, 3, 0, 1):
            if c in tune["fva"][t]:
                if tune["fvd"][t]:
                    lin(ch("GR", c), IND(R("V", S_(0, T0)), oc("S%d" % t, c)), 0.0, -1.0)
                    dma(ch("GR", c), zc(t, 1024 * c, 1024 * c + 1024), "g", True)
                    lin(ch("DS", c), ch("GR", c), 0.0, 1.0, "v", True)
                else:
                    cp(ch("GR", c), IND(R("V", S_(0, T0)), oc("S%d" % t, c)), "a")
                for b, bank in enumerate(() if tune["fvd"][t] else ("p6", "p7")):
                    x = S_(1024 * c + 512 * b, 1024 * c + 512 * b + 512)
                    mm([(R(bank), R("ID"), zc(t, x.start, x.stop), True, False), (R(bank), R("NID"), R("GR", x), False, False)])
                    lin(R("DS", x), R(bank), 0.0, 1.0, "a", True)
            else:
                tt(ch("DS", c), IND(R("V", S_(0, T0)), oc("S%d" % t, c)), zc(t, 1024 * c, 1024 * c + 1024), ALU.max)
            whole[c] = dpass(fb(c), "DS", c, TWO, True)["id"]
        if t:
            cp(R("Pf"), R("p5", S_(0, L)), "a")

    def offspring(t, hf):
        top = T0 if t < 3 else W
        mm([(half(pbank(hf), hf), R("ID4"), half("Pp", hf), True, False)])
        if t in (1, 2):
            mm([(half(obank(hf), hf), R("ID4"), half("Pf", hf), True, False)])
        for c in (2 * hf, 2 * hf + 1):
            at = oc("S%d" % TILE[t], c)
            cut = tune["cut"] if c == 2 * HALVES[1] + 1 else ()
            for a, b in zip((0,) + cut, cut + (64,)):
                cp(R("G2", S_(1024 * c + 16 * a, 1024 * c + 16 * b)), IND(R("T2", S_(0, top)), R("S%d" % TILE[t], S_(64 * c + a, 64 * c + b))), "v" if a else "a")
            gate = tt(ch("DA", c), IND(R("CV", S_(0, top)), at), zc(t, 1024 * c, 1024 * c + 1024), ALU.max)["id"]
            o = dpass(pbank(hf), "DA", c, TWO, t < 3)
            dpass(pbank(hf), "G2", c, KID, t < 3)["after"] = o["id"]
            if t < 3:
                dpass(obank(hf), "G2", c, OWN2 if c in tune["fva"][t] else OWN, True)["after"] = whole[c]
        if t < 3:
            lin(half("Ps", hf), half(obank(hf), hf), -TIE)
        return gate

    def books(t):
        tau = TILE[t]
        if t == 0:
            cp(R("Pi"), R("P1"))
        ts(R("ids"), R("Pi"), 4095, ALU.bitwise_and)
        if tau in TILE[t + 1:]:
            cp(R("S%d" % tau), R("ids"))
            ts(R("K%d" % tau), R("Pi"), -12289, ALU.bitwise_and)
        else:
            ys_rows(tau)
            yb_rows(tau)

    ts(pc(7), pc(1), 8.0, ALU.is_ge, -508.0, ALU.mult)
    lin(pc(6), pc(1), pc(7), 64.0)
    iota(R("t2"), [[512, 2], [8, 8]], 0, 0)
    lin(R("t1"), R("t2"), pc(6))
    for t in range(3):
        ts(R("oP%d" % t), R("t1"), float(t), ALU.add)
    zrep(0)
    late = len(ops) - 1
    dma(R("Z4"), R("zs"))["after"] = late
    dma(R("Q", S_(0, T0)), R("nq"))["after"] = late
    dma(R("V", S_(T0, GB)), R("V", S_(0, GB - T0)))["after"] = late
    dma(R("Q", S_(T0, GB)), R("Q", S_(0, GB - T0)))
    lin(R("Pp"), IND(R("nz0"), R("oB")), TIE)
    cp(R("S0"), IND(R("SN"), R("oP0")))
    first_dist(0)
    cp(R("B64"), R("BI"))
    ts(R("YK", S_(0, 64)), R("B64"), 0.0, ALU.is_lt, float(NONE + 1), ALU.mult)
    tt(R("Bo"), R("YK", S_(0, 64)), R("B64"), ALU.add)
    for b in range(2):
        cp(R("XB", ALL, b, ALL), R("Bo"), "a")
    bunch(2)
    tr(R("XBT"), R("XB"))
    for h in range(4):
        cp(R("B16", S_(h, 64, 4)), IND(R("XBT", S_(32 * h, 32 * h + 32)), R("oT", S_(0, 1))))
    bunch(4)
    lin(R("VBt"), IND(R("F"), R("B16")), 0.0, pc(11))
    tt(R("VB"), IND(R("V", S_(0, GB)), R("B16")), R("VBt"), ALU.add)
    lin(R("MB"), R("BO"), 0.0, -128.0)
    dma(R("EXP", S_(0, 4)), R("ZE")); dma(R("EXP", S_(4, 8)), R("ZE")); dma(R("EXP", S_(8, 16)), R("EXP", S_(0, 8)))
    for k in range(16):
        dma(RP("EXP", S_(k, 128, 16), k), RP("MB", S_(k, 128, 16)))
    zrep(1)
    ts(R("Yt"), R("SN", S_(515, 1024, 4)), 4096.0, ALU.mult)
    tt(R("YS", S_(3, 512, 4)), R("Yt"), R("SN", S_(3, 512, 4)), ALU.add)

    cp(R("S1"), IND(R("SN"), R("oP1"))); cp(R("S2"), IND(R("SN"), R("oP2")))
    start = len(ops)
    for t in range(RO):
        tau = TILE[t]
        n0 = T0 + L * t
        top = T0 if t == 0 else GB + L * t
        old = "Ps" if t < 3 else "K%d" % tau
        gate = offspring(t, HALVES[0])
        offspring(t, HALVES[1])
        if t > 0:
            at = len(ops)
            books(t - 1)
            for o in ops[at:]:
                if o["eng"] == "v":
                    o["after"] = gate
            gv = R("V", S_(GB + L * (t - 1), GB + L * t))
            gd = R("p3", S_(0, 16))
            mm([(R("p3", S_(0, L)), R("ID"), gv, True, False), (R("p3", S_(0, L)), R("NID"), R("Z", S_(tau, 1024, 4)), False, True)])
            act(R("dg"), R("p3", S_(0, L)), ACT.Abs, 0.0, DU)
            mm([(gd, R("ID4"), R("dumW"), True, False)])
            mm([(gd, R("SEL", ONES, S_(15 - m, 143 - m)), R("dg", ALL, m), False, False) for m in range(16)])
            lin(R("Pm"), gd, GB + L * (t - 1) - W + TIE)
            act(R("sgn", S_(L, L + 16)), R("Pm"), ACT.Sign, 0.5 - KILL * DU)
            lin(R("Pmb"), IND(R("Pm"), R("oB")), TIE)
        for hf in HALVES:
            u0, u1, w0, w1 = 128 * hf, 128 * hf + 128, 8 * hf, 8 * hf + 8
            A = lambda n, at=0: half(n, hf, at)
            Bn = lambda n: R(n, S_(w0, w1))
            sc = lambda j: R("sc", S_(272 * hf + 144 * j, 272 * hf + 144 * j + 128))
            FF = lambda j, at: R("FF", S_(288 * hf + 144 * j + at, 288 * hf + 144 * j + at + 128))
            th = lambda n: R("th", S_(24 * hf, 24 * hf + n))
            pb, yb = pbank(hf), "p3" if hf == HALVES[0] else "p4"
            tt(A("P1"), A(pb), A(old), ALU.min)
            mm([(A(pb), R("ID4"), A("P1"), True, False)])
            scan(sc(0), A("big"), A("P1"), 0.0, ALU.add, ALU.min)
            if t == 0:
                lin(th(8), R("sc", S_(272 * hf + 15, 272 * hf + 128, 16)), DU / 2, 1.0, "v")
                tt(A("nf"), IND(th(8), R("oB", S_(0, 8))), A("P1"), ALU.is_le)
                mm([(A(pb), R("IDB"), A("nf"), False, False)])
                scan(A("sc3"), A("stp"), A(pb), 0.0, ALU.add, ALU.min)
                cp(Bn("Ri"), R("sc3", S_(u0 + 15, u1, 16)))
            else:
                yp = R(yb, S_(L, L + 128))
                mm([(yp, R("ID4"), A("Pmb"), True, False)])
                scan(sc(1), A("seg"), A("P1"), 0.0, ALU.mult, ALU.max)
                tt(th(17), R("sc", S_(272 * hf + 15, 272 * hf + 272, 16)), R("near", S_(1, 18)), ALU.add)
                tt(R("FF", S_(288 * hf + 16, 288 * hf + 288)), IND(th(17), R("oW", S_(0, 17))), R("sc", S_(272 * hf, 272 * hf + 272)), ALU.is_gt)
                mm([(A(pb), R("NIDB"), FF(0, 16), False, False), (A(pb), R("IDB"), FF(0, 15), False, False),
                    (A(pb), R("IDB"), A("seg"), False, False), (A(pb), R("NIDH"), FF(1, 15), False, False), (A(pb), R("IDH"), A("seg"), False, False)])
                mm([(yp, R("NIDB"), FF(1, 15), False, False), (yp, R("IDB"), FF(1, 16), False, False), (yp, R("IDB"), A("seg"), False, False)])
                tt(A("Pi"), yp, A("P1"), ALU.min)
                act(A("sgn"), A("P1"), ACT.Sign, 0.5 - KILL * DU)
                scan(A("sc3"), A("big"), A(pb), 0.0, ALU.add, ALU.min)
                tt(Bn("Ri"), R("sc3", S_(u0 + 15, u1, 16)), Bn("Pm"), ALU.min)
            ts(Bn("ai"), Bn("Ri"), 4095, ALU.bitwise_and)
            cp(Bn("a16"), Bn("ai"))
            if t == 0:
                scan(sc(1), A("seg"), A("P1"), 0.0, ALU.mult, ALU.max)
                act(R("lv", S_(w0, w1)), R("sc", S_(272 * hf + 159, 272 * hf + 272, 16)), ACT.Sign, 0.5 - KILL * DU)
            cp(A("va"), IND(R("V", S_(0, top)), Bn("a16")), "a")
            cp(A("q16"), IND(R("Q", S_(0, top)), Bn("a16")))
        lin(R("nFa"), IND(R("F"), R("a16")), 0.0, pc(12))
        for k in range(16):
            if k < tune["vrw"]:
                cp(R("vr", S_(k, 4096, 16)), R("va"), tune["vr"][0][k])
            else:
                for x, hf in enumerate(HALVES):
                    cp(R("vr", S_(2048 * hf + k, 2048 * hf + 2048, 16)), half("va", hf), tune["vr"][x][k])
        if t > 0:
            far = R("p5", S_(L, L + 16))
            mm([(far, R("ID"), R("sgn", S_(L, L + 16)), True, False)] + [(far, R("ID"), R("sgn", S_(k, L, 16)), False, False) for k in range(16)])
            act(R("lv", S_(0, 16)), far, ACT.Sign, 14.0)
        vb = R("p5", S_(0, L))
        mm([(R("p5", S_(m, L, 16)), R("EXP", m), R("lv"), m == 0, False) for m in range(16)])
        for hf in HALVES:
            mm([(half("p5", hf), R("ID"), half("va", hf), False, False)])
        mm([(vb, R("NID"), R("nFa"), False, False)])
        lin(R("VB", S_(tau, 1024, 4)), vb, 128.0)
        if t < RO - 1:
            cp(R("Q", S_(n0, n0 + L)), R("q16"))
            send("Q", t, n0, "aq%d" % t)
        if t < 2:
            lin(R("tk"), IND(R("T2", S_(0, top)), R("a16")), 0.0, pc(5))
        if t < 3:
            zrep(t + 2)
        WW = R("p5", S_(0, L))
        mm([(R("p6", S_(L, 2 * L)), R("BO"), R("nFa"), True, True)])
        ts(R("ar16"), R("p6", S_(L, 2 * L)), -1.0 / EPS, ALU.mult)
        lin(R("dd"), R("lv"), 2048.0, -2048.0)
        tt(R("apf"), R("ai"), R("dd"), ALU.add)
        for h in range(16):
            e = 128 * (h // 8 + 1)
            ts(R("E", h, S_(0, e - 16 * h)), R("ar16", S_(16 * h, e)), R("apf", S_(h, h + 1)), ALU.is_equal)
            if h % 4 == 3:
                bunch(4)
        mm([(WW, R("DW"), R("E", ALL, S_(0, 16)), True, False)] +
           [(R("p5", S_(16 * h + 16, 128 * (h // 8 + 1))), R("BO"), R("E", h, S_(16, 128 - 16 * (h % 8))), False, False) for h in range(16) if h % 8 < 7])
        tt(R("fl"), WW, R("tri"), ALU.mult)
        scan(R("cnt"), R("seg"), R("fl"), 0.0, ALU.mult, ALU.max)
        tt(R("t2"), R("cnt", S_(15, L, 16)), R("apf"), ALU.max)
        tt(R("t1"), R("t2"), R("dumW"), ALU.min)
        cp(R("o16"), R("t1"))
        if t == RO - 1:
            cp(R("tn"), R("F", S_(n0, n0 + L)), "a")
            for hf in HALVES:
                scat(hf)
            books(t)
        else:
            lin(R("Pp"), IND(R("nz%d" % TILE[t + 1]), R("oB")), TIE)
        if t < 2:
            first_dist(t + 1)
        banks = ("p0", "p1", "p2", "p7")
        how = dict(zip([c for hf in HALVES for c in (2 * hf, 2 * hf + 1)], tune["zq"][t]))
        for x, hf in enumerate(HALVES):
            h = lambda n, *ix: R(n, *ix, S_(128 * hf, 128 * hf + 128))
            q4 = lambda n, j: R(n, S_(128 * j, 128 * j + 128))
            D1, D2 = h("p3"), h("p4")
            mm([(D2, R("BO"), h("cm32"), True, False)])
            mm([(D1, R("BO"), h("nFa"), True, False)])
            for c in (c for c in how if x == 0 and how[c] != "f"):
                lin(ch("DC", c), IND(R("Z"), oc("q16", c)), 0.0, -1.0 if how[c] == "d" else 1.0)
                if how[c] == "d":
                    dma(ch("DC", c), ch("vr", c), "g", True)
            for c in (2 * hf, 2 * hf + 1):
                tt(ch("DB", c), IND(R("VB"), oc("q16", c)), ch("vr", c), ALU.subtract)
                sizes("DB", "DA", c, "p3", 2 * x + c % 2 in tune["bpos"][t])
                if how[c] == "f":
                    tt(ch("DC", c), IND(R("Z"), oc("q16", c)), ch("vr", c), ALU.subtract)
                if how[c] != "p":
                    sizes("DC", "GR", c, "p4", 2 * x + c % 2 in tune["gpos"][t])
                for b in range(2 if how[c] == "p" else 0):
                    bank = banks[2 * (c % 2) + b]
                    mm([y for j in range(8) for y in ((oc(bank, j), R("ID"), R("DC", S_(1024 * c + 8 * b + j, 1024 * c + 1024, 16)), j == 0, False),
                                                      (oc(bank, j), R("NID"), oc("va", c), False, False))])
                    act(R("AC", 2 * c + b), R(bank), ACT.Abs)
                    mm([(oc("p4", c), R("SEL", ONES, S_(15 - 8 * b - j, 143 - 8 * b - j)), R("AC", 2 * c + b, S_(64 * j, 64 * j + 64)), False, False) for j in range(8)])
            runs = [(2 * hf, 2 * hf + 2)] if how[2 * hf] == how[2 * hf + 1] else [(2 * hf, 2 * hf + 1), (2 * hf + 1, 2 * hf + 2)]
            for b in range(4):
                lst = []
                for j in range(4):
                    for c0, c1 in runs:
                        out = R(banks[b], S_(128 * j + 64 * (c0 % 2), 128 * j + 64 * (c1 - 2 * hf)))
                        lst.append((out, R("NID" if how[c0] == "d" else "ID"), R("DC", S_(1024 * c0 + 4 * b + j, 1024 * c1, 16)), not lst, False))
                        if how[c0] == "p":
                            lst.append((out, R("NID"), R("va", S_(64 * c0, 64 * c1)), False, False))
                mm(lst)
            act(h("A1"), D1, ACT.Abs)
            either("a", {"a": ("act", (h("wx", 0), h("A1"), ACT.Relu, -8800.0, 8.0)),
                         "v": ("ts", (h("wx", 0), h("A1"), 1100.0, 8192.0, ALU.is_gt, ALU.mult))}, [h("A1")], h("wx", 0))
            either("a", {"a": ("act", (h("wx", 1), h("A1"), ACT.Relu, 2048.0, -2.0 ** 26)),
                         "v": ("ts", (h("wx", 1), h("A1"), 0.0, 2048.0, ALU.is_equal, ALU.mult))}, [h("A1")], h("wx", 1))
            mm([(D2, R("ID"), h("wx", 0), False, False), (D2, R("NID"), h("wx", 1), False, False)], True)
            tt(h("att"), D2, h("A1"), ALU.is_ge)
            H, X = q4("p6", 2 + hf), q4("p6", hf)
            mm([(H, R("ID"), h("va"), True, False)])
            mm([(H, R("BO"), h("att"), False, False)])
            for u in range(4):
                mm([(q4(banks[u], j), R("EXP", 4 * u + j), h("att"), False, False) for j in range(4)])
                sg = R("U", 4 * hf + u)
                either("a" if 4 * x + u in tune["sact"][t] else "v", {"a": ("act", (sg, R(banks[u]), ACT.Sign, 0.0, 1.0)),
                       "v": ("ts", (sg, R(banks[u]), -1.0, 1.0, ALU.max, ALU.min))}, [R(banks[u])], sg)
                mm([(H, R("ID"), R("U", 4 * hf + u, S_(128 * j, 128 * j + 128)), False, False) for j in range(4)])
            if not x:
                lin(R("lo"), R("va"), -2.0, 1.0, "v", True)
                ts(R("hi"), R("va"), 2.0, ALU.add, 63.0, ALU.min)
            new = S_(n0 + 128 * hf, n0 + 128 * hf + 128)
            tt(X, H, h("lo"), ALU.max)
            tt(R("V", new), X, h("hi"), ALU.min)
            if t < RO - 1:
                cp(IND(R("CV"), R("o16", S_(8 * hf, 8 * hf + 8))), R("V", new))
                mm([(X, R("ID"), R("F", new), True, False), (X, R("QC"), R("V", new), False, False)] + [(X, R("ID"), h("tk"), False, False)] * (t < 2))
                cp(h("tn"), X, "a")
                scat(hf)
        if t < RO - 1:
            send("V", t, n0, "av%d" % t)
        dma(R("yv", S_(L * t, L * t + L)), R("V", S_(n0, n0 + L)))
    dma(R("ys"), R("YS")); dma(R("yb"), R("B64"))
    dma(R("YL"), RP("T2", S_(0, 128, 16), S_(0, W))); dma(R("YH"), RP("T2", S_(1, 128, 16), S_(0, W)))
    lin(R("YL"), R("YL"), 0.0, 1.0 / 32)
    tt(R("YI"), R("YL"), R("YH"), ALU.add)
    cp(R("YK"), R("YI"))
    dma(R("yk"), R("YK"))

    hist = {}
    for o in ops:
        dep = set()
        acc = [(r, False) for r in o["rd"]] + [(r, True) for r in o["wr"]]
        for r, wr in acc:
            fb, pb = _foot(r)[:2]
            ps = _where(r["n"]) == "psum"
            for (j, fb2, pb2, wr2) in hist.get(r["n"], []):
                if j == o["id"]:
                    continue
                if ps and o["eng"] == "p" and ops[j]["eng"] == "p":
                    if ops[j]["group"] != o["group"] or j == o["group"]:
                        dep.add(j)
                elif (ps and (ops[j]["eng"] != o["eng"] or "alt" in o or "alt" in ops[j])) or ((wr or wr2) and (fb & fb2) and (pb & pb2)):
                    dep.add(j)
        for r, wr in acc:
            fb, pb = _foot(r)[:2]
            hist.setdefault(r["n"], []).append((o["id"], fb, pb, wr))
        if "after" in o:
            dep.add(o["after"])
        o["dep"] = dep
    first = lambda e, n, k=0: [o["id"] for o in ops if o["eng"] == e and o["wr"] and o["wr"][0]["n"] == n][k]
    behind = {"g": first("g", "zr0", 3), "v": first("v", "DS", tune["late"][0]), "a": first("a", "G2", tune["late"][1])}
    for o in ops[:start]:
        if o["wr"] and (o["eng"], o["wr"][0]["n"]) in LATE:
            o["dep"].add(behind[o["eng"]])
    new, seen = [], set()

    def put(i):
        if i not in seen:
            seen.add(i)
            for j in sorted(ops[i]["dep"]):
                put(j)
            new.append(i)

    for i in range(len(ops)):
        put(i)
    at = {i: k for k, i in enumerate(new)}
    for o in ops:
        o.update({x: at[o[x]] for x in ("id", "group", "after", "link", "only") if x in o})
        o["dep"] = {at[j] for j in o["dep"]}
    return [ops[i] for i in new]


def cost(o, m, e=None):
    cyc = 0.83 * m["f"]
    k, a = o["alt"][e] if e else (o["kind"], o["args"])
    if k == "many":
        d = sum(cost({"kind": x, "args": y}, m)[0] for x, y in a)
        return d, d
    if k == "recv":
        return 0.0, m["rem"]
    if k == "send":
        d = m["snd"] + m["snd1"] * (a[2] == "aq0")
        return d, d + 700.0
    if k == "dma":
        fo, fi = _foot(a[0]), _foot(a[1])
        by = fo[2] * fo[3] * (2 if _dtype(a[0]["n"]) in (B, U2) else 4)
        if o["eng"] == "g":
            d = m["gd"] + m["gd1"] * o.get("once", 0)
            return d, d + 0.6 * m["dma"] + by / (150.0 if o["acc"] else 200.0)
        return m["dh"] + by / 300.0, m["dma"] + by / 200.0 + 5.0 * max(fo[3], fi[3])
    if k == "mm":
        d = sum(max(64, _foot(x[2])[2]) * (4 if _dtype(x[2]["n"]) == F4 else 1) for x in a) * m["pe"] * m["f"] + m["po"] * len(a)
        return d, d + 100.0
    n = _count(a[0])
    if k == "iota":
        d = 130.0 * m["f"] + m["gx"] + 2 * n * cyc
    elif k == "asel":
        d = 170.0 * m["f"] + m["gx"] + 2 * n * cyc
    elif a[0]["off"] is not None:
        d = 50.0 + n * m["sca"] * cyc
    elif isinstance(a[1], dict) and a[1]["off"] is not None:
        d = 60.0 + n * m["ga"] * cyc
    else:
        big = [x for x in a if isinstance(x, dict) and _foot(x)[2] > 1]
        two = all(_dtype(x["n"]) in (B, U2) for x in big)
        if k == "tt":
            c = 2.0 if _where(a[1]["n"]) == "sbuf" and _where(a[2]["n"]) == "sbuf" else 1.0
        elif k == "act":
            c = 1.0
        else:
            c = 0.5 if two else 1.0
        d = max(64.0, n * c) * cyc + m["ov"] + o.get("once", 0.0)
    return d, d


def idle(ops, o):
    return "only" in o and ops[o["only"]]["eng"] != "v"


def _pass(ops, cs, nxt, nprev, pr, m, back, hold):
    n = len(ops)
    left = list(nprev)
    ready = [(cs[i][1] - cs[i][0]) if back else 0.0 for i in range(n)]
    cand = {}
    for i in range(n):
        if left[i] == 0:
            cand.setdefault(ops[i]["eng"], []).append(i)
    free = {}
    order, start, end = [], [0.0] * n, 0.0
    while len(order) < n:
        best = None
        for e, lst in cand.items():
            if not lst:
                continue
            fr = free.get(e, 0.0) if e else 0.0
            lst.sort(key=lambda i: -pr[i])
            soon = 1e30
            for i in lst:
                st = max(ready[i], fr)
                if (e is None or soon >= st + cs[i][0] * hold) and (best is None or (st, -pr[i]) < best[0]):
                    best = ((st, -pr[i]), i)
                soon = min(soon, st)
        (st, _), i = best
        e = ops[i]["eng"]
        cand[e].remove(i)
        order.append(i)
        start[i] = st
        end = max(end, st + (cs[i][0] if back else cs[i][1]))
        if e:
            free[e] = st + cs[i][0]
        for j in nxt[i]:
            lat = (0.0 if e == "p" else m["lat0"]) if ops[j]["eng"] == e else m["lat"]
            ready[j] = max(ready[j], st + (cs[i][0] + cs[j][1] - cs[j][0] if back else cs[i][1]) + lat)
            left[j] -= 1
            if left[j] == 0:
                cand.setdefault(ops[j]["eng"], []).append(j)
    return order, start, end


def schedule(ops, m, turns=3):
    n = len(ops)
    cs = [(0.0, 0.0) if idle(ops, o) else cost(o, m) for o in ops]
    anc = [0] * n
    pred = []
    for o in ops:
        far = 0
        for j in o["dep"]:
            far |= anc[j]
        pred.append([j for j in o["dep"] if not (far >> j) & 1])
        for j in o["dep"]:
            far |= 1 << j
        anc[o["id"]] = far
    succ = [[] for _ in ops]
    for i in range(n):
        for j in pred[i]:
            succ[j].append(i)
    best = None
    for hold in m["holds"]:
        pr = [0.0] * n
        for i in range(n - 1, -1, -1):
            pr[i] = cs[i][1] + max([pr[j] + m["lat"] for j in succ[i]] + [0.0])
        for _ in range(turns):
            order, st, end = _pass(ops, cs, succ, [len(x) for x in pred], pr, m, False, hold)
            if best is None or end < best[0]:
                best = (end, order)
            _o, bs, _e = _pass(ops, cs, pred, [len(x) for x in succ], [st[i] + cs[i][0] for i in range(n)], m, True, hold)
            pr = [bs[i] + cs[i][0] for i in range(n)]
    lead = [i for i in range(n) if "lead" in ops[i]]
    for k in range(1, len(lead)):
        anc[lead[k]] |= anc[lead[k - 1]] | 1 << lead[k - 1]
    order = lead + [i for i in best[1] if i not in lead]
    order = _polish(ops, order, m, anc, pred) if m["moves"] else order
    for o in ops:
        if "alt" in o:
            o["kind"], o["args"] = o["alt"][o["eng"]]
    return [i for i in order if not idle(ops, ops[i])]


def _polish(ops, order, m, anc, pred):
    n = len(ops)
    QS = "vapgs-"
    mixes = [dict(m, **ch) for ch in m["also"]]
    price = [[{e: cost(o, x, e) for e in o["alt"]} if "alt" in o else {o["eng"]: cost(o, x)} for o in ops] for x in mixes]

    def gap(x, e, f):
        return (0.0 if e == "p" else x["lat0"]) if e == f else x["lat"]

    def starts(order, z):
        x, free, st = mixes[z], {}, [0.0] * n
        cs = [(0.0, 0.0) if idle(ops, o) else price[z][i][o["eng"]] for i, o in enumerate(ops)]
        for i in order:
            e = ops[i]["eng"]
            st[i] = max([free.get(e, 0.0)] + [st[j] + cs[j][1] + gap(x, e, ops[j]["eng"]) for j in pred[i]])
            if e:
                free[e] = st[i] + cs[i][0]
        return st, cs

    def run(od, a, q, F, was, lim):
        rel, pl, hold, tail, last = F
        a -= a % 8
        st, by, marks = was[1][:], was[2][:], was[4][:a // 8 + 1]
        free, who, end, at = marks[-1]
        free, who = free[:], who[:]
        k = a
        for i in od[a:]:
            e = q[i]
            s, w = free[e], who[e]
            if rel[i] > s:
                s, w = rel[i], -1
            for j, d in pl[i]:
                if st[j] + d > s:
                    s, w = st[j] + d, j
            st[i], by[i] = s, w
            if e < 5:
                free[e], who[e] = s + hold[i], i
            s += tail[i]
            if s > end:
                if s > lim:
                    return None
                end, at = s, i
            k += 1
            if not k & 7:
                marks.append((free[:], who[:], end, at))
        for e in range(5):
            if free[e] + last[e] > end:
                end, at = free[e] + last[e], who[e]
        return (end, st, by, at, marks) if end <= lim else None

    rng = np.random.default_rng(m["seed"])
    spans = m.get("only") or [(lo, min(n, lo + span)) for span in m["spans"] for lo in range(0, n - span // 2, span // 2)]
    Z = range(len(mixes))
    for lo, hi in spans:
        st = starts(order, 0)[0]
        order = [i for _s, _k, i in sorted((st[i], k, i) for k, i in enumerate(order))]
        ids = order[lo:hi]
        w = len(ids)
        loc = {i: k for k, i in enumerate(ids)}
        q = [QS.index(ops[i]["eng"] or "-") for i in ids]
        inner = [[loc[j] for j in pred[i] if j in loc] for i in ids]
        nxt = [[] for _ in ids]
        for k in range(w):
            for j in inner[k]:
                nxt[j].append(k)
        up = [sum(1 << y for y in range(k) if (anc[i] >> ids[y]) & 1) for k, i in enumerate(ids)]
        flex = {k for k, i in enumerate(ids) if "alt" in ops[i] and ops[i].get("link", i) in loc}
        frames, beyond, full, base = [], [], [], []
        for z in Z:
            st, cs = starts(order, z)
            free = [0.0] * 6
            for i in order[:lo]:
                if ops[i]["eng"]:
                    free[QS.index(ops[i]["eng"])] = st[i] + cs[i][0]
            out, last = [c[1] for c in cs], [0.0] * 5
            for i in reversed(order[hi:]):
                e = ops[i]["eng"]
                if e:
                    out[i] = max(out[i], cs[i][0] + last[QS.index(e)])
                    last[QS.index(e)] = out[i]
                for j in pred[i]:
                    out[j] = max(out[j], cs[j][1] + gap(mixes[z], e, ops[j]["eng"]) + out[i])
            rel = [max([0.0] + [st[j] + cs[j][1] + gap(mixes[z], ops[i]["eng"], ops[j]["eng"]) for j in pred[i] if j not in loc]) for i in ids]
            beyond.append([out[i] - cs[i][1] for i in ids])
            full.append([cs[i][1] for i in ids])
            frames.append((rel, [None] * w, [cs[i][0] for i in ids], [0.0] * w, last))
            base.append((0, [0.0] * w, [-1] * w, 0, [(free, [-1] * 6, 0.0, -1)]))

        def links(ks):
            for z in Z:
                x, pl, tail, fu = mixes[z], frames[z][1], frames[z][3], full[z]
                for k in ks:
                    pl[k] = [(j, fu[j] + ((0.0 if q[k] == 2 else x["lat0"]) if q[j] == q[k] else x["lat"])) for j in inner[k]]
                tail[:] = [a + b for a, b in zip(fu, beyond[z])]
                for k in range(w - 1, -1, -1):
                    t = tail[k]
                    for j, d in pl[k]:
                        if d + t > tail[j]:
                            tail[j] = d + t

        def turn(pairs):
            undo, ks = [], set()
            for k, e in pairs:
                o = ops[ids[k]]
                undo.append((k, o["eng"]))
                o["eng"], q[k] = e, QS.index(e)
                ks.update([k] + nxt[k])
                for z in Z:
                    frames[z][2][k], full[z][k] = price[z][ids[k]][e]
                    if "link" in o:
                        y = loc[o["link"]]
                        frames[z][2][y], full[z][y] = price[z][o["link"]]["p"] if e == "v" else (0.0, 0.0)
                        ks.update(nxt[y])
            links(ks)
            return undo

        links(range(w))
        od = list(range(w))
        base = [run(od, 0, q, frames[z], base[z], 1e30) for z in Z]
        cur = sum(b[0] for b in base)
        best = (cur, od, q[:])
        way = [(None,)] * len(mixes)
        turns = m["moves"] // len(spans)
        rnd = rng.random((turns, 7)).tolist()
        for it in range(turns):
            if it % 200 == 199:
                st = base[it // 200 % len(mixes)][1]
                od = [i for _s, _k, i in sorted((st[i], k, i) for k, i in enumerate(od))]
                base = [run(od, 0, q, frames[z], base[z], 1e30) for z in Z]
            r = rnd[it]
            z = int(r[0] * len(mixes))
            if way[z][0] is not base[z]:
                by, i = base[z][2], base[z][3]
                pairs, can = [], []
                while i >= 0:
                    j = by[i]
                    if j >= 0 and q[j] == q[i] and not (up[i] >> j) & 1:
                        pairs.append((j, i))
                    if i in flex:
                        can.append(i)
                    i = j
                way[z] = (base[z], pairs, can)
            pairs, can = way[z][1:]
            undo = None
            if r[5] < m["flip"]:
                if not can:
                    continue
                k = can[int(r[1] * len(can))]
                es = [e for e in ops[ids[k]]["alt"] if e != QS[q[k]]]
                ch = [(k, es[int(r[2] * len(es))])]
                if r[6] < 0.5:
                    at = od.index(k)
                    can = [y for y in od[max(0, at - 40):at + 40] if y in flex and QS[q[y]] == ch[0][1] and QS[q[k]] in ops[ids[y]]["alt"]]
                    if can:
                        ch.append((can[int(r[3] * len(can))], QS[q[k]]))
                undo = turn(ch)
                new, a = od, 0
            else:
                if not pairs:
                    continue
                p, i = pairs[int(r[1] * len(pairs))]
                a, b = od.index(p), od.index(i)
                if r[2] < 0.5:
                    for _ in range(int(r[3] ** 2 * 8)):
                        c = a - 1
                        while c >= 0 and q[od[c]] != q[i]:
                            c -= 1
                        if c < 0 or (up[i] >> od[c]) & 1:
                            break
                        a = c
                    mid, u = od[a:b + 1], up[i] | 1 << i
                    new = od[:a] + [x for x in mid if (u >> x) & 1] + [x for x in mid if not (u >> x) & 1] + od[b + 1:]
                else:
                    for _ in range(int(r[3] ** 2 * 16)):
                        c = b + 1
                        while c < w and q[od[c]] != q[i]:
                            c += 1
                        if c >= w or (up[od[c]] >> p) & 1:
                            break
                        b = c
                    mid = od[a:b + 1]
                    new = od[:a] + [x for x in mid if x != p and not (up[x] >> p) & 1] + [x for x in mid if x == p or (up[x] >> p) & 1] + od[b + 1:]
            room = m["heat"] * len(mixes) * (1.0 - it / turns) * r[4]
            res = [None] * len(mixes)
            for y in [z] + [y for y in Z if y != z]:
                res[y] = run(new, a, q, frames[y], base[y], base[y][0] + (room if y == z else 1e9))
                if res[y] is None:
                    break
            if res[y] is not None and sum(x[0] for x in res) <= cur + room:
                od, base, cur = new, res, sum(x[0] for x in res)
                if cur < best[0]:
                    best = (cur, new, q[:])
            elif undo:
                turn(undo)
        for k, i in enumerate(ids):
            if "alt" in ops[i]:
                ops[i]["eng"] = QS[best[2][k]]
        order = order[:lo] + [ids[k] for k in best[1]] + order[hi:]
    return order


_PLAN = []


def plan():
    if not _PLAN:
        ops = build_ops(TUNE)
        _PLAN.append((ops, schedule(ops, NOM)))
    return _PLAN[0]


def rank_program(g, core, T, topo):
    rank = T.rank_of(core)
    if rank is None:
        return
    ops, order = plan()
    qs = {"v": g.vector, "a": g.scalar, "p": g.tensor, "g": g, "s": g.sync}
    known = {e: {} for e in qs}
    done = {}
    cnt = {e: 0 for e in CNT}
    ndma = [0]
    final, seen = {}, {}
    nr = len(T.cores)
    closes = {ops[i]["group"]: i for i in order if ops[i]["eng"] == "p"}

    def lanes(src, dst):
        en = topo.engines(src, dst)
        return sum(1 << x for x in en), len(en)

    def issue(q, k, a, last):
        if k == "mm":
            for z, (po, lt, rh, st, sp) in enumerate(a):
                ins = q.matmul(_ap(T, po), _ap(T, lt), _ap(T, rh), st, last and z == len(a) - 1)
            return ins
        x = [_ap(T, r) for r in a]
        if k == "copy":
            return q.tensor_copy(x[0], x[1])
        if k == "tt":
            return q.tensor_tensor(x[0], x[1], x[2], x[3])
        if k == "ts":
            return q.tensor_scalar(x[0], x[1], x[2], None, x[4]) if x[5] is None else q.tensor_scalar(x[0], x[1], x[2], x[3], x[4], x[5])
        if k == "scan":
            return q.tensor_tensor_scan(x[0], x[1], x[2], x[3], x[4], x[5])
        if k == "tr":
            return q.transpose(x[0], x[1])
        if k == "ms":
            return q.memset(x[0], x[1])
        if k == "act":
            return q.activation(x[0], x[1], x[2]) if a[0]["off"] is not None else q.activation(x[0], x[1], x[2], bias=x[3], scale=x[4])
        if k == "iota":
            return q.iota(x[0], x[1], x[2], x[3]) if _dtype(a[0]["n"]) == I4 else q.iota(x[0], x[1], x[2], x[3], allow_small_or_imprecise_dtypes=True)
        return q.affine_select(x[0], x[1], x[2], x[3], x[4], x[5], x[6])

    for i in order:
        o = ops[i]
        e, k, a = o["eng"], o["kind"], o["args"]
        if k == "recv":
            src = T.cores[(rank - ops[o["after"]]["args"][3]) % nr]
            done[i] = (a, lanes(src, core)[1], {})
            final[a] = done[i][1]
            continue
        q = qs[e]
        kn = known[e]
        need = {}
        for j in o["dep"]:
            if (e == "p" and ops[j]["eng"] == "p") or idle(ops, ops[j]):
                continue
            need[j] = done[j]
        for j in sorted(need, reverse=True):
            s, v, imp = need[j]
            top = max(x[1] for x in need.values() if x[0] == s)
            if kn.get(s, 0) < v and v == top:
                q.wait_ge(T.sem[s], v)
                kn[s] = v
                seen[s] = max(seen.get(s, 0), v)
                for s2, v2 in imp.items():
                    kn[s2] = max(kn.get(s2, 0), v2)
        x = [_ap(T, r) for r in a] if k in ("send", "dma") else None
        if k == "send":
            dst = T.cores[(rank + a[3]) % nr]
            rid, pid, _ = topo.addr(dst)
            mask, ne = lanes(core, dst)
            g.remote_dma(x[0], x[1], T.sem[a[2]], T.sem["snt"], pid, rid, mask)
            final["snt"] = final.get("snt", 0) + ne
            done[i] = ("snt", final["snt"], dict(kn))
            continue
        if k == "dma":
            s = "d%d" % ndma[0]
            ndma[0] += 1
            (q.dma_start(x[0], x[1], accum_op=ALU.add) if o["acc"] else q.dma_start(x[0], x[1])).then_inc(T.sem[s], 16)
            done[i] = (s, 16, dict(kn))
            final[s] = 16
            continue
        for k, a in (a if k == "many" else [(k, a)]):
            issue(q, k, a, closes.get(o.get("group")) == i).then_inc(T.sem[CNT[e]], 1)
            cnt[e] += 1
        imp = dict(kn)
        imp[CNT[e]] = cnt[e]
        done[i] = (CNT[e], cnt[e], imp)
        final[CNT[e]] = cnt[e]
    for s, v in final.items():
        if seen.get(s, 0) < v:
            g.sync.wait_ge(T.sem[s], v)
